import numpy as np, ml_dtypes
CORES = [9,25,41,57]
N = 4
BF = ml_dtypes.bfloat16
def gentries(a):
    return np.ascontiguousarray(a.reshape(8, 16, -1).transpose(0, 2, 1)).reshape(8, -1)
def gtable(e):
    e = np.asarray(e); return np.ascontiguousarray(e.reshape(8, -1, 16).transpose(0, 2, 1)).reshape(128, -1).astype(np.int32)
A, W0, B, STEPS, W = 1024, 1792, 256, 5, 2560
def tidy(x):
    return np.asarray(x, np.float32).astype(BF).astype(np.float32)
def sign(rng, m, *shape):
    return (m * (2 * rng.integers(0, 2, shape) - 1)).astype(np.float32)
def num(rng, m, *shape):
    return tidy((np.float32(0.25) + np.float32(0.75) * rng.random(shape, dtype=np.float32)) * sign(rng, m, *shape))
def brink(rng, lo, hi, share, *shape):
    e = np.where(rng.random(shape) < 0.5, lo, hi)
    return np.where(rng.random(shape) < share, e, rng.integers(lo, hi + 1, shape))
def parts(rng):
    d = {"ut": num(rng, 0.5, N, 128, W0), "vt": num(rng, 0.5, N, 128, W0), "bs": num(rng, 1.0, N, 128, A)}
    d["zs"] = num(rng, 1.0, N, 128, B); d["cs"] = num(rng, 0.5, N, 128, B); d["tg"] = num(rng, 1.0, N, 128, B)
    d["ui"] = rng.integers(0, W0, (N, 8, 16, A)); d["vo"] = rng.integers(0, W0, (N, 8, 16, A))
    d["ad"] = rng.integers(0, A, (N, 8, B)); d["nx"] = rng.integers(0, A, (N, 8, 2, A))
    hot = np.argsort(rng.random((N, 8, 16)), axis=2)[..., :2]
    for name in ("sl", "tr"):
        w = np.take_along_axis(hot, rng.integers(0, 2, (N, 8, STEPS * B)), 2)
        d[name] = np.where(rng.random(w.shape) < 0.75, w, rng.integers(0, 16, w.shape)).reshape(N, 8, STEPS, B)
    d["hv"] = rng.integers(6, 12, (N, 8, STEPS, B))
    return d
def pack(d):
    out = {}
    for k in ("ut", "vt"): out[k] = d[k].astype(BF)
    for k in ("ui", "vo"): out[k] = np.ascontiguousarray(d[k].reshape(N, 128, A)).astype(np.int32)
    for k in ("bs", "zs", "cs", "tg"): out[k] = d[k].astype(BF)
    out["ad"] = np.stack([gtable(a) for a in d["ad"]])
    for k in ("nx", "sl", "tr", "hv"): out[k] = np.ascontiguousarray(d[k].reshape(N, 8, -1)).astype(np.int32)
    return out
def setup_inputs(rng):
    return pack(parts(rng))
def setup_inputs_spread(rng):
    d = parts(rng)
    for k in ("ut", "vt", "bs", "zs", "cs", "tg"):
        n = d[k].shape[2]
        d[k] = tidy(d[k] * np.repeat(np.exp2(-rng.integers(0, 3, (N, 8, n)).astype(np.float32)), 16, axis=1))
    lo = (W0 * rng.random((N, 8, 16, A)) ** 2).astype(np.int64); hi = W0 - 1 - (W0 * rng.random((N, 8, 16, A)) ** 2).astype(np.int64)
    m = rng.random((N, 8, 1, A)) < rng.random((N, 8, 1, 1))
    d["ui"] = np.where(m, lo, hi); d["vo"] = np.where(m, hi, lo)
    w = rng.random((N, 8, 16, A)) < 0.4
    d["ui"], d["vo"] = np.where(w, d["vo"], d["ui"]), np.where(w, d["ui"], d["vo"])
    d["ad"] = (A * rng.random((N, 8, B)) ** 2).astype(np.int64); d["nx"] = (A * rng.random((N, 8, 2, A)) ** 1.5).astype(np.int64)
    d["sl"] = (16 * rng.random((N, 8, STEPS, B)) ** 2).astype(np.int64); d["tr"] = (16 * rng.random((N, 8, STEPS, B)) ** 2).astype(np.int64)
    d["hv"] = rng.integers(1, 17, (N, 8, STEPS, B))
    return pack(d)
def setup_inputs_ends(rng):
    d = {"ut": sign(rng, 0.5, N, 128, W0), "vt": sign(rng, 0.5, N, 128, W0), "bs": sign(rng, 1.0, N, 128, A)}
    d["zs"] = sign(rng, 1.0, N, 128, B); d["cs"] = sign(rng, 0.5, N, 128, B); d["tg"] = sign(rng, 1.0, N, 128, B)
    d["ui"] = brink(rng, 0, W0 - 1, 0.7, N, 8, 16, A); d["vo"] = brink(rng, 0, W0 - 1, 0.7, N, 8, 16, A)
    for a in (A - 1, 2): d["ui"][..., a] = W0 - 1; d["vo"][..., a] = 0
    for a in (0, A - 3): d["ui"][..., a] = 0; d["vo"][..., a] = W0 - 1
    d["ui"][..., 1] = W0 - 1; d["vo"][..., 1] = W0 - 1
    d["ad"] = brink(rng, 0, A - 1, 0.65, N, 8, B); d["nx"] = brink(rng, 0, A - 1, 0.65, N, 8, 2, A)
    d["ad"][..., B - 1] = A - 1; d["ad"][..., B - 2] = 2; d["ad"][..., 3] = 1; d["ad"][..., 4] = 0; d["ad"][..., 5] = A - 3
    d["sl"] = 15 * rng.integers(0, 2, (N, 8, STEPS, B)); d["tr"] = 15 * rng.integers(0, 2, (N, 8, STEPS, B))
    d["hv"] = brink(rng, 1, 16, 0.8, N, 8, STEPS, B)
    d["hv"][:, :, 0, B - 1] = 16; d["hv"][:, :, 0, B - 2] = 16; d["hv"][:, :, 0, 3:6] = 1
    for p, s in ((127, 1.0), (126, -1.0), (15, 1.0), (14, -1.0)):
        d["ut"][:, p, W0 - 1] = 0.5; d["vt"][:, p, 0] = 0.5 * s; d["zs"][:, p, B - 2:] = 1.0; d["bs"][:, p, A - 1] = s; d["bs"][:, p, 2] = s
    return pack(d)
def setup_inputs_corners(rng):
    d = parts(rng); q = (0, 1, 2, 3, 8, 14, 15, 16); own = np.arange(A)
    for g in range(8):
        same_ad = rng.permutation(np.arange(1, A - 1))[:B]; same_ad[0] = A - 1; same_ad[B - 1] = 0
        k0, k1 = rng.permutation(16)[:2]; kind = g % 4
        for r in range(N):
            n = q[(g + 3 * r) % 8]
            yes = np.argsort(rng.random((16, A)), axis=0) < n
            lo = rng.integers(0, W0 - 1, (16, A)); hi = lo + 1 + (rng.random((16, A)) * (W0 - 1 - lo)).astype(np.int64)
            hi = np.where(rng.random((16, A)) < 0.3, lo + 1, hi); far = rng.random((16, A)) < 0.1
            lo = np.where(far, 0, lo); hi = np.where(far, W0 - 1, hi); tie = rng.random((16, A)) < 0.3
            d["ui"][r, g] = np.where(yes, hi, lo); d["vo"][r, g] = np.where(yes, lo, np.where(tie, lo, hi))
            d["hv"][r, g] = np.clip(n + rng.integers(0, 2, (STEPS, B)), 1, 16)
            if kind == 0:
                d["nx"][r, g, 0] = rng.permutation(A); d["nx"][r, g, 1] = rng.permutation(A)
                d["sl"][r, g] = 15 * rng.integers(0, 2, (STEPS, B)); d["tr"][r, g] = 15 * rng.integers(0, 2, (STEPS, B))
            elif kind == 2:
                d["nx"][r, g] = np.where(rng.random((2, A)) < 0.6, own[None, :], (A - 1) * rng.integers(0, 2, (2, A)))
            else:
                d["ad"][r, g] = same_ad; d["nx"][r, g, 0] = own; d["nx"][r, g, 1] = own if kind == 1 else own[::-1]
                d["sl"][r, g, :2] = k0; d["sl"][r, g, 2:] = k1; d["tr"][r, g] = k0
    return pack(d)
def setup_inputs_crowd(rng):
    d = parts(rng); own = np.arange(A)
    for g in range(8):
        kind = g % 4; p, w = [int(x) for x in rng.permutation(A)[:2]]; k0, k1 = [int(x) for x in rng.permutation(16)[:2]]; ring = rng.permutation(A)[:B]
        if g == 0: p, w = A - 1, 0
        if g == 1: p, w = 0, A - 1
        for r in range(N):
            if kind < 2:
                d["ad"][r, g] = p; d["nx"][r, g] = own[None, :]
                if kind == 1:
                    d["ad"][r, g, B - 1 if g == 1 else 0] = w
                    d["nx"][r, g, 1, p] = w; d["nx"][r, g, 1, w] = p
                d["sl"][r, g] = k0; d["tr"][r, g] = np.where(rng.random((STEPS, B)) < 0.5, k0, k1); d["tr"][r, g, 2] = k0
                if g == 1:
                    yes = (((np.arange(16) - k0) % 16) >= 1) & (((np.arange(16) - k0) % 16) <= 7)
                    for a in (p, w):
                        lo = rng.integers(0, W0 // 2, 16); hi = rng.integers(W0 // 2, W0, 16)
                        d["ui"][r, g, :, a] = np.where(yes, hi, lo); d["vo"][r, g, :, a] = np.where(yes, lo, hi)
                    d["hv"][r, g, :2] = 16; d["hv"][r, g, 0, B - 2] = 1; d["hv"][r, g, 2, B - 2:] = 8
            elif g == 6:
                lo = rng.integers(0, W0 // 2, (16, A)); hi = lo + rng.integers(1, W0 // 2, (16, A)); yes = ((np.arange(16) - k0) % 16)[:, None] < 8
                d["ui"][r, g] = np.where(yes, hi, lo); d["vo"][r, g] = np.where(yes, lo, hi)
                d["ad"][r, g] = ring; d["nx"][r, g, 0] = own; d["nx"][r, g, 0, ring] = np.roll(ring, -1); d["nx"][r, g, 1] = own[::-1]
                d["sl"][r, g] = k0; d["hv"][r, g, :4] = 16; d["hv"][r, g, 4:] = 8
            elif kind == 2:
                d["ad"][r, g] = np.where(rng.random(B) < 0.5, p, w); d["nx"][r, g, 0] = p; d["nx"][r, g, 1] = w
                for a in (p, w):
                    d["ui"][r, g, :8, a] = W0 - 1; d["vo"][r, g, :8, a] = 0; d["ui"][r, g, 8:, a] = 0; d["vo"][r, g, 8:, a] = W0 - 1
                d["hv"][r, g] = 8 + rng.integers(0, 2, (STEPS, B)); d["sl"][r, g] = rng.choice(np.array([0, 8, 15]), (STEPS, B)); d["tr"][r, g] = rng.choice(np.array([0, 8, 15]), (STEPS, B))
            else:
                m0, n0 = [int(x) for x in np.sort(rng.permutation(W0)[:2])]
                if r == 0: m0, n0 = 0, W0 - 1
                if (r + g // 4) % 2: m0, n0 = n0, m0
                d["ui"][r, g] = n0; d["vo"][r, g] = m0
                o = rng.permutation(A)[:B]; d["ad"][r, g] = o; d["nx"][r, g, 0] = rng.permutation(A); d["nx"][r, g, 1] = rng.permutation(A)
                if g == 7: d["ui"][r, g, :, o[0]] = m0; d["vo"][r, g, :, o[0]] = n0
                d["hv"][r, g] = (15 if n0 > m0 else 1) + rng.integers(0, 2, (STEPS, B))
    return pack(d)
def setup_inputs_brim(rng):
    d = parts(rng); one = int(rng.integers(0, 8))
    for r in range(N):
        for g in range(8):
            full = (g == one) == (r % 2 == 0)
            if full and r % 4 < 2:
                d["ad"][r, g] = int(rng.integers(0, A)); continue
            k = int(rng.integers(0, 16)); m = int(rng.integers(0, W0))
            o = d["vo"][r, g]; o[o == m] = (m + 1) % W0; o[k] = m
            d["ad"][r, g] = rng.permutation(A)[:B]
            w = (k + rng.integers(1, 16, B)) % 16
            if full: w[:] = k
            w[B - 1] = k
            d["tr"][r, g, 0] = w
            if not full:
                nm = rng.permutation(W0); nm = nm[nm != m][:B - 1]
                if g == (one + 4) % 8: nm[1] = nm[0]
                o[w[:B - 1], d["ad"][r, g, :B - 1]] = nm
    return pack(d)
def check_ranges(d):
    bad = []
    for k, lo, hi in (("ui", 0, W0 - 1), ("vo", 0, W0 - 1), ("ad", 0, A - 1), ("nx", 0, A - 1), ("sl", 0, 15), ("tr", 0, 15), ("hv", 1, 16)):
        if np.min(d[k]) < lo or np.max(d[k]) > hi: bad.append("range of " + k)
    for k, lo, hi in (("ut", 2.0 ** -5, 0.5), ("vt", 2.0 ** -5, 0.5), ("cs", 2.0 ** -5, 0.5), ("bs", 2.0 ** -4, 1.0), ("zs", 2.0 ** -4, 1.0), ("tg", 2.0 ** -4, 1.0)):
        v = np.abs(np.asarray(d[k]).astype(np.float64))
        if not np.all((v >= lo) & (v <= hi)): bad.append("range of " + k)
    return bad
def first(key, ok):
    w = np.where(ok, key, -1 - np.arange(B)[None, :]); o = np.argsort(w, axis=1, kind="stable"); s = np.take_along_axis(w, o, 1)
    f = np.ones(s.shape, bool); f[:, 1:] = s[:, 1:] != s[:, :-1]
    m = np.zeros(s.shape, bool); np.put_along_axis(m, o, f, 1)
    return m & ok
def name_at(x, k):
    return np.take_along_axis(x, k[:, None, :], 1)[:, 0]
def vector_at(x, k):
    return np.take_along_axis(x, k[:, None, None, :], 2)[:, :, 0]
def moved(x):
    h = B // 2; w = np.roll(x, 1, axis=0); w[..., h:] = np.roll(x, -1, axis=0)[..., h:]
    return w
def reference(ut, vt, ui, vo, bs, zs, cs, tg, ad, nx, sl, tr, hv):
    U = np.zeros((N, 8, 16, W)); V = np.zeros((N, 8, 16, W))
    U[..., :W0] = ut.astype(np.float64).reshape(N, 8, 16, W0); V[..., :W0] = vt.astype(np.float64).reshape(N, 8, 16, W0)
    I = ui.astype(np.int64).reshape(N, 8, 16, A); O = vo.astype(np.int64).reshape(N, 8, 16, A)
    b = bs.astype(np.float64).reshape(N, 8, 16, A); goal = tg.astype(np.float64).reshape(N, 8, 16, B)
    z = zs.astype(np.float64).reshape(N, 8, 16, B); c = cs.astype(np.float64).reshape(N, 8, 16, B)
    a = np.stack([gentries(x) for x in ad]).astype(np.int64); nxt = nx.astype(np.int64)
    sw, tn, hn = [x.astype(np.int64).reshape(N, 8, STEPS, B) for x in (sl, tr, hv)]
    ys = np.zeros((N, 8, 16, STEPS + 1, B))
    for t in range(STEPS + 1):
        zn, cn, an = np.zeros_like(z), np.zeros_like(c), np.zeros_like(a)
        for r in range(N):
            ai = a[r][:, None, :]
            In = np.take_along_axis(I[r], ai, 2); On = np.take_along_axis(O[r], ai, 2)
            pu = np.take_along_axis(U[r], In.reshape(8, 1, 16 * B), 2).reshape(8, 16, 16, B)
            pv = np.take_along_axis(V[r], On.reshape(8, 1, 16 * B), 2).reshape(8, 16, 16, B)
            y = np.take_along_axis(b[r], ai, 2) + 0.0625 * np.add.reduce(pu * pv, axis=2) * z[r]
            ys[r, :, :, t] = y
            if t == STEPS: continue
            e = y - goal[r]
            votes = np.add.reduce((In > On).astype(np.int64), axis=1)
            an[r] = np.take_along_axis(nxt[r], np.where(votes >= hn[r, :, t], A, 0) + a[r], 1)
            zn[r] = np.clip(y, -1.0, 1.0)
            act = first(a[r], np.ones((8, B), bool))
            if t % 2 == 0: X, Y, P, px, py, Pn, Qn = U, V, I, pu, pv, In, On
            else: X, Y, P, px, py, Pn, Qn = V, U, O, pv, pu, On, In
            k, j = sw[r, :, t], tn[r, :, t]
            xk, yk, xj = vector_at(px, k), vector_at(py, k), vector_at(px, j)
            pj, qj = name_at(Pn, j), name_at(Qn, j)
            go = act
            if t >= 2: go = act & (pj < W0 + B * (t // 2 - 1))
            go = first(qj, go)
            n = W0 + B * (t // 2) + np.arange(B)
            cn[r] = np.where(act[:, None, :], xk, c[r])
            more = 0.0625 * (xk - c[r]) * yk; less = 0.0625 * e * xj * z[r]
            for g in range(8):
                s = np.nonzero(act[g])[0]
                X[r, g][:, n[s]] = c[r, g][:, s]
                P[r, g][k[g, s], a[r, g, s]] = n[s]
                b[r, g][:, a[r, g, s]] += more[g][:, s]
                s = np.nonzero(go[g])[0]
                Y[r, g][:, qj[g, s]] -= less[g][:, s]
        if t < STEPS: z, c, a = moved(zn), moved(cn), moved(an)
    return {"ys": ys.reshape(N, 128, (STEPS + 1) * B).astype(np.float32), "fb": b.reshape(N, 128, A).astype(np.float32), "fc": c.reshape(N, 128, B).astype(np.float32)}

def check_inputs(d):
    bad = list(check_ranges(d))
    if not bad:
        for name, y in reference(**d).items():
            for q in range(N):
                v = np.abs(np.asarray(y[q], np.float64)); s = np.sqrt(np.mean(v * v))
                if v.max() > 3 * s or s < 2.0 ** -4: bad.append('%s of rank %d is uneven or too small' % (name, q))
    return bad

@@ -1,0 +1,749 @@
+from concourse.bass import DstId, RemoteDMATransfer
+from concourse.mybir import AluOpType, ActivationFunctionType
+
+AL = AluOpType
+AF = ActivationFunctionType
+A, W0, B, STEPS = 1024, 1792, 256, 5
+CEN = 1280
+BIG = 4096.0
+NS, NV = 8, 8
+SAMEQ = True
+
+F32, BF, F16, U16, I32 = "float32", "bfloat16", "float16", "uint16", "int32"
+_S = {
+    "U": (2816, F32), "V": (2816, F32), "IT": (1280, F32), "OT": (1280, F32), "BT": (1280, F32),
+    "Ub": (W0, BF), "Vb": (W0, BF), "uii": (1024, I32), "voi": (1024, I32), "adi": (16, I32), "adf": (16, F32),
+    "cmpi": (240, I32), "cmpb": (240, BF), "sqb": (160, BF), "nxi": (128, I32), "nxh": (256, I32), "nxc": (256, BF),
+    "NX": (2048, BF), "R1": (3840, BF), "R2": (2560, BF), "zsb": (256, BF), "tgb": (256, BF),
+    "py": (3 * 4096, F32), "prod": (4096, F32),
+    "oh": (2560, BF), "ohn": (1280, F32), "kj": (160, U16), "hl": (80, BF),
+    "nm": (6 * 512, F32), "n16": (6 * 512, U16), "M": (2 * 1024, F16), "M0": (256, F16),
+    "XR": (6 * 512, BF), "xs": (5 * 256, BF), "au": (6 * 16, U16), "KL": (6 * 32, F16), "L16": (5 * 32, F16),
+    "pju": (5 * 16, U16), "sg": (5 * 16, BF), "rs": (5 * 16, BF), "idx": (5 * 16, U16), "Gs": (5 * 16, BF),
+    "tmn": (5 * 32, F32), "o12": (5 * 32, U16), "tmx": (6 * 32, F32), "o03": (6 * 32, U16),
+    "ab": (768, BF), "eq": (768, BF),
+    "seg": (1024, BF), "bg": (3 * 256, F32), "yk": (2 * 256, F32), "yj": (2 * 256, F32), "cn": (5 * 256, F32), "more": (256, F32),
+    "w": (256, F32), "less": (256, F32), "y": (6 * 256, F32), "r1": (256, F32), "r2": (256, F32),
+    "zo": (5 * 256, F32), "z": (6 * 256, F32), "fcl": (256, F32),
+    "pi": (8, I32), "pc": (8, F32), "one": (144, F32), "idf": (128, F32), "bof": (128, F32), "bot": (128, F32), "ff": (144, F32),
+    "Ib": (128, BF), "nIb": (128, BF), "I5": (128, BF), "Ih": (128, F16), "nIh": (128, F16), "BOb": (128, BF), "BOh": (128, F16),
+    "Fb": (144, BF), "nFb": (144, BF), "Fh": (144, F16), "Sel": (144, BF), "Q1": (128, BF), "Q2": (128, BF), "q1f": (128, F32),
+    "q1g": (128, F32), "tiny": (128, BF), "irow": (256, BF), "rr": (256, F32), "dg": (256, F32), "tri": (512, BF), "cov": (256, BF),
+    "cf": (16, F32), "cu": (16, U16), "seat": (16, F32), "dmn": (96, F32), "dmx": (32, F32), "s4": (16, BF), "s16f": (160, F32),
+    "s16": (240, BF),
+}
+_P = ["PA", "PB", "PC", "PG", "PH", "PL", "PK", "PE"]
+SCRATCH = {k: ("sbuf", [128, v[0]], v[1]) for k, v in _S.items()}
+for _b in _P:
+    SCRATCH[_b] = ("psum", [128, 512], F32)
+NDMA = 24
+SEMAPHORES = (["qv", "qs", "qp", "qg", "sent", "outs"] + ["d%d" % i for i in range(NDMA)]
+              + ["a%s%d" % (k, t) for k in "xc" for t in range(STEPS)] + ["az%d%d" % (t, h) for t in range(STEPS) for h in range(2)])
+
+COSTS = [(1.0, 0.5, 1.56, 3.8, 3000.0, 150.0), (1.0, 0.5, 1.1, 2.0, 4000.0, 200.0), (1.0, 0.5, 2.0, 5.5, 2500.0, 100.0)]
+ROUNDS, MOVES, SEED, NLOAD, EPS = 1500, 60000, 1, 11, 40.0
+PARTS = [("PA", 0, 192, 256), ("PE", 0, 128, 192), ("PA", 64, 64, 128), ("PE", 64, 0, 64)]
+
+
+def n0(t):
+    return W0 + B * (t // 2)
+
+
+def build(CYC, PCY, GA, SC, RL):
+    ops = []
+    tag = ["0"]
+
+    def ap(T, r):
+        if len(r) == 3:
+            return T[r[0]][:, r[1]:r[2]]
+        if len(r) == 4:
+            return T[r[0]][:, r[1]:r[2]:r[3]]
+        return T[r[0]][r[4]:r[5], r[1]:r[2]:r[3]]
+
+    def add(eng, cost, fn, rd, wr, kind="c", lat=0.0, name=""):
+        ops.append({"eng": eng, "cost": cost, "fn": fn, "rd": [r[:3] for r in rd], "wr": [r[:3] for r in wr], "kind": kind,
+                    "lat": lat, "name": name, "tag": tag[0]})
+
+    def width(r):
+        return (r[2] - r[1] + (r[3] if len(r) > 3 else 1) - 1) // (r[3] if len(r) > 3 else 1)
+
+    def vcost(n, k=1.0):
+        return 30.0 + max(64.0, n * k) * CYC
+
+    def psum(r):
+        return r[0] in _P
+
+    def tt(out, a, b, op):
+        k = 1.0 if psum(a) or psum(b) else 2.0
+        add("v", vcost(width(out), k), lambda g, T, X: g.vector.tensor_tensor(ap(T, out), ap(T, a), ap(T, b), op), [a, b], [out])
+
+    def ttg(out, win, off, b, op):
+        add("v", 50 + width(out) * GA * CYC,
+            lambda g, T, X: g.vector.tensor_tensor(ap(T, out), ap(T, win).indirect(ap(T, off)), ap(T, b), op), [win, off, b], [out])
+
+    def tts(win, off, a, b, op):
+        add("v", 50 + width(a) * SC * CYC,
+            lambda g, T, X: g.vector.tensor_tensor(ap(T, win).indirect(ap(T, off)), ap(T, a), ap(T, b), op), [off, a, b], [win])
+
+    def ts(out, a, s1, op0, s2=None, op1=None):
+        rd = [a] + [s for s in (s1, s2) if isinstance(s, tuple)]
+
+        def fn(g, T, X):
+            x1 = ap(T, s1) if isinstance(s1, tuple) else s1
+            x2 = ap(T, s2) if isinstance(s2, tuple) else s2
+            if op1 is None:
+                return g.vector.tensor_scalar(ap(T, out), ap(T, a), x1, None, op0)
+            return g.vector.tensor_scalar(ap(T, out), ap(T, a), x1, x2, op0, op1)
+        add("v", vcost(width(out)), fn, rd, [out])
+
+    def cp(out, a):
+        add("v", vcost(width(out)), lambda g, T, X: g.vector.tensor_copy(ap(T, out), ap(T, a)), [a], [out])
+
+    def cpg(out, win, off):
+        add("v", 50 + width(out) * GA * CYC,
+            lambda g, T, X: g.vector.tensor_copy(ap(T, out), ap(T, win).indirect(ap(T, off))), [win, off], [out])
+
+    def mset(out, v):
+        add("v", vcost(width(out)), lambda g, T, X: g.vector.memset(ap(T, out), v), [], [out])
+
+    def act(out, a, f, bias=0.0, scale=1.0, off=None):
+        rd = [a] + ([off] if off else []) + ([bias] if isinstance(bias, tuple) else [])
+
+        def fn(g, T, X):
+            x = ap(T, a).indirect(ap(T, off)) if off else ap(T, a)
+            bb = ap(T, bias) if isinstance(bias, tuple) else bias
+            return g.scalar.activation(ap(T, out), x, f, bias=bb, scale=scale)
+        add("s", 65 + width(out) * GA * CYC if off else vcost(width(out)), fn, rd, [out])
+
+    def mm(lst, f32=False, first=True, last=True):
+        cost = sum(max(64, width(m[2])) for m in lst) * (4 if f32 else 1) * PCY + (60 if last else 0)
+
+        def fn(g, T, X):
+            ins = None
+            for i, m in enumerate(lst):
+                ins = g.tensor.matmul(ap(T, m[0]), ap(T, m[1]), ap(T, m[2]), first and i == 0, last and i == len(lst) - 1)
+            return ins
+        add("p", cost, fn, [m[1] for m in lst] + [m[2] for m in lst], [m[0] for m in lst])
+
+    def dma(q, fo, fi, rd, wr, nbytes, kind="d"):
+        def fn(g, T, X):
+            return (g if q == "g" else g.sync).dma_start(fo(T), fi(T))
+        add(q, 700.0 if q == "g" else 100.0, fn, rd, wr, kind, 2000.0 + nbytes / 250.0)
+
+    def iota(out, pat, base, cm):
+        fl = _S[out[0]][1] != I32
+
+        def fn(g, T, X):
+            if fl:
+                return g.iota(ap(T, out), pat, base, cm, allow_small_or_imprecise_dtypes=True)
+            return g.iota(ap(T, out), pat, base, cm)
+        add("g", 130 + 2 * width(out) * CYC, fn, [], [out])
+
+    def asel(out, a, pat, op, base, cm):
+        add("g", 170 + 2 * width(out) * CYC,
+            lambda g, T, X: g.affine_select(ap(T, out), ap(T, a), pat, op, 0.0, base, cm), [a], [out])
+
+    def send(sem, src, dst, nbytes, halves=(0, 1)):
+        if len(halves) == 1:
+            h = halves[0]
+            add("g", 300.0, lambda g, T, X: g.remote_dma(ap(T, dst), ap(T, src), T.sem[sem], T.sem["sent"], X["to"][h][1], X["to"][h][0],
+                                                         X["to"][0][2] | X["to"][1][2]), [src], [dst], "r", RL + nbytes / 100.0, sem)
+            return
+
+        def fn(g, T, X):
+            tr = []
+            for h in range(2):
+                rid, pid, m = X["to"][h]
+                tr.append(RemoteDMATransfer(dst_ids=[DstId(rid=rid, pnc=pid)], dma_engine_mask=m, remote_sem=T.sem[sem],
+                                            src=T[src[0]][:, src[1] + 128 * h:src[1] + 128 * h + 128],
+                                            dst=T[dst[0]][:, dst[1] + 128 * h:dst[1] + 128 * h + 128]))
+            return g.remote_dma_fused(tr, local_sem=T.sem["sent"])
+        add("g", 300.0, fn, [src], [dst], "r", RL + nbytes / 100.0, sem)
+
+    def sel(buf, r, k=128):
+        return (buf, 15 - r, 143 - r, 1, 0, k)
+
+    def blk(buf, t, n):
+        return (buf, t * n, (t + 1) * n)
+
+    dma("y", lambda T: T.adi[:], lambda T: T.ad[:], [], [("adi", 0, 16)], 8192)
+    for k, nme in enumerate(("sl", "tr", "hv")):
+        dma("y", lambda T, k=k: T.cmpi[:, 80 * k:80 * k + 80], lambda T, nme=nme: T[nme][:], [], [("cmpi", 80 * k, 80 * k + 80)], 50000)
+    dma("y", lambda T: T.voi[:], lambda T: T.vo[:], [], [("voi", 0, 1024)], 600000)
+    dma("y", lambda T: T.Vb[:], lambda T: T.vt[:], [], [("Vb", 0, W0)], 900000)
+    dma("y", lambda T: T.uii[:], lambda T: T.ui[:], [], [("uii", 0, 1024)], 1200000)
+    dma("y", lambda T: T.Ub[:], lambda T: T.ut[:], [], [("Ub", 0, W0)], 1500000)
+    dma("y", lambda T: T.nxi[:], lambda T: T.nx[:], [], [("nxi", 0, 128)], 1400000)
+    dma("y", lambda T: T.zsb[:], lambda T: T.zs[:], [], [("zsb", 0, 256)], 1400000)
+    dma("y", lambda T: T.tgb[:], lambda T: T.tg[:], [], [("tgb", 0, 256)], 1400000)
+    dma("g", lambda T: T.U[:, 256:2048], lambda T: T.ut[:], [("voi", 0, 1)], [("U", 256, 2048)], 1200000)
+    dma("g", lambda T: T.U[:, 2048:2304], lambda T: T.cs[:], [("voi", 0, 1)], [("U", 2048, 2304)], 1200000)
+    dma("g", lambda T: T.BT[:, 0:1024], lambda T: T.bs[:], [("voi", 0, 1)], [("BT", 0, 1024)], 1200000)
+    dma("g", lambda T: T.V[:, 256:2048], lambda T: T.vt[:], [("voi", 0, 1)], [("V", 256, 2048)], 1200000)
+
+    P0, PSQ, PM, P16 = ("pc", 0, 1), ("pc", 1, 2), ("pc", 2, 3), ("pc", 3, 4)
+    iota(("pi", 0, 1), [[0, 1]], 0, 1)
+    mset(("one", 0, 144), 1.0)
+    asel(("idf", 0, 128), ("one", 0, 128), [[-1, 128]], AL.is_equal, 0, 1)
+    asel(("bot", 0, 128), ("one", 0, 128), [[-16, 8], [0, 16]], AL.is_ge, 0, 1)
+    asel(("bof", 0, 128), ("bot", 0, 128), [[16, 8], [0, 16]], AL.is_ge, 15, -1)
+    iota(("cf", 0, 16), [[1, 16]], 0, 0)
+    iota(("rr", 0, 256), [[0, 16], [1, 16]], 0, 0)
+    asel(("Sel", 0, 144, 1, 0, 8), ("one", 0, 144, 1, 0, 8), [[1, 144]], AL.is_equal, -15, -16)
+    iota(("q1f", 0, 128, 1, 0, 8), [[0, 8], [2, 16]], 0, 0)
+    asel(("q1g", 0, 128, 1, 0, 8), ("one", 0, 128, 1, 0, 8), [[1, 8], [0, 16]], AL.is_equal, 0, -1)
+    iota(("irow", 0, 256, 1, 0, 1), [[1, 256]], 0, 0)
+    iota(("s16f", 0, 160), [[0, 10], [256, 16]], 0, 0)
+    iota(("NX", 0, 2048), [[0, 2048]], 0, 0)
+    ts(("pi", 4, 5), ("pi", 0, 1), 15, AL.bitwise_and)
+    cp(P0, ("pi", 4, 5))
+    ts(PSQ, P0, P0, AL.mult)
+    ts(PM, PSQ, -1.0, AL.mult, 1.0, AL.add)
+    ts(P16, P0, 16.0, AL.mult)
+    for m in range(3):
+        ts(("pc", 4 + m, 5 + m), PSQ, -BIG, AL.mult, float(n0(2 * m) - CEN), AL.add)
+    act(("Ib", 0, 128), ("idf", 0, 128), AF.Copy)
+    act(("nIb", 0, 128), ("idf", 0, 128), AF.Copy, scale=-1.0)
+    act(("I5", 0, 128), ("idf", 0, 128), AF.Copy, scale=512.0)
+    act(("BOb", 0, 128), ("bof", 0, 128), AF.Copy)
+    cp(("Ih", 0, 128), ("idf", 0, 128))
+    ts(("nIh", 0, 128), ("idf", 0, 128), -1.0, AL.mult)
+    cp(("BOh", 0, 128), ("bof", 0, 128))
+    mset(("ff", 0, 144), 0.0)
+    cp(("ff", 15, 143, 16), ("bof", 0, 128, 16))
+    act(("Fb", 0, 144), ("ff", 0, 144), AF.Copy)
+    act(("nFb", 0, 144), ("ff", 0, 144), AF.Copy, scale=-1.0)
+    cp(("Fh", 0, 144), ("ff", 0, 144))
+    tt(("Q1", 0, 128, 1, 0, 8), ("q1f", 0, 128, 1, 0, 8), ("q1g", 0, 128, 1, 0, 8), AL.mult)
+    ts(("Q2", 0, 128, 1, 0, 8), ("q1g", 0, 128, 1, 0, 8), -1.0, AL.mult)
+    mset(("tiny", 0, 128, 1, 0, 1), 1.0 / BIG)
+    ts(("dg", 0, 256), ("rr", 0, 256), P0, AL.is_equal)
+    ts(("tri", 256, 512), ("rr", 0, 256), P0, AL.is_le, BIG, AL.mult)
+    act(("tri", 0, 256), ("tri", 256, 512), AF.Identity, bias=-float(CEN))
+    mset(("cov", 0, 128), -float(CEN))
+    mset(("cov", 128, 256), 0.0)
+    cp(("cu", 0, 16), ("cf", 0, 16))
+    ts(("seat", 0, 16), ("cf", 0, 16), 16.0, AL.mult, P0, AL.add)
+    SEAT = ("seat", 0, 16)
+    for m in range(3):
+        act(("dmn", 32 * m, 32 * m + 16), SEAT, AF.Identity, bias=float(A - CEN))
+        act(("dmn", 32 * m + 16, 32 * m + 32), SEAT, AF.Identity, bias=float(n0(2 * m) - CEN))
+    for m in range(2):
+        act(("dmx", 16 * m, 16 * m + 16), SEAT, AF.Identity, bias=-float(CEN + 256))
+    act(("s4", 0, 16), SEAT, AF.Identity, bias=BIG, scale=BIG)
+    ts(("s16", 0, 160), ("s16f", 0, 160), P16, AL.add)
+    mset(("s16", 160, 240), 0.0)
+
+    cp(("au", 0, 16), ("adi", 0, 16))
+    cpg(("n16", 256, 512), ("voi", 0, 1024), ("au", 0, 16))
+    cpg(("n16", 0, 256), ("uii", 0, 1024), ("au", 0, 16))
+    ts(("OT", 256, 1280), ("voi", 0, 1024), -float(CEN), AL.add)
+    ts(("IT", 256, 1280), ("uii", 0, 1024), -float(CEN), AL.add)
+    cp(("adf", 0, 16), ("adi", 0, 16))
+    ts(("KL", 0, 16), ("adi", 0, 16), -float(CEN), AL.add)
+    ttg(("M0", 0, 256), ("adf", 0, 16), ("cu", 0, 16), ("dg", 0, 256), AL.mult)
+    act(("z", 0, 256), ("zsb", 0, 256), AF.Copy, scale=0.0625)
+    for bank, col, lo, hi in PARTS:
+        act((bank, 256 + col, 256 + col + hi - lo), ("tgb", lo, hi), AF.Copy)
+    for m in range(4):
+        act(blk("seg", m, 256), ("rr", 0, 256), AF.Sign)
+
+    cp(("cmpb", 0, 240), ("cmpi", 0, 240))
+    act(("sqb", 0, 160), ("cmpb", 0, 160), AF.Square)
+    for k in range(3):
+        dma("y", lambda T, k=k: T.R1[0:8, 1280 * k:1280 * k + 1280], lambda T, k=k: T.cmpb[:, 80 * k:80 * k + 80],
+            [("cmpb", 80 * k, 80 * k + 80)], [("R1", 1280 * k, 1280 * k + 1280)], 50000)
+    for k in range(2):
+        dma("y", lambda T, k=k: T.R2[0:8, 1280 * k:1280 * k + 1280], lambda T, k=k: T.sqb[:, 80 * k:80 * k + 80],
+            [("sqb", 80 * k, 80 * k + 80)], [("R2", 1280 * k, 1280 * k + 1280)], 50000)
+    ts(("nxh", 0, 128), ("nxi", 0, 128), 992, AL.bitwise_and)
+    ts(("nxh", 128, 256), ("nxi", 0, 128), 31, AL.bitwise_and)
+    cp(("nxc", 0, 256), ("nxh", 0, 256))
+    for k in range(2):
+        dma("y", lambda T, k=k: T.NX[k:128:16, :], lambda T, k=k: T.nxc[:, 128 * k:128 * k + 128],
+            [("nxc", 0, 256), ("NX", 0, 2048)], [("NXp", k, k + 1)], 50000)
+
+    def masks(t):
+        lo = 256 * t
+        tag[0] = "mask%d" % t
+        mm([(("PG", 0, 256), ("Q1", 0, 128, 1, 0, 8), ("R1", lo, lo + 256, 1, 0, 8)),
+            (("PG", 0, 256), ("Q2", 0, 128, 1, 0, 8), ("R2", lo, lo + 256, 1, 0, 8))])
+        mm([(("PG", 256, 512), ("Q1", 0, 128, 1, 0, 8), ("R1", 1280 + lo, 1536 + lo, 1, 0, 8)),
+            (("PG", 256, 512), ("Q2", 0, 128, 1, 0, 8), ("R2", 1280 + lo, 1536 + lo, 1, 0, 8))])
+        act(("oh", 512 * t, 512 * t + 512), ("PG", 0, 512), AF.Relu, bias=PM)
+        mm([(("PH", 256, 512), ("Q1", 0, 128, 1, 0, 8), ("R1", lo, lo + 256, 1, 0, 8)),
+            (("PH", 256, 512), ("Q2", 0, 128, 1, 0, 8), ("R2", lo, lo + 256, 1, 0, 8)),
+            (("PH", 256, 512), ("tiny", 0, 128, 1, 0, 1), ("irow", 0, 256, 1, 0, 1))])
+        act(blk("ohn", t, 256), ("PH", 256, 512), AF.Identity, bias=("pc", 4 + t // 2, 5 + t // 2), scale=BIG)
+
+    masks(0)
+    mm([(("PH", 0, 240), ("Ib", 0, 128), ("s16", 0, 240))]
+       + [(("PH", 0, 240), sel("Sel", r, 8), ("R1", r, 3840, 16, 0, 8)) for r in range(16)])
+    act(("hl", 0, 80), ("PH", 160, 240), AF.Copy)
+    cp(("kj", 0, 160), ("PH", 0, 160))
+
+    def lists_in(t):
+        s = t - 1
+        tag[0] = "list%d" % t
+        mm([(("PK", 0, 32), sel("Fb", r), ("XR", 512 * t + r, 512 * t + 512, 16)) for r in range(16)]
+           + [(("PK", 16, 32), ("nIb", 0, 128), ("s4", 0, 16))])
+        cp(blk("au", t, 16), ("PK", 0, 16))
+        if t < STEPS:
+            ts(("KL", 32 * t, 32 * t + 16), ("PK", 0, 16), -float(CEN), AL.add)
+        G = blk("Gs", s, 16)
+        act(G, ("PK", 16, 32), AF.Copy)
+        lst = [(("PK", 64, 80), ("Ih", 0, 128), ("KL", 32 * s, 32 * s + 16)), (("PK", 64, 80), ("nIb", 0, 128), G)]
+        mm(lst)
+        lst = [(("PK", 80, 112), ("Ih", 0, 128), blk("L16", s, 32)), (("PK", 80, 96), ("nIb", 0, 128), G),
+               (("PK", 96, 112), ("Ib", 0, 128), G)]
+        if s >= 2:
+            lst.append((("PK", 96, 112), ("nIb", 0, 128), blk("rs", s, 16)))
+        mm(lst)
+        ts(("KL", 32 * t + 16, 32 * t + 32), ("PK", 96, 112), -BIG, AL.max)
+        tt(blk("tmn", s, 32), ("PK", 64, 96), blk("dmn", s // 2, 32), AL.min)
+        ts(blk("o12", s, 32), blk("tmn", s, 32), float(CEN), AL.add)
+
+    def lowest(t):
+        parts = [h for h in range(2) if (t < STEPS if h == 0 else t > 0)]
+        p0, p1 = parts[0], parts[-1] + 1
+        tag[0] = "lowe%d" % t
+        rows = {0: (("BOh", "M0", 0) if t == 0 else ("BOb", "XR", 512 * t)), 1: ("BOh", "M", 1024 * ((t - 1) % 2) + 256)}
+        k0, k1 = 32 * t + 16 * p0, 32 * t + 16 * p1
+        lst = [(("PG", 256 * p0, 256 * p1), ("Ib", 0, 128), ("tri", 256 * p0, 256 * p1))]
+        for h in parts:
+            lst.append((("PG", 256 * h, 256 * h + 256), (rows[h][0], 0, 128), (rows[h][1], rows[h][2], rows[h][2] + 256)))
+        lst += [(("PG", 256 * p0 + r, 256 * p1, 16), ("nIh", 0, 128), ("KL", k0, k1)) for r in range(16)]
+        mm(lst)
+        act(("ab", 256 * p0, 256 * p1), ("PG", 256 * p0, 256 * p1), AF.Abs)
+        lst = [(("PH", 128 * p0, 128 * p1), ("Ib", 0, 128), ("cov", 128 * p0, 128 * p1))]
+        for h in parts:
+            for m in range(8):
+                c = rows[h][2] + 32 * m + 16
+                lst.append((("PH", 128 * h + 16 * m, 128 * h + 16 * m + 16), (rows[h][0], 0, 128), (rows[h][1], c, c + 16)))
+        lst += [(("PH", 128 * p0 + r, 128 * p1, 16), ("nIh", 0, 128), ("KL", k0, k1, 2)) for r in range(16)]
+        mm(lst)
+        act(("ab", 512 + 128 * p0, 512 + 128 * p1), ("PH", 128 * p0, 128 * p1), AF.Abs)
+        if len(parts) == 2:
+            act(("eq", 0, 768), ("ab", 0, 768), AF.Relu, bias=BIG, scale=-BIG)
+        else:
+            act(("eq", 256 * p0, 256 * p1), ("ab", 256 * p0, 256 * p1), AF.Relu, bias=BIG, scale=-BIG)
+            act(("eq", 512 + 128 * p0, 512 + 128 * p1), ("ab", 512 + 128 * p0, 512 + 128 * p1), AF.Relu, bias=BIG, scale=-BIG)
+        c0, c1 = 128 + 16 * p0, 128 + 16 * p1
+        mm([(("PK", c0, c1), ("Ih", 0, 128), ("KL", k0, k1))]
+           + [(("PK", c0, c1), sel("nFb", r), ("eq", 256 * p0 + r, 256 * p1, 16)) for r in range(16)]
+           + [(("PK", c0 + 1, c1, 2), sel("nFb", r), ("eq", 512 + 128 * p0 + r, 512 + 128 * p1, 16)) for r in range(16)])
+        tt(("tmx", k0, k1), ("PK", c0, c1), ("dmx", 16 * p0, 16 * p1), AL.max)
+        ts(("o03", k0, k1), ("tmx", k0, k1), float(CEN + 256), AL.add)
+
+    def names(t):
+        b = 512 * t
+        tag[0] = "name%d" % t
+        au = blk("au", t, 16)
+        act(("nm", b, b + 256), ("IT", 256, 1280), AF.Copy, off=au)
+        act(("nm", b + 256, b + 512), ("OT", 256, 1280), AF.Copy, off=au)
+        if t > 0:
+            ts(("n16", b, b + 512), ("nm", b, b + 512), float(CEN), AL.add)
+        if t == STEPS:
+            return
+        act(("PC", 0, 512), ("nm", b, b + 512), AF.Copy)
+        m = 1024 * (t % 2)
+        p, q = 256 * (t % 2), 256 * (1 - t % 2)
+        ohk, ohj = ("oh", b, b + 256), ("oh", b + 256, b + 512)
+        tt(("M", m + 768, m + 1024), ("PC", 0, 256), ("nm", b + 256, b + 512), AL.is_gt)
+        tt(("M", m, m + 256), ("PC", p, p + 256), ohk, AL.mult)
+        tt(("M", m + 256, m + 512), ("PC", q, q + 256), ohj, AL.mult)
+        tt(("M", m + 512, m + 768), ("PC", p, p + 256), ohj, AL.mult)
+        mm([(("PL", 0, 64), sel("Fh", r), ("M", m + r, m + 1024, 16)) for r in range(16)]
+           + [(("PL", 48, 64), ("nIb", 0, 128), blk("hl", t, 16))])
+        act(blk("sg", t, 16), ("PL", 48, 64), AF.Sign, bias=0.5)
+        if t >= 2:
+            act(blk("rs", t, 16), ("PL", 32, 48), AF.Relu, bias=-BIG * (n0(t - 2) - CEN - 1), scale=BIG)
+        mm([(("PL", 64, 80), ("I5", 0, 128), blk("sg", t, 16)), (("PL", 64, 80), ("Ih", 0, 128), ("KL", 32 * t, 32 * t + 16))])
+        ts(blk("idx", t, 16), ("PL", 64, 80), float(CEN + 512), AL.add)
+        cp(blk("L16", t, 32), ("PL", 0, 32))
+        ts(blk("pju", t, 16), ("PL", 32, 48), float(CEN), AL.add)
+        au2 = blk("idx", t, 16)
+        add("s", 65 + 256 * GA * CYC,
+            lambda g, T, X: g.scalar.activation(ap(T, blk("xs", t, 256)), T.NX[:, 0:2048].indirect(ap(T, au2)), AF.Copy),
+            [("NX", 0, 2048), ("NXp", 0, 2), au2], [blk("xs", t, 256)])
+        send("ax%d" % t, blk("xs", t, 256), ("XR", 512 * (t + 1), 512 * (t + 1) + 256), 65536)
+
+    def switch(t):
+        tab = "IT" if t % 2 == 0 else "OT"
+        p = 512 * t + 256 * (t % 2)
+        tag[0] = "swit%d" % t
+        for m in range(7, -1, -1):
+            tts((tab, 0, 1280), ("o03", 32 * t + 2 * m, 32 * t + 2 * m + 2), ("nm", p + 32 * m, p + 32 * m + 32),
+                ("ohn", 256 * t + 32 * m, 256 * t + 32 * m + 32), AL.max)
+        act(("XR", 512 * (t + 1) + 256, 512 * (t + 1) + 512), (tab, 256, 1280), AF.Relu, bias=-BIG * (n0(t) - CEN - 1), scale=BIG,
+            off=blk("au", t, 16))
+
+    def filled(tab, t):
+        return 256 + W0 + B * ((t + 1) // 2 if tab == "U" else t // 2)
+
+    def early(t):
+        tab = "V" if t % 2 == 0 else "U"
+        q = 512 * t + 256 * (1 - t % 2)
+        n = 4096 // NS
+        tag[0] = "early%d" % t
+        for c in range(NS - 1, -1, -1):
+            o = 4096 * (t % 3) + n * c
+            act(("py", o, o + n), (tab, 256, filled(tab, t)) if t else ("Vb", 0, W0), AF.Copy,
+                off=("n16", q + c * n // 16, q + (c + 1) * n // 16))
+
+    def late(t):
+        tab = "U" if t % 2 == 0 else "V"
+        p = 512 * t + 256 * (t % 2)
+        n = 4096 // NV
+        o, oy = 0, 4096 * (t % 3)
+        todo = list(PARTS)
+        for c in range(NV - 1, -1, -1):
+            tag[0] = "late%d" % t
+            ttg(("prod", o + n * c, o + n * c + n), (tab, 256, filled(tab, t)) if t else ("Ub", 0, W0),
+                ("n16", p + c * n // 16, p + (c + 1) * n // 16), ("py", oy + n * c, oy + n * c + n), AL.mult)
+            if c * n % 1024 == 0:
+                h = c * n // 1024
+                if t == STEPS and h == 0:
+                    add("v", vcost(1024), lambda g, T, X: g.vector.tensor_tensor_scan(
+                        T.py[:, 0:1024], T.seg[:, 0:1024], T.prod[:, 0:1024], 0.0, AL.mult, AL.add),
+                        [("seg", 0, 1024), ("prod", 0, 1024)], [("py", 0, 1024)])
+                    continue
+                bank, col, lo = [x[:3] for x in PARTS if x[2] <= 64 * h < x[3]][0]
+                while todo[0][0] == bank and todo[0][2] > 64 * h:
+                    tail(t, *todo.pop(0))
+                col += 64 * h - lo
+                for k0 in range(0, 16, 4):
+                    mm([((bank, col, col + 64), ("idf", 0, 128), ("prod", o + 1024 * h + k, o + 1024 * h + 1024, 16))
+                        for k in range(k0, k0 + 4)], True, k0 == 0, k0 == 12)
+        for x in todo:
+            tail(t, *x)
+
+    def side(t):
+        X, oy = ("U" if t % 2 == 0 else "V"), 4096 * (t % 3)
+        f = filled(X, t)
+        tag[0] = "side%d" % t
+        act(blk("cn", t, 256), (X, 256, f + 256), AF.Copy, off=("o12", 32 * t + 16, 32 * t + 32))
+        Y = "V" if t % 2 == 0 else "U"
+        send("ac%d" % t, blk("cn", t, 256), (Y, filled(Y, t), filled(Y, t) + 256) if t < STEPS - 1 else ("fcl", 0, 256), 131072)
+        act(blk("yk", t % 2, 256), ("py", oy, oy + 4096), AF.Copy, scale=0.0625, off=blk("kj", t, 16))
+        act(blk("yj", t % 2, 256), ("py", oy, oy + 4096), AF.Copy, off=blk("kj", 5 + t, 16))
+        act(("PB", 256, 512), (X, f, f + 256), AF.Copy)
+        tt(("PB", 256, 512), blk("cn", t, 256), ("PB", 256, 512), AL.subtract)
+        tt(("more", 0, 256), ("PB", 256, 512), blk("yk", t % 2, 256), AL.mult)
+        tts(("BT", 0, 1280), ("o12", 32 * t, 32 * t + 16), blk("bg", t % 3, 256), ("more", 0, 256), AL.add)
+        for h in (1, 0):
+            tag[0] = "w%d%d" % (t, h)
+            ttg(("w", 128 * h, 128 * h + 128), (X, 256, f), blk("pju", 2 * t + h, 8), blk("z", 2 * t + h, 128), AL.mult)
+
+    def tail(t, bank, col, lo, hi):
+        Y = "V" if t % 2 == 0 else "U"
+        k, j, b, bb = 32 * (t + 1) + 16, 256 * (t % 2), 256 * t, 256 * (t % 3)
+        tag[0] = "tail%d%d" % (t, lo)
+        S, y = (bank, col, col + hi - lo), ("y", b + lo, b + hi)
+        tt(S, ("py", 15, 1024, 16) if t == STEPS and lo == 0 else S, ("z", b + lo, b + hi), AL.mult)
+        tt(y, S, ("bg", bb + lo, bb + hi), AL.add)
+        if t == STEPS:
+            dma("y", lambda T: T.ys[:, y[1]:y[2]], lambda T: ap(T, y), [y], [], 32768, "o")
+            return
+        tt(S, y, (bank, 256 + col, 256 + col + hi - lo), AL.subtract)
+        tt(("less", lo, hi), S, ("w", lo, hi), AL.mult)
+        for m in range(hi // 32 - 1, lo // 32 - 1, -1):
+            tts((Y, 0, filled(Y, t)), ("o03", k + 2 * m, k + 2 * m + 2), ("yj", j + 32 * m, j + 32 * m + 32),
+                ("less", 32 * m, 32 * m + 32), AL.subtract)
+        if lo % 128:
+            return
+        h = lo // 128
+        tag[0] = "clip%d%d" % (t, h)
+        act(blk("r1", h, 128), blk("y", 2 * t + h, 128), AF.Relu, bias=1.0)
+        act(blk("r2", h, 128), blk("r1", h, 128), AF.Relu, bias=2.0, scale=-1.0)
+        act(blk("zo", 2 * t + h, 128), blk("r2", h, 128), AF.Identity, bias=0.0625, scale=-0.0625)
+        send("az%d%d" % (t, h), blk("zo", 2 * t + h, 128), blk("z", 2 * t + 2 + h, 128), 65536, (h,))
+        if h == 0:
+            dma("y", lambda T: T.ys[:, b:b + 256], lambda T: T.y[:, b:b + 256], [blk("y", t, 256)], [], 131072, "o")
+
+    early(0)
+    names(0)
+    lowest(0)
+    switch(0)
+    for t in range(STEPS + 1):
+        tag[0] = "bg%d" % t
+        act(blk("bg", t % 3, 256), ("BT", 0, 1024), AF.Copy, off=blk("au", t, 16))
+        if t < STEPS:
+            if t + 1 < STEPS:
+                masks(t + 1)
+            lists_in(t + 1)
+            names(t + 1)
+            lowest(t + 1)
+            if t + 1 < STEPS:
+                switch(t + 1)
+            early(t + 1)
+            side(t)
+        late(t)
+        if t == STEPS - 1:
+            dma("y", lambda T: T.fb[:], lambda T: T.BT[:, 0:1024], [("BT", 0, 1024)], [], 524288, "o")
+            dma("y", lambda T: T.fc[:], lambda T: T.fcl[:], [("fcl", 0, 256)], [], 131072, "o")
+    return ops
+
+
+def schedule():
+    others = [(build(*c[:5]), c[5]) for c in COSTS]
+    ops = others[0][0]
+    n = len(ops)
+    deps = [dict() for _ in range(n)]
+    seen = {}
+    for j, o in enumerate(ops):
+        acc = [(r, False) for r in o["rd"]] + [(r, True) for r in o["wr"]]
+        for r, wr in acc:
+            for (i, c0, c1, iw) in seen.get(r[0], ()):
+                other = ops[i]["eng"] != o["eng"] or ops[i]["kind"] != "c" or o["kind"] != "c"
+                if r[0] in _P and other:
+                    deps[j][i] = True
+                elif r[0] in _P and o["eng"] == "p":
+                    deps[j].setdefault(i, False)
+                elif c0 < r[2] and r[1] < c1 and (wr or iw):
+                    deps[j][i] = deps[j].get(i, False) or other or (iw and not wr) or (SAMEQ and o["eng"] != "p")
+        for r, wr in acc:
+            seen.setdefault(r[0], []).append((j, r[1], r[2], wr))
+    for a, b in zip(range(NLOAD - 1), range(1, NLOAD)):
+        deps[b].setdefault(a, False)
+    eng = [o["eng"] for o in ops]
+    anc, near = [0] * n, []
+    for j in range(n):
+        far = 0
+        for i in deps[j]:
+            far |= anc[i]
+        near.append({i: w for i, w in deps[j].items() if not far >> i & 1 or ops[i]["lat"]})
+        for i in deps[j]:
+            far |= 1 << i
+        anc[j] = far
+    sets = []
+    for oo, lat in others:
+        sets.append(([o["cost"] for o in oo], [o["lat"] for o in oo],
+                     [[(i, oo[i]["lat"] + lat if w else 0.0) for i, w in near[j].items()] for j in range(n)]))
+    cost, tail, pred = sets[0]
+    back = [[] for _ in range(n)]
+    for j in range(n):
+        for i, d in pred[j]:
+            back[i].append((j, d))
+
+    def place(seq, pr, first):
+        busy = {e: [] for e in "vspgy"}
+        st = [0.0] * n
+        for j in seq:
+            t = first[j]
+            for i, d in pr[j]:
+                x = st[i] + cost[i] + d
+                if x > t:
+                    t = x
+            b, c = busy[eng[j]], cost[j]
+            k = len(b)
+            while k > 0 and b[k - 1][1] > t:
+                k -= 1
+            while k < len(b) and b[k][0] < t + c:
+                t = max(t, b[k][1])
+                k += 1
+            b.insert(k, (t, t + c))
+            st[j] = t
+        return st
+
+    def replay(seq):
+        tot = 0.0
+        for c, tl, pr in sets:
+            free = {e: 0.0 for e in "vspgy"}
+            en = [0.0] * n
+            for j in seq:
+                t = free[eng[j]]
+                for i, d in pr[j]:
+                    x = en[i] + d
+                    if x > t:
+                        t = x
+                en[j] = free[eng[j]] = t + c[j]
+            tot += max(en[j] + tl[j] for j in range(n)) / sum(c)
+        return tot
+
+    def topo_by(key):
+        k2 = list(key)
+        for j in range(n):
+            for i, d in pred[j]:
+                if k2[j] <= k2[i]:
+                    k2[j] = k2[i] + 1e-3
+        return sorted(range(n), key=lambda j: k2[j])
+
+    zero = [0.0] * n
+
+    def eager(key, eps):
+        left = [len(p) for p in pred]
+        ready, st = [0.0] * n, [0.0] * n
+        free = {e: 0.0 for e in "vspgy"}
+        pool = {e: [] for e in "vspgy"}
+        nxt = {e: 1e18 for e in "vspgy"}
+        for j in range(n):
+            if not left[j]:
+                pool[eng[j]].append(j)
+                nxt[eng[j]] = 0.0
+        for _ in range(n):
+            e = min(nxt, key=nxt.get)
+            t0, p = nxt[e] + eps, pool[e]
+            j = min((j for j in p if ready[j] <= t0), key=lambda j: key[j])
+            p.remove(j)
+            st[j] = max(nxt[e], ready[j])
+            f = free[e] = st[j] + cost[j]
+            for k, d in back[j]:
+                if f + d > ready[k]:
+                    ready[k] = f + d
+                left[k] -= 1
+                if not left[k]:
+                    pool[eng[k]].append(k)
+                    nxt[eng[k]] = min(nxt[eng[k]], max(free[eng[k]], ready[k]))
+            nxt[e] = max(f, min(ready[k] for k in p)) if p else 1e18
+        return st
+
+    def improve(key, k=2):
+        st = place(topo_by(key), pred, zero)
+        for _ in range(k):
+            fw = sorted(range(n), key=lambda j: (st[j] + cost[j], j), reverse=True)
+            bk = place(fw, back, tail)
+            st = place(topo_by([-(bk[j] + cost[j]) for j in range(n)]), pred, zero)
+        seq = sorted(range(n), key=lambda j: (st[j], j))
+        res = (replay(seq), seq, st)
+        s2 = eager(st, EPS)
+        seq = sorted(range(n), key=lambda j: (s2[j], j))
+        return min(res, (replay(seq), seq, s2), key=lambda x: x[0])
+
+    prio = [0.0] * n
+    for i in range(n - 1, -1, -1):
+        prio[i] = cost[i] + max([prio[j] + d for j, d in back[i]] + [tail[i]])
+    whole = [o["tag"][:4] in ("mask", "list", "lowe", "name", "swit") for o in ops]
+    best = min((improve([-p - (b if w else 0.0) for p, w in zip(prio, whole)]) for b in (0.0, 5e3, 1e4, 2e4, 4e4)), key=lambda x: x[0])
+    tags = sorted(set(o["tag"] for o in ops))
+    cur, rnd = best, [SEED]
+
+    def draw():
+        rnd[0] = (rnd[0] * 1103515245 + 12345) % 2147483648
+        return rnd[0] / 2147483648.0
+
+    for it in range(ROUNDS):
+        amp = (100.0, 400.0, 1500.0)[it % 3]
+        mv = {tags[int(draw() * len(tags))]: (draw() - 0.5) * 12000.0 for _ in range(1 + it % 4)}
+        new = improve([cur[2][j] + amp * draw() + mv.get(ops[j]["tag"], 0.0) for j in range(n)], it % 2)
+        if new[0] < cur[0] * 1.001:
+            cur = new
+        if new[0] < best[0]:
+            best = new
+    ei = ["vspgy".index(e) for e in eng]
+    norm = [sum(s[0]) for s in sets]
+    ends = [j for j in range(n) if not back[j]]
+
+    def run(seq, k0, old):
+        out, tot = [], 0.0
+        for (c, tl, pr), en0, nm in zip(sets, old, norm):
+            en, free, k = list(en0), [-1.0] * 5, k0 - 1
+            miss = 5
+            while k >= 0 and miss:
+                if free[ei[seq[k]]] < 0:
+                    free[ei[seq[k]]] = en[seq[k]]
+                    miss -= 1
+                k -= 1
+            for j in seq[k0:]:
+                e = ei[j]
+                t = free[e]
+                for i, d in pr[j]:
+                    x = en[i] + d
+                    if x > t:
+                        t = x
+                en[j] = free[e] = t + c[j]
+            tot += (max([en[j] + tl[j] for j in ends]) + 0.1 * sum(en) / n) / nm
+            out.append(en)
+        return tot, out
+
+    seq = list(best[1])
+    val, en = run(seq, 0, [zero] * len(sets))
+    top = (val, list(seq), en)
+    for it in range(MOVES):
+        a = int(draw() * n)
+        j, step, hops = seq[a], (1 if draw() < 0.5 else -1), 1 + int(draw() * draw() * 6)
+        b = a
+        while hops and 0 <= b + step < n:
+            i = seq[b + step]
+            if (anc[i] >> j & 1) if step > 0 else (anc[j] >> i & 1):
+                break
+            b += step
+            hops -= ei[i] == ei[j]
+        if hops:
+            continue
+        new = list(seq)
+        new.insert(b, new.pop(a))
+        v2, en2 = run(new, min(a, b), en)
+        if v2 <= val + 0.0004 * (1.0 - it / MOVES) * draw():
+            seq, val, en = new, v2, en2
+            if val < top[0]:
+                top = (val, list(seq), en)
+    order = top[1]
+    start = [top[2][0][j] - cost[j] for j in range(n)]
+    best = (replay(order),)
+    done = [start[j] + cost[j] + tail[j] for j in range(n)]
+    token, count, nd = {}, {e: 0 for e in "vspg"}, 0
+    known = {e: {} for e in "vspgy"}
+    clock, waits = {}, {}
+    for j in order:
+        o, e = ops[j], ops[j]["eng"]
+        w = {}
+        for i in sorted((i for i in deps[j] if deps[j][i]), key=lambda i: -done[i]):
+            s, v = token[i]
+            if known[e].get(s, 0) >= v:
+                continue
+            w[s] = max(w.get(s, 0), v)
+            for s2, v2 in clock[i].items():
+                known[e][s2] = max(known[e].get(s2, 0), v2)
+        waits[j] = w
+        if o["kind"] == "c":
+            count[e] += 1
+            token[j] = ("q" + e, count[e])
+        elif o["kind"] == "d":
+            token[j] = ("d%d" % nd, 16)
+            nd += 1
+        elif o["kind"] == "o":
+            token[j] = ("outs", 0)
+        else:
+            token[j] = (o["name"], 8)
+        clock[j] = {} if o["kind"] == "r" else dict(known[e])
+        clock[j][token[j][0]] = token[j][1]
+    return ops, {"score": best[0], "order": order, "waits": waits, "token": token, "count": count, "start": start, "done": done, "nd": nd}
+
+
+_PLAN = {}
+
+
+def rank_program(g, core, T, topo):
+    rank = T.rank_of(core)
+    if rank is None:
+        return
+    if not _PLAN:
+        _PLAN["ops"], _PLAN["s"] = schedule()
+    ops, s = _PLAN["ops"], _PLAN["s"]
+    n = len(T.cores)
+    to = []
+    for h, d in enumerate((T.cores[(rank + 1) % n], T.cores[(rank - 1) % n])):
+        rid, pid, _ = topo.addr(d)
+        eng = topo.engines(core, d)
+        k = len(eng) // 2
+        to.append((rid, pid, sum(1 << e for e in eng[h * k:h * k + 4])))
+    X = {"to": to}
+    q = {"v": g.vector, "s": g.scalar, "p": g.tensor, "g": g, "y": g.sync}
+    outs = sends = 0
+    for j in s["order"]:
+        o = ops[j]
+        for sem, v in s["waits"][j].items():
+            q[o["eng"]].wait_ge(T.sem[sem], v)
+        ins = o["fn"](g, T, X)
+        if o["kind"] == "c":
+            ins.then_inc(T.sem[s["token"][j][0]], 1)
+        elif o["kind"] == "r":
+            sends += 1
+        else:
+            ins.then_inc(T.sem[s["token"][j][0]], 16)
+            outs += o["kind"] == "o"
+    for e, v in s["count"].items():
+        g.wait_ge(T.sem["q" + e], v)
+    g.wait_ge(T.sem["sent"], 8 * sends)
+    g.sync.wait_ge(T.sem["outs"], 16 * outs)

@@ -4,45 +4,49 @@ from concourse.mybir import AluOpType, ActivationFunctionType
 AL = AluOpType
 AF = ActivationFunctionType
 A, W0, B, STEPS = 1024, 1792, 256, 5
+OFF = 256
 CEN = 1280
 BIG = 4096.0
-NS, NV = 8, 8
-SAMEQ = True
+NS, NV = 4, 4
+APART = 1
+ONV = 0
 
 F32, BF, F16, U16, I32 = "float32", "bfloat16", "float16", "uint16", "int32"
 _S = {
-    "U": (2816, F32), "V": (2816, F32), "IT": (1280, F32), "OT": (1280, F32), "BT": (1280, F32),
-    "Ub": (W0, BF), "Vb": (W0, BF), "uii": (1024, I32), "voi": (1024, I32), "adi": (16, I32), "adf": (16, F32),
-    "cmpi": (240, I32), "cmpb": (240, BF), "sqb": (160, BF), "nxi": (128, I32), "nxh": (256, I32), "nxc": (256, BF),
-    "NX": (2048, BF), "R1": (3840, BF), "R2": (2560, BF), "zsb": (256, BF), "tgb": (256, BF),
+    "U": (2816, F32), "V": (2816, F32), "IT": (1280, F32), "OT": (1280, F32), "BT": (1792, F32),
+    "Ub": (W0, BF), "Vb": (W0, BF), "uii": (1024, I32), "voi": (1024, I32), "adi": (16, I32),
+    "cmpi": (240, I32), "cmpb": (240, BF), "nxi": (128, I32), "nxh": (256, I32), "nxc": (256, BF),
+    "NX": (2048, BF), "R1": (3840, BF), "RR": (2560, BF), "zsb": (256, BF), "tgb": (256, BF),
     "py": (3 * 4096, F32), "prod": (4096, F32),
-    "oh": (2560, BF), "ohn": (1280, F32), "kj": (160, U16), "hl": (80, BF),
-    "nm": (6 * 512, F32), "n16": (6 * 512, U16), "M": (2 * 1024, F16), "M0": (256, F16),
+    "oh": (2560, BF), "oh0": (512, BF), "dd": (256, F32), "id16": (128, F32), "trb": (288, BF), "nw": (512, F32), "kj": (160, U16), "hl": (80, BF),
+    "nm": (6 * 512, F32), "n16": (6 * 512, U16), "M": (2 * 1024, F16),
     "XR": (6 * 512, BF), "xs": (5 * 256, BF), "au": (6 * 16, U16), "KL": (6 * 32, F16), "L16": (5 * 32, F16),
-    "pju": (5 * 16, U16), "sg": (5 * 16, BF), "rs": (5 * 16, BF), "idx": (5 * 16, U16), "Gs": (5 * 16, BF),
+    "pj": (5 * 32, U16), "sg": (5 * 16, BF), "rs": (5 * 16, BF), "Gs": (5 * 16, BF),
     "tmn": (5 * 32, F32), "o12": (5 * 32, U16), "tmx": (6 * 32, F32), "o03": (6 * 32, U16),
-    "ab": (768, BF), "eq": (768, BF),
-    "seg": (1024, BF), "bg": (3 * 256, F32), "yk": (2 * 256, F32), "yj": (2 * 256, F32), "cn": (5 * 256, F32), "more": (256, F32),
+    "ab": (256, BF), "eq": (768, BF),
+    "seg": (1024, BF), "bg": (3 * 256, F32), "yj": (2 * 256, F32), "cn": (5 * 256, F32), "more": (256, F32),
     "w": (256, F32), "less": (256, F32), "y": (6 * 256, F32), "r1": (256, F32), "r2": (256, F32),
     "zo": (5 * 256, F32), "z": (6 * 256, F32), "fcl": (256, F32),
-    "pi": (8, I32), "pc": (8, F32), "one": (144, F32), "idf": (128, F32), "bof": (128, F32), "bot": (128, F32), "ff": (144, F32),
-    "Ib": (128, BF), "nIb": (128, BF), "I5": (128, BF), "Ih": (128, F16), "nIh": (128, F16), "BOb": (128, BF), "BOh": (128, F16),
-    "Fb": (144, BF), "nFb": (144, BF), "Fh": (144, F16), "Sel": (144, BF), "Q1": (128, BF), "Q2": (128, BF), "q1f": (128, F32),
-    "q1g": (128, F32), "tiny": (128, BF), "irow": (256, BF), "rr": (256, F32), "dg": (256, F32), "tri": (512, BF), "cov": (256, BF),
-    "cf": (16, F32), "cu": (16, U16), "seat": (16, F32), "dmn": (96, F32), "dmx": (32, F32), "s4": (16, BF), "s16f": (160, F32),
-    "s16": (240, BF),
+    "pi": (8, I32), "pc": (8, F32), "pb": (8, BF), "one": (144, BF), "idf": (128, F32), "bot": (128, BF), "Zb": (128, BF),
+    "Ib": (128, BF), "nIb": (128, BF), "I5": (128, BF), "In": (384, BF), "BOb": (128, BF), "Fb": (144, BF), "nFb": (144, BF),
+    "Sel": (144, BF), "irow": (256, BF), "cf": (16, F32), "csf": (144, F32), "cs": (144, F32), "seatb": (16, BF),
+    "s16f": (160, F32), "s16": (160, BF), "colb": (32, BF), "colf": (16, F32), "DL": (2048, BF), "TR": (2304, BF),
 }
+_S["cst"] = _S.pop("cs")
 _P = ["PA", "PB", "PC", "PG", "PH", "PL", "PK", "PE"]
 SCRATCH = {k: ("sbuf", [128, v[0]], v[1]) for k, v in _S.items()}
 for _b in _P:
     SCRATCH[_b] = ("psum", [128, 512], F32)
+SCRATCH["RD"] = ("dram", [8, 2560], BF)
 NDMA = 24
-SEMAPHORES = (["qv", "qs", "qp", "qg", "sent", "outs"] + ["d%d" % i for i in range(NDMA)]
+SEMAPHORES = (["qv", "qs", "qp", "qg", "sent", "outs", "rd", "rr"] + ["d%d" % i for i in range(NDMA)]
               + ["a%s%d" % (k, t) for k in "xc" for t in range(STEPS)] + ["az%d%d" % (t, h) for t in range(STEPS) for h in range(2)])
 
-COSTS = [(1.0, 0.5, 1.56, 3.8, 3000.0, 150.0), (1.0, 0.5, 1.1, 2.0, 4000.0, 200.0), (1.0, 0.5, 2.0, 5.5, 2500.0, 100.0)]
-ROUNDS, MOVES, SEED, NLOAD, EPS = 1500, 60000, 1, 11, 40.0
-PARTS = [("PA", 0, 192, 256), ("PE", 0, 128, 192), ("PA", 64, 64, 128), ("PE", 64, 0, 64)]
+COSTS = [(0.85, 0.43, 1.56, 3.8, 3000.0, 150.0), (0.95, 0.48, 1.15, 2.2, 4000.0, 200.0), (1.15, 0.58, 1.9, 5.2, 3000.0, 120.0),
+         (1.1, 0.56, 1.5, 3.5, 5500.0, 250.0)]
+ROUNDS, MOVES, SEED, SOON, ONPATH, HEAT = 3000, 35000, 1, 0.1, 0.6, 0.001
+PARTS = [("PA", 0, 128, 256), ("PE", 0, 64, 128), ("PB", 0, 0, 64)]
+CB = ("PL", 256, 512)
 
 
 def n0(t):
@@ -73,6 +77,9 @@ def build(CYC, PCY, GA, SC, RL):
     def psum(r):
         return r[0] in _P
 
+    def short(*rs):
+        return 0.5 if all(r[0] in _S and _S[r[0]][1] in (BF, F16, U16) for r in rs) else 1.0
+
     def tt(out, a, b, op):
         k = 1.0 if psum(a) or psum(b) else 2.0
         add("v", vcost(width(out), k), lambda g, T, X: g.vector.tensor_tensor(ap(T, out), ap(T, a), ap(T, b), op), [a, b], [out])
@@ -85,7 +92,15 @@ def build(CYC, PCY, GA, SC, RL):
         add("v", 50 + width(a) * SC * CYC,
             lambda g, T, X: g.vector.tensor_tensor(ap(T, win).indirect(ap(T, off)), ap(T, a), ap(T, b), op), [off, a, b], [win])
 
-    def ts(out, a, s1, op0, s2=None, op1=None):
+    def scatter(eng, win, off, a):
+        if eng == "v":
+            add("v", 50 + width(a) * SC * CYC,
+                lambda g, T, X: g.vector.tensor_copy(ap(T, win).indirect(ap(T, off)), ap(T, a)), [off, a], [win])
+        else:
+            add("s", 65 + width(a) * SC * CYC,
+                lambda g, T, X: g.scalar.activation(ap(T, win).indirect(ap(T, off)), ap(T, a), AF.Silu), [off, a], [win])
+
+    def ts(out, a, s1, op0, s2=None, op1=None, more=()):
         rd = [a] + [s for s in (s1, s2) if isinstance(s, tuple)]
 
         def fn(g, T, X):
@@ -94,41 +109,43 @@ def build(CYC, PCY, GA, SC, RL):
             if op1 is None:
                 return g.vector.tensor_scalar(ap(T, out), ap(T, a), x1, None, op0)
             return g.vector.tensor_scalar(ap(T, out), ap(T, a), x1, x2, op0, op1)
-        add("v", vcost(width(out)), fn, rd, [out])
+        add("v", vcost(width(out), short(out, *rd)), fn, rd + list(more), [out])
 
     def cp(out, a):
-        add("v", vcost(width(out)), lambda g, T, X: g.vector.tensor_copy(ap(T, out), ap(T, a)), [a], [out])
+        add("v", vcost(width(out), short(out, a)), lambda g, T, X: g.vector.tensor_copy(ap(T, out), ap(T, a)), [a], [out])
 
     def cpg(out, win, off):
         add("v", 50 + width(out) * GA * CYC,
             lambda g, T, X: g.vector.tensor_copy(ap(T, out), ap(T, win).indirect(ap(T, off))), [win, off], [out])
 
     def mset(out, v):
-        add("v", vcost(width(out)), lambda g, T, X: g.vector.memset(ap(T, out), v), [], [out])
+        add("v", vcost(width(out), short(out)), lambda g, T, X: g.vector.memset(ap(T, out), v), [], [out])
 
-    def act(out, a, f, bias=0.0, scale=1.0, off=None):
-        rd = [a] + ([off] if off else []) + ([bias] if isinstance(bias, tuple) else [])
+    def act(out, a, f, bias=0.0, scale=1.0, off=None, more=(), extra=0.0):
+        rd = [a] + ([off] if off else []) + [x for x in (bias, scale) if isinstance(x, tuple)] + list(more)
 
         def fn(g, T, X):
             x = ap(T, a).indirect(ap(T, off)) if off else ap(T, a)
             bb = ap(T, bias) if isinstance(bias, tuple) else bias
-            return g.scalar.activation(ap(T, out), x, f, bias=bb, scale=scale)
-        add("s", 65 + width(out) * GA * CYC if off else vcost(width(out)), fn, rd, [out])
+            ss = ap(T, scale) if isinstance(scale, tuple) else scale
+            return g.scalar.activation(ap(T, out), x, f, bias=bb, scale=ss)
+        add("s", extra + (65 + width(out) * GA * CYC if off else vcost(width(out))), fn, rd, [out])
 
-    def mm(lst, f32=False, first=True, last=True):
-        cost = sum(max(64, width(m[2])) for m in lst) * (4 if f32 else 1) * PCY + (60 if last else 0)
+    def mm(lst, f32=False, first=True, last=True, solo=False):
+        cost = sum(max(64, width(m[2])) for m in lst) * (4 if f32 else 1) * PCY + (40 if last else 0)
 
         def fn(g, T, X):
             ins = None
             for i, m in enumerate(lst):
-                ins = g.tensor.matmul(ap(T, m[0]), ap(T, m[1]), ap(T, m[2]), first and i == 0, last and i == len(lst) - 1)
+                ins = g.tensor.matmul(ap(T, m[0]), ap(T, m[1]), ap(T, m[2]), solo or (first and i == 0),
+                                      solo or (last and i == len(lst) - 1))
             return ins
         add("p", cost, fn, [m[1] for m in lst] + [m[2] for m in lst], [m[0] for m in lst])
 
-    def dma(q, fo, fi, rd, wr, nbytes, kind="d"):
+    def dma(q, fo, fi, rd, wr, nbytes, kind="d", name=""):
         def fn(g, T, X):
-            return (g if q == "g" else g.sync).dma_start(fo(T), fi(T))
-        add(q, 700.0 if q == "g" else 100.0, fn, rd, wr, kind, 2000.0 + nbytes / 250.0)
+            return {"g": g, "y": g.sync, "s": g.scalar}[q].dma_start(fo(T), fi(T))
+        add(q, 700.0 if q == "g" else 100.0, fn, rd, wr, kind, 2000.0 + nbytes / 600.0, name)
 
     def iota(out, pat, base, cm):
         fl = _S[out[0]][1] != I32
@@ -139,9 +156,9 @@ def build(CYC, PCY, GA, SC, RL):
             return g.iota(ap(T, out), pat, base, cm)
         add("g", 130 + 2 * width(out) * CYC, fn, [], [out])
 
-    def asel(out, a, pat, op, base, cm):
+    def asel(out, a, pat, op, base, cm, fill=0.0):
         add("g", 170 + 2 * width(out) * CYC,
-            lambda g, T, X: g.affine_select(ap(T, out), ap(T, a), pat, op, 0.0, base, cm), [a], [out])
+            lambda g, T, X: g.affine_select(ap(T, out), ap(T, a), pat, op, fill, base, cm), [a], [out])
 
     def send(sem, src, dst, nbytes, halves=(0, 1)):
         if len(halves) == 1:
@@ -166,217 +183,204 @@ def build(CYC, PCY, GA, SC, RL):
     def blk(buf, t, n):
         return (buf, t * n, (t + 1) * n)
 
-    dma("y", lambda T: T.adi[:], lambda T: T.ad[:], [], [("adi", 0, 16)], 8192)
-    for k, nme in enumerate(("sl", "tr", "hv")):
-        dma("y", lambda T, k=k: T.cmpi[:, 80 * k:80 * k + 80], lambda T, nme=nme: T[nme][:], [], [("cmpi", 80 * k, 80 * k + 80)], 50000)
-    dma("y", lambda T: T.voi[:], lambda T: T.vo[:], [], [("voi", 0, 1024)], 600000)
-    dma("y", lambda T: T.Vb[:], lambda T: T.vt[:], [], [("Vb", 0, W0)], 900000)
-    dma("y", lambda T: T.uii[:], lambda T: T.ui[:], [], [("uii", 0, 1024)], 1200000)
-    dma("y", lambda T: T.Ub[:], lambda T: T.ut[:], [], [("Ub", 0, W0)], 1500000)
-    dma("y", lambda T: T.nxi[:], lambda T: T.nx[:], [], [("nxi", 0, 128)], 1400000)
-    dma("y", lambda T: T.zsb[:], lambda T: T.zs[:], [], [("zsb", 0, 256)], 1400000)
-    dma("y", lambda T: T.tgb[:], lambda T: T.tg[:], [], [("tgb", 0, 256)], 1400000)
-    dma("g", lambda T: T.U[:, 256:2048], lambda T: T.ut[:], [("voi", 0, 1)], [("U", 256, 2048)], 1200000)
-    dma("g", lambda T: T.U[:, 2048:2304], lambda T: T.cs[:], [("voi", 0, 1)], [("U", 2048, 2304)], 1200000)
-    dma("g", lambda T: T.BT[:, 0:1024], lambda T: T.bs[:], [("voi", 0, 1)], [("BT", 0, 1024)], 1200000)
-    dma("g", lambda T: T.V[:, 256:2048], lambda T: T.vt[:], [("voi", 0, 1)], [("V", 256, 2048)], 1200000)
+    def tri(r):
+        return ("TR", 143 * r, 143 * r + 128)
 
-    P0, PSQ, PM, P16 = ("pc", 0, 1), ("pc", 1, 2), ("pc", 2, 3), ("pc", 3, 4)
-    iota(("pi", 0, 1), [[0, 1]], 0, 1)
+    tag[0] = "load"
+    dma("y", lambda T: T.adi[:], lambda T: T.ad[:], [], [("adi", 0, 16)], 8192)
+    dma("y", lambda T: T.voi[:], lambda T: T.vo[:], [], [("voi", 0, 1024)], 600000)
+    dma("y", lambda T: T.uii[:], lambda T: T.ui[:], [], [("uii", 0, 1024)], 1100000)
+    dma("y", lambda T: T.Vb[:], lambda T: T.vt[:], [], [("Vb", 0, W0)], 1550000)
+    dma("y", lambda T: T.Ub[:], lambda T: T.ut[:], [], [("Ub", 0, W0)], 2000000)
+    dma("y", lambda T: T.zsb[:], lambda T: T.zs[:], [], [("zsb", 0, 256)], 2000000)
+    dma("y", lambda T: T.tgb[:], lambda T: T.tg[:], [], [("tgb", 0, 256)], 2000000)
+    for k, nme in ((2, "hv"), (0, "sl"), (1, "tr")):
+        dma("s", lambda T, k=k: T.cmpi[:, 80 * k:80 * k + 80], lambda T, nme=nme: T[nme][:], [], [("cmpi", 80 * k, 80 * k + 80)], 100000)
+    dma("s", lambda T: T.nxi[:], lambda T: T.nx[:], [], [("nxi", 0, 128)], 200000)
+    tag[0] = "0"
+    dma("g", lambda T: T.BT[:, 0:1024], lambda T: T.bs[:], [("uii", 0, 1)], [("BT", 0, 1024)], 1500000)
+    dma("g", lambda T: T.U[:, 256:2048], lambda T: T.ut[:], [("uii", 0, 1)], [("U", 256, 2048)], 2000000)
+    dma("g", lambda T: T.U[:, 2048:2304], lambda T: T.cs[:], [("uii", 0, 1)], [("U", 2048, 2304)], 2000000)
+    dma("g", lambda T: T.V[:, 256:2048], lambda T: T.vt[:], [("uii", 0, 1)], [("V", 256, 2048)], 2000000)
+
+    P0, PB0 = ("pc", 0, 1), ("pb", 0, 1)
+    ID, NID, ONE = ("Ib", 0, 128), ("nIb", 0, 128), ("one", 0, 128)
     mset(("one", 0, 144), 1.0)
-    asel(("idf", 0, 128), ("one", 0, 128), [[-1, 128]], AL.is_equal, 0, 1)
-    asel(("bot", 0, 128), ("one", 0, 128), [[-16, 8], [0, 16]], AL.is_ge, 0, 1)
-    asel(("bof", 0, 128), ("bot", 0, 128), [[16, 8], [0, 16]], AL.is_ge, 15, -1)
+    mset(("NX", 0, 2048), 0.0)
+    mset(("Fb", 0, 144), 0.0)
+    iota(("pi", 0, 1), [[0, 1]], 0, 1)
     iota(("cf", 0, 16), [[1, 16]], 0, 0)
-    iota(("rr", 0, 256), [[0, 16], [1, 16]], 0, 0)
+    asel(("idf", 0, 128), ONE, [[-1, 128]], AL.is_equal, 0, 1)
+    asel(("bot", 0, 128), ONE, [[-16, 8], [0, 16]], AL.is_ge, 0, 1)
+    asel(("BOb", 0, 128), ("bot", 0, 128), [[16, 8], [0, 16]], AL.is_ge, 15, -1)
+    asel(("Zb", 0, 128), ("BOb", 0, 128), [[-1, 128]], AL.not_equal, 0, 1, -1.0)
     asel(("Sel", 0, 144, 1, 0, 8), ("one", 0, 144, 1, 0, 8), [[1, 144]], AL.is_equal, -15, -16)
-    iota(("q1f", 0, 128, 1, 0, 8), [[0, 8], [2, 16]], 0, 0)
-    asel(("q1g", 0, 128, 1, 0, 8), ("one", 0, 128, 1, 0, 8), [[1, 8], [0, 16]], AL.is_equal, 0, -1)
     iota(("irow", 0, 256, 1, 0, 1), [[1, 256]], 0, 0)
-    iota(("s16f", 0, 160), [[0, 10], [256, 16]], 0, 0)
-    iota(("NX", 0, 2048), [[0, 2048]], 0, 0)
+    iota(("s16f", 0, 160), [[0, 10], [16, 16]], 0, 0)
+    iota(("csf", 0, 96), [[256, 3], [W0 - A, 2], [16, 16]], A - CEN, 0)
+    iota(("csf", 96, 128), [[0, 2], [16, 16]], -CEN - 256, 0)
+    iota(("csf", 128, 144), [[16, 16]], 0, 0)
+    for m in range(8):
+        asel(blk("seg", m, 128), ONE, [[0, 8], [1, 16]], AL.is_gt, 0, 0)
     ts(("pi", 4, 5), ("pi", 0, 1), 15, AL.bitwise_and)
     cp(P0, ("pi", 4, 5))
-    ts(PSQ, P0, P0, AL.mult)
-    ts(PM, PSQ, -1.0, AL.mult, 1.0, AL.add)
-    ts(P16, P0, 16.0, AL.mult)
-    for m in range(3):
-        ts(("pc", 4 + m, 5 + m), PSQ, -BIG, AL.mult, float(n0(2 * m) - CEN), AL.add)
-    act(("Ib", 0, 128), ("idf", 0, 128), AF.Copy)
-    act(("nIb", 0, 128), ("idf", 0, 128), AF.Copy, scale=-1.0)
+    cp(PB0, ("pi", 4, 5))
+    ts(("cst", 0, 144), ("csf", 0, 144), P0, AL.add)
+    ts(("s16", 0, 160), ("s16f", 0, 160), P0, AL.add, 16.0, AL.mult)
+    ts(("colb", 0, 16), ("cf", 0, 16), P0, AL.is_equal)
+    ts(("colb", 16, 32), ("cf", 0, 16), P0, AL.is_equal, -1.0, AL.add)
+    ts(("colf", 0, 16), ("cf", 0, 16), P0, AL.is_lt, -BIG, AL.mult)
+    act(ID, ("idf", 0, 128), AF.Copy)
+    act(NID, ("idf", 0, 128), AF.Copy, scale=-1.0)
     act(("I5", 0, 128), ("idf", 0, 128), AF.Copy, scale=512.0)
-    act(("BOb", 0, 128), ("bof", 0, 128), AF.Copy)
-    cp(("Ih", 0, 128), ("idf", 0, 128))
-    ts(("nIh", 0, 128), ("idf", 0, 128), -1.0, AL.mult)
-    cp(("BOh", 0, 128), ("bof", 0, 128))
-    mset(("ff", 0, 144), 0.0)
-    cp(("ff", 15, 143, 16), ("bof", 0, 128, 16))
-    act(("Fb", 0, 144), ("ff", 0, 144), AF.Copy)
-    act(("nFb", 0, 144), ("ff", 0, 144), AF.Copy, scale=-1.0)
-    cp(("Fh", 0, 144), ("ff", 0, 144))
-    tt(("Q1", 0, 128, 1, 0, 8), ("q1f", 0, 128, 1, 0, 8), ("q1g", 0, 128, 1, 0, 8), AL.mult)
-    ts(("Q2", 0, 128, 1, 0, 8), ("q1g", 0, 128, 1, 0, 8), -1.0, AL.mult)
-    mset(("tiny", 0, 128, 1, 0, 1), 1.0 / BIG)
-    ts(("dg", 0, 256), ("rr", 0, 256), P0, AL.is_equal)
-    ts(("tri", 256, 512), ("rr", 0, 256), P0, AL.is_le, BIG, AL.mult)
-    act(("tri", 0, 256), ("tri", 256, 512), AF.Identity, bias=-float(CEN))
-    mset(("cov", 0, 128), -float(CEN))
-    mset(("cov", 128, 256), 0.0)
-    cp(("cu", 0, 16), ("cf", 0, 16))
-    ts(("seat", 0, 16), ("cf", 0, 16), 16.0, AL.mult, P0, AL.add)
-    SEAT = ("seat", 0, 16)
     for m in range(3):
-        act(("dmn", 32 * m, 32 * m + 16), SEAT, AF.Identity, bias=float(A - CEN))
-        act(("dmn", 32 * m + 16, 32 * m + 32), SEAT, AF.Identity, bias=float(n0(2 * m) - CEN))
-    for m in range(2):
-        act(("dmx", 16 * m, 16 * m + 16), SEAT, AF.Identity, bias=-float(CEN + 256))
-    act(("s4", 0, 16), SEAT, AF.Identity, bias=BIG, scale=BIG)
-    ts(("s16", 0, 160), ("s16f", 0, 160), P16, AL.add)
-    mset(("s16", 160, 240), 0.0)
+        act(blk("In", m, 128), ("idf", 0, 128), AF.Silu, scale=float(n0(2 * m) + OFF), extra=0.0 if m else 1300.0)
+    act(("Fb", 15, 143, 16), ("BOb", 0, 128, 16), AF.Copy)
+    act(("nFb", 0, 144), ("Fb", 0, 144), AF.Copy, scale=-1.0)
+    act(("seatb", 0, 16), ("cst", 128, 144), AF.Copy)
+    for r in range(16):
+        ts(blk("DL", r, 128), ("Zb", 0, 128), ("colb", 16 + r, 17 + r), AL.max, ("colb", r, r + 1), AL.min)
+        act(tri(r), ("idf", 0, 128), AF.Copy, scale=("colf", r, r + 1))
+    iota(("trb", 0, 144), [[0, 144]], -int(BIG), 0)
+    asel(("trb", 144, 288), ("trb", 0, 144), [[0, 16], [-16, 9]], AL.is_ge, 0, 1)
+    asel(("TR", 0, 2304, 16), ("trb", 144, 288), [[1, 16], [16, 9]], AL.is_ge, -1, -1)
+    act(("id16", 0, 128), ("idf", 0, 128), AF.Copy, scale=16.0)
 
     cp(("au", 0, 16), ("adi", 0, 16))
     cpg(("n16", 256, 512), ("voi", 0, 1024), ("au", 0, 16))
     cpg(("n16", 0, 256), ("uii", 0, 1024), ("au", 0, 16))
-    ts(("OT", 256, 1280), ("voi", 0, 1024), -float(CEN), AL.add)
-    ts(("IT", 256, 1280), ("uii", 0, 1024), -float(CEN), AL.add)
-    cp(("adf", 0, 16), ("adi", 0, 16))
+    ts(("OT", 256, 1280), ("voi", 0, 1024), float(OFF), AL.add)
+    ts(("IT", 256, 1280), ("uii", 0, 1024), float(OFF), AL.add)
     ts(("KL", 0, 16), ("adi", 0, 16), -float(CEN), AL.add)
-    ttg(("M0", 0, 256), ("adf", 0, 16), ("cu", 0, 16), ("dg", 0, 256), AL.mult)
     act(("z", 0, 256), ("zsb", 0, 256), AF.Copy, scale=0.0625)
     for bank, col, lo, hi in PARTS:
         act((bank, 256 + col, 256 + col + hi - lo), ("tgb", lo, hi), AF.Copy)
-    for m in range(4):
-        act(blk("seg", m, 256), ("rr", 0, 256), AF.Sign)
 
-    cp(("cmpb", 0, 240), ("cmpi", 0, 240))
-    act(("sqb", 0, 160), ("cmpb", 0, 160), AF.Square)
-    for k in range(3):
-        dma("y", lambda T, k=k: T.R1[0:8, 1280 * k:1280 * k + 1280], lambda T, k=k: T.cmpb[:, 80 * k:80 * k + 80],
-            [("cmpb", 80 * k, 80 * k + 80)], [("R1", 1280 * k, 1280 * k + 1280)], 50000)
+    cp(("cmpb", 160, 240), ("cmpi", 160, 240))
+    cp(("cmpb", 0, 160), ("cmpi", 0, 160))
+    mm([(("PG", 256 * k + 80 * r, 256 * k + min(256, 80 * r + 80)), m, ("cmpb", 80 * k, 80 * k + min(80, 256 - 80 * r)))
+        for k in range(2) for r in range(4) for m in (blk("DL", r, 128), ID)])
+    ts(("oh0", 0, 512), ("PG", 0, 512), P0, AL.is_equal)
     for k in range(2):
-        dma("y", lambda T, k=k: T.R2[0:8, 1280 * k:1280 * k + 1280], lambda T, k=k: T.sqb[:, 80 * k:80 * k + 80],
-            [("sqb", 80 * k, 80 * k + 80)], [("R2", 1280 * k, 1280 * k + 1280)], 50000)
+        dma("y", lambda T, k=k: T.RD[:, 1280 * k:1280 * k + 1280], lambda T, k=k: T.cmpb[:, 80 * k:80 * k + 80],
+            [("cmpb", 80 * k, 80 * k + 80)], [("RD", 1280 * k, 1280 * k + 1280)], 50000, "d", "rd")
+    for k in (2, 0, 1):
+        dma("y", lambda T, k=k: T.R1[0:8, 1280 * k:1280 * k + 1280], lambda T, k=k: T.cmpb[:, 80 * k:80 * k + 80],
+            [("cmpb", 80 * k, 80 * k + 80)], [("R1", 1280 * k, 1280 * k + 1280)], 200000)
+    for r in range(16):
+        dma("y", lambda T, r=r: T.RR[r:128:16, :], lambda T: T.RD[:, :], [("RD", 0, 2560)], [("RRp", r, r + 1)], 400000, "d", "rr")
+    for k in range(2):
+        ts(("oh", 1280 * k + 256, 1280 * k + 1280), ("RR", 1280 * k + 256, 1280 * k + 1280), PB0, AL.is_equal, more=[("RRp", 0, 16)])
     ts(("nxh", 0, 128), ("nxi", 0, 128), 992, AL.bitwise_and)
     ts(("nxh", 128, 256), ("nxi", 0, 128), 31, AL.bitwise_and)
-    cp(("nxc", 0, 256), ("nxh", 0, 256))
+    ts(("nxc", 0, 128), ("nxh", 0, 128), -float(CEN), AL.add)
+    cp(("nxc", 128, 256), ("nxh", 128, 256))
     for k in range(2):
         dma("y", lambda T, k=k: T.NX[k:128:16, :], lambda T, k=k: T.nxc[:, 128 * k:128 * k + 128],
-            [("nxc", 0, 256), ("NX", 0, 2048)], [("NXp", k, k + 1)], 50000)
+            [blk("nxc", k, 128), ("NX", 0, 2048)], [("NXp", k, k + 1)], 200000)
+    mm([(("PK", 0, 80), sel("Sel", r, 8), ("R1", 2560 + r, 3840, 16, 0, 8)) for r in range(16)])
+    act(("hl", 0, 80), ("PK", 0, 80), AF.Copy)
+    mm([(("PB", 0, 160), sel("Sel", r, 8), ("R1", r, 2560, 16, 0, 8)) for r in range(16)] + [(("PB", 0, 160), ID, ("s16", 0, 160))])
+    cp(("kj", 0, 160), ("PB", 0, 160))
 
-    def masks(t):
-        lo = 256 * t
-        tag[0] = "mask%d" % t
-        mm([(("PG", 0, 256), ("Q1", 0, 128, 1, 0, 8), ("R1", lo, lo + 256, 1, 0, 8)),
-            (("PG", 0, 256), ("Q2", 0, 128, 1, 0, 8), ("R2", lo, lo + 256, 1, 0, 8))])
-        mm([(("PG", 256, 512), ("Q1", 0, 128, 1, 0, 8), ("R1", 1280 + lo, 1536 + lo, 1, 0, 8)),
-            (("PG", 256, 512), ("Q2", 0, 128, 1, 0, 8), ("R2", 1280 + lo, 1536 + lo, 1, 0, 8))])
-        act(("oh", 512 * t, 512 * t + 512), ("PG", 0, 512), AF.Relu, bias=PM)
-        mm([(("PH", 256, 512), ("Q1", 0, 128, 1, 0, 8), ("R1", lo, lo + 256, 1, 0, 8)),
-            (("PH", 256, 512), ("Q2", 0, 128, 1, 0, 8), ("R2", lo, lo + 256, 1, 0, 8)),
-            (("PH", 256, 512), ("tiny", 0, 128, 1, 0, 1), ("irow", 0, 256, 1, 0, 1))])
-        act(blk("ohn", t, 256), ("PH", 256, 512), AF.Identity, bias=("pc", 4 + t // 2, 5 + t // 2), scale=BIG)
-
-    masks(0)
-    mm([(("PH", 0, 240), ("Ib", 0, 128), ("s16", 0, 240))]
-       + [(("PH", 0, 240), sel("Sel", r, 8), ("R1", r, 3840, 16, 0, 8)) for r in range(16)])
-    act(("hl", 0, 80), ("PH", 160, 240), AF.Copy)
-    cp(("kj", 0, 160), ("PH", 0, 160))
-
-    def lists_in(t):
+    def lists_in(t, parts=(0, 1)):
         s = t - 1
         tag[0] = "list%d" % t
-        mm([(("PK", 0, 32), sel("Fb", r), ("XR", 512 * t + r, 512 * t + 512, 16)) for r in range(16)]
-           + [(("PK", 16, 32), ("nIb", 0, 128), ("s4", 0, 16))])
-        cp(blk("au", t, 16), ("PK", 0, 16))
-        if t < STEPS:
-            ts(("KL", 32 * t, 32 * t + 16), ("PK", 0, 16), -float(CEN), AL.add)
+        p0, p1 = parts[0], parts[-1] + 1
+        mm([(("PK", 16 * p0, 16 * p1), sel("Fb", r), ("XR", 512 * t + 256 * p0 + r, 512 * t + 256 * p1, 16)) for r in range(16)]
+           + [(("PK", 16, 32), NID, ("seatb", 0, 16))] * (p1 - 1))
+        if p0 == 0:
+            ts(blk("au", t, 16), ("PK", 0, 16), float(CEN), AL.add)
+            if t < STEPS:
+                cp(("KL", 32 * t, 32 * t + 16), ("PK", 0, 16))
+        if p1 == 1:
+            return
         G = blk("Gs", s, 16)
-        act(G, ("PK", 16, 32), AF.Copy)
-        lst = [(("PK", 64, 80), ("Ih", 0, 128), ("KL", 32 * s, 32 * s + 16)), (("PK", 64, 80), ("nIb", 0, 128), G)]
-        mm(lst)
-        lst = [(("PK", 80, 112), ("Ih", 0, 128), blk("L16", s, 32)), (("PK", 80, 96), ("nIb", 0, 128), G),
-               (("PK", 96, 112), ("Ib", 0, 128), G)]
+        act(G, ("PK", 16, 32), AF.Relu, bias=BIG, scale=-4 * BIG)
+        mm([(("PK", 64, 80), ID, ("KL", 32 * s, 32 * s + 16)), (("PK", 64, 80), ID, G)])
+        lst = [(("PK", 80, 112), ID, blk("L16", s, 32)), (("PK", 80, 96), ID, G), (("PK", 96, 112), NID, G)]
         if s >= 2:
-            lst.append((("PK", 96, 112), ("nIb", 0, 128), blk("rs", s, 16)))
+            lst.append((("PK", 96, 112), NID, blk("rs", s, 16)))
         mm(lst)
         ts(("KL", 32 * t + 16, 32 * t + 32), ("PK", 96, 112), -BIG, AL.max)
-        tt(blk("tmn", s, 32), ("PK", 64, 96), blk("dmn", s // 2, 32), AL.min)
-        ts(blk("o12", s, 32), blk("tmn", s, 32), float(CEN), AL.add)
+        tt(blk("tmn", s, 32), ("PK", 64, 96), blk("cst", s // 2, 32), AL.min)
+        ts(blk("o12", s, 32), blk("tmn", s, 32), CEN + 0.25, AL.add)
 
-    def lowest(t):
-        parts = [h for h in range(2) if (t < STEPS if h == 0 else t > 0)]
+    def lowest(t, parts=(0, 1)):
+        parts = [h for h in parts if (t < STEPS if h == 0 else t > 0)]
         p0, p1 = parts[0], parts[-1] + 1
         tag[0] = "lowe%d" % t
-        rows = {0: (("BOh", "M0", 0) if t == 0 else ("BOb", "XR", 512 * t)), 1: ("BOh", "M", 1024 * ((t - 1) % 2) + 256)}
+        rows = {0: ("XR", 512 * t), 1: ("M", 1024 * ((t - 1) % 2) + 256)}
         k0, k1 = 32 * t + 16 * p0, 32 * t + 16 * p1
-        lst = [(("PG", 256 * p0, 256 * p1), ("Ib", 0, 128), ("tri", 256 * p0, 256 * p1))]
-        for h in parts:
-            lst.append((("PG", 256 * h, 256 * h + 256), (rows[h][0], 0, 128), (rows[h][1], rows[h][2], rows[h][2] + 256)))
-        lst += [(("PG", 256 * p0 + r, 256 * p1, 16), ("nIh", 0, 128), ("KL", k0, k1)) for r in range(16)]
-        mm(lst)
-        act(("ab", 256 * p0, 256 * p1), ("PG", 256 * p0, 256 * p1), AF.Abs)
-        lst = [(("PH", 128 * p0, 128 * p1), ("Ib", 0, 128), ("cov", 128 * p0, 128 * p1))]
-        for h in parts:
-            for m in range(8):
-                c = rows[h][2] + 32 * m + 16
-                lst.append((("PH", 128 * h + 16 * m, 128 * h + 16 * m + 16), (rows[h][0], 0, 128), (rows[h][1], c, c + 16)))
-        lst += [(("PH", 128 * p0 + r, 128 * p1, 16), ("nIh", 0, 128), ("KL", k0, k1, 2)) for r in range(16)]
-        mm(lst)
-        act(("ab", 512 + 128 * p0, 512 + 128 * p1), ("PH", 128 * p0, 128 * p1), AF.Abs)
-        if len(parts) == 2:
-            act(("eq", 0, 768), ("ab", 0, 768), AF.Relu, bias=BIG, scale=-BIG)
+        mm([(("PG", 256 * p0 + r, 256 * p1, 16), blk("DL", r, 128), ("KL", k0, k1)) for r in range(16)], solo=True)
+        act(("eq", 256 * p0, 256 * p1), ("PG", 256 * p0, 256 * p1), AF.Sign, bias=0.5)
+        lst = []
+        if t == 0:
+            lst += [(("PH", r, 128, 16), m, ("KL", 1, 16, 2)) for r in range(16) for m in (blk("DL", r, 128), ID)]
         else:
-            act(("eq", 256 * p0, 256 * p1), ("ab", 256 * p0, 256 * p1), AF.Relu, bias=BIG, scale=-BIG)
-            act(("eq", 512 + 128 * p0, 512 + 128 * p1), ("ab", 512 + 128 * p0, 512 + 128 * p1), AF.Relu, bias=BIG, scale=-BIG)
+            for h in parts:
+                for m in range(8):
+                    c = rows[h][1] + 32 * m + 16
+                    lst.append((("PH", 128 * h + 16 * m, 128 * h + 16 * m + 16), ("BOb", 0, 128), (rows[h][0], c, c + 16)))
+        lst += [(("PH", 128 * p0 + r, 128 * p1, 16), NID, ("KL", k0, k1, 2)) for r in range(16)]
+        mm(lst)
+        act(("ab", 128 * p0, 128 * p1), ("PH", 128 * p0, 128 * p1), AF.Abs)
+        act(("eq", 512 + 128 * p0, 512 + 128 * p1), ("ab", 128 * p0, 128 * p1), AF.Relu, bias=4 * BIG, scale=-8 * BIG)
         c0, c1 = 128 + 16 * p0, 128 + 16 * p1
-        mm([(("PK", c0, c1), ("Ih", 0, 128), ("KL", k0, k1))]
-           + [(("PK", c0, c1), sel("nFb", r), ("eq", 256 * p0 + r, 256 * p1, 16)) for r in range(16)]
+        mm([(("PK", c0, c1), ID, ("KL", k0, k1))]
+           + [(("PK", c0, c1), tri(r), ("eq", 256 * p0 + r, 256 * p1, 16)) for r in range(16)]
            + [(("PK", c0 + 1, c1, 2), sel("nFb", r), ("eq", 512 + 128 * p0 + r, 512 + 128 * p1, 16)) for r in range(16)])
-        tt(("tmx", k0, k1), ("PK", c0, c1), ("dmx", 16 * p0, 16 * p1), AL.max)
-        ts(("o03", k0, k1), ("tmx", k0, k1), float(CEN + 256), AL.add)
+        tt(("tmx", k0, k1), ("PK", c0, c1), ("cst", 96 + 16 * p0, 96 + 16 * p1), AL.max)
+        ts(("o03", k0, k1), ("tmx", k0, k1), CEN + 256 + (0.1 if t % 2 else 0.35), AL.add)
 
     def names(t):
         b = 512 * t
         tag[0] = "name%d" % t
         au = blk("au", t, 16)
-        act(("nm", b, b + 256), ("IT", 256, 1280), AF.Copy, off=au)
-        act(("nm", b + 256, b + 512), ("OT", 256, 1280), AF.Copy, off=au)
-        if t > 0:
-            ts(("n16", b, b + 512), ("nm", b, b + 512), float(CEN), AL.add)
+        p, q = b + 256 * (t % 2), b + 256 * (1 - t % 2)
+        P, Q = ("nm", p, p + 256), ("nm", q, q + 256)
+        lean = -0.2 if t % 2 else 0.2
+        if t == 0:
+            ts(Q, ("n16", q, q + 256), lean - CEN, AL.add)
+            ts(P, ("n16", p, p + 256), float(OFF), AL.add)
+        else:
+            act(Q, ("IT" if t % 2 else "OT", 256, 1280), AF.Identity, bias=lean - OFF - CEN, off=au)
+            act(P, ("OT" if t % 2 else "IT", 256, 1280), AF.Copy, off=au)
+            ts(("n16", q, q + 256), Q, CEN - lean + 0.25, AL.add)
+            ts(("n16", p, p + 256), P, 0.25 - OFF, AL.add)
         if t == STEPS:
             return
-        act(("PC", 0, 512), ("nm", b, b + 512), AF.Copy)
         m = 1024 * (t % 2)
-        p, q = 256 * (t % 2), 256 * (1 - t % 2)
-        ohk, ohj = ("oh", b, b + 256), ("oh", b + 256, b + 512)
-        tt(("M", m + 768, m + 1024), ("PC", 0, 256), ("nm", b + 256, b + 512), AL.is_gt)
-        tt(("M", m, m + 256), ("PC", p, p + 256), ohk, AL.mult)
-        tt(("M", m + 256, m + 512), ("PC", q, q + 256), ohj, AL.mult)
-        tt(("M", m + 512, m + 768), ("PC", p, p + 256), ohj, AL.mult)
-        mm([(("PL", 0, 64), sel("Fh", r), ("M", m + r, m + 1024, 16)) for r in range(16)]
-           + [(("PL", 48, 64), ("nIb", 0, 128), blk("hl", t, 16))])
-        act(blk("sg", t, 16), ("PL", 48, 64), AF.Sign, bias=0.5)
+        ohk, ohj = (blk("oh", t, 256), blk("oh", 5 + t, 256)) if t else (blk("oh0", 0, 256), blk("oh0", 1, 256))
+        PC, OJ = ("PC", 0, 256), ("PC", 256, 512)
+        mm([(OJ, ID, ohj)])
+        act(PC, P, AF.Identity, bias=-float(OFF + CEN))
+        tt(("M", m + 512, m + 768), PC, Q, AL.is_lt if t % 2 else AL.is_gt)
+        tt(("M", m, m + 256), PC, ohk, AL.mult)
+        tt(("M", m + 256, m + 512), OJ, Q, AL.mult)
+        tt(("M", m + 768, m + 1024), PC, ohj, AL.mult)
+        mm([(("PL", 0, 64), sel("Fb", r), ("M", m + r, m + 1024, 16)) for r in range(16)] + [(("PL", 32, 48), NID, blk("hl", t, 16))])
+        act(blk("sg", t, 16), ("PL", 32, 48), AF.Sign, bias=0.5)
         if t >= 2:
-            act(blk("rs", t, 16), ("PL", 32, 48), AF.Relu, bias=-BIG * (n0(t - 2) - CEN - 1), scale=BIG)
-        mm([(("PL", 64, 80), ("I5", 0, 128), blk("sg", t, 16)), (("PL", 64, 80), ("Ih", 0, 128), ("KL", 32 * t, 32 * t + 16))])
-        ts(blk("idx", t, 16), ("PL", 64, 80), float(CEN + 512), AL.add)
+            act(blk("rs", t, 16), ("PL", 48, 64), AF.Relu, bias=-4 * BIG * (n0(t - 2) - CEN - 0.5), scale=4 * BIG)
         cp(blk("L16", t, 32), ("PL", 0, 32))
-        ts(blk("pju", t, 16), ("PL", 32, 48), float(CEN), AL.add)
-        au2 = blk("idx", t, 16)
-        add("s", 65 + 256 * GA * CYC,
-            lambda g, T, X: g.scalar.activation(ap(T, blk("xs", t, 256)), T.NX[:, 0:2048].indirect(ap(T, au2)), AF.Copy),
-            [("NX", 0, 2048), ("NXp", 0, 2), au2], [blk("xs", t, 256)])
+        mm([(("PL", 64, 80), ("I5", 0, 128), blk("sg", t, 16)), (("PL", 64, 80), ("I5", 0, 128), ("one", 0, 16)),
+            (("PL", 64, 80), ID, ("KL", 32 * t, 32 * t + 16))])
+        ts(blk("pj", t, 32), ("PL", 48, 80), CEN + 0.25, AL.add)
+        act(blk("xs", t, 256), ("NX", 0, 2048), AF.Copy, off=("pj", 32 * t + 16, 32 * t + 32), more=[("NXp", 0, 2)])
         send("ax%d" % t, blk("xs", t, 256), ("XR", 512 * (t + 1), 512 * (t + 1) + 256), 65536)
+        tag[0] = "fres%d" % t
+        E = ("PH", 256, 512)
+        mm([(E, blk("In", t // 2, 128), ohk), (E, ("one", 0, 128, 1, 0, 1), ("irow", 0, 256, 1, 0, 1))])
+        tt(blk("nw", t % 2, 256), E, P, AL.max)
 
     def switch(t):
         tab = "IT" if t % 2 == 0 else "OT"
-        p = 512 * t + 256 * (t % 2)
         tag[0] = "swit%d" % t
         for m in range(7, -1, -1):
-            tts((tab, 0, 1280), ("o03", 32 * t + 2 * m, 32 * t + 2 * m + 2), ("nm", p + 32 * m, p + 32 * m + 32),
-                ("ohn", 256 * t + 32 * m, 256 * t + 32 * m + 32), AL.max)
-        act(("XR", 512 * (t + 1) + 256, 512 * (t + 1) + 512), (tab, 256, 1280), AF.Relu, bias=-BIG * (n0(t) - CEN - 1), scale=BIG,
-            off=blk("au", t, 16))
+            c = 256 * (t % 2) + 32 * m
+            scatter("v" if m < ONV else "s", (tab, 0, 1280), ("o03", 32 * t + 2 * m, 32 * t + 2 * m + 2), ("nw", c, c + 32))
+        act(("XR", 512 * (t + 1) + 256, 512 * (t + 1) + 512), (tab, 256, 1280), AF.Relu, bias=0.75 - n0(t) - OFF, off=blk("au", t, 16))
 
     def filled(tab, t):
         return 256 + W0 + B * ((t + 1) // 2 if tab == "U" else t // 2)
@@ -388,7 +392,7 @@ def build(CYC, PCY, GA, SC, RL):
         tag[0] = "early%d" % t
         for c in range(NS - 1, -1, -1):
             o = 4096 * (t % 3) + n * c
-            act(("py", o, o + n), (tab, 256, filled(tab, t)) if t else ("Vb", 0, W0), AF.Copy,
+            act(("py", o, o + n), (tab, 256, filled(tab, t)) if t else ("Vb", 0, W0), AF.Copy, scale=0.0625 if t < STEPS else 1.0,
                 off=("n16", q + c * n // 16, q + (c + 1) * n // 16))
 
     def late(t):
@@ -412,8 +416,9 @@ def build(CYC, PCY, GA, SC, RL):
                 while todo[0][0] == bank and todo[0][2] > 64 * h:
                     tail(t, *todo.pop(0))
                 col += 64 * h - lo
+                tag[0] = "sums%d" % t
                 for k0 in range(0, 16, 4):
-                    mm([((bank, col, col + 64), ("idf", 0, 128), ("prod", o + 1024 * h + k, o + 1024 * h + 1024, 16))
+                    mm([((bank, col, col + 64), ("id16" if t < STEPS else "idf", 0, 128), ("prod", o + 1024 * h + k, o + 1024 * h + 1024, 16))
                         for k in range(k0, k0 + 4)], True, k0 == 0, k0 == 12)
         for x in todo:
             tail(t, *x)
@@ -425,15 +430,15 @@ def build(CYC, PCY, GA, SC, RL):
         act(blk("cn", t, 256), (X, 256, f + 256), AF.Copy, off=("o12", 32 * t + 16, 32 * t + 32))
         Y = "V" if t % 2 == 0 else "U"
         send("ac%d" % t, blk("cn", t, 256), (Y, filled(Y, t), filled(Y, t) + 256) if t < STEPS - 1 else ("fcl", 0, 256), 131072)
-        act(blk("yk", t % 2, 256), ("py", oy, oy + 4096), AF.Copy, scale=0.0625, off=blk("kj", t, 16))
-        act(blk("yj", t % 2, 256), ("py", oy, oy + 4096), AF.Copy, off=blk("kj", 5 + t, 16))
-        act(("PB", 256, 512), (X, f, f + 256), AF.Copy)
-        tt(("PB", 256, 512), blk("cn", t, 256), ("PB", 256, 512), AL.subtract)
-        tt(("more", 0, 256), ("PB", 256, 512), blk("yk", t % 2, 256), AL.mult)
-        tts(("BT", 0, 1280), ("o12", 32 * t, 32 * t + 16), blk("bg", t % 3, 256), ("more", 0, 256), AL.add)
+        act(blk("yj", t % 2, 256), ("py", oy, oy + 4096), AF.Copy, scale=16.0, off=blk("kj", 5 + t, 16))
+        act(CB, (X, f, f + 256), AF.Copy)
+        act(("dd", 0, 256), ("py", oy, oy + 4096), AF.Copy, off=blk("kj", t, 16))
+        tt(CB, blk("cn", t, 256), CB, AL.subtract)
+        tt(("more", 0, 256), CB, ("dd", 0, 256), AL.mult)
+        tts(("BT", 0, 1792), ("o12", 32 * t, 32 * t + 16), blk("bg", t % 3, 256), ("more", 0, 256), AL.add)
         for h in (1, 0):
             tag[0] = "w%d%d" % (t, h)
-            ttg(("w", 128 * h, 128 * h + 128), (X, 256, f), blk("pju", 2 * t + h, 8), blk("z", 2 * t + h, 128), AL.mult)
+            ttg(blk("w", h, 128), (X, 256, f), ("pj", 32 * t + 8 * h, 32 * t + 8 * h + 8), blk("z", 2 * t + h, 128), AL.mult)
 
     def tail(t, bank, col, lo, hi):
         Y = "V" if t % 2 == 0 else "U"
@@ -469,11 +474,12 @@ def build(CYC, PCY, GA, SC, RL):
         tag[0] = "bg%d" % t
         act(blk("bg", t % 3, 256), ("BT", 0, 1024), AF.Copy, off=blk("au", t, 16))
         if t < STEPS:
-            if t + 1 < STEPS:
-                masks(t + 1)
-            lists_in(t + 1)
+            if t < APART:
+                lists_in(t + 1, (1,))
+                lowest(t + 1, (1,))
+            lists_in(t + 1, (0,) if t < APART else (0, 1))
             names(t + 1)
-            lowest(t + 1)
+            lowest(t + 1, (0,) if t < APART else (0, 1))
             if t + 1 < STEPS:
                 switch(t + 1)
             early(t + 1)
@@ -495,18 +501,18 @@ def schedule():
         acc = [(r, False) for r in o["rd"]] + [(r, True) for r in o["wr"]]
         for r, wr in acc:
             for (i, c0, c1, iw) in seen.get(r[0], ()):
-                other = ops[i]["eng"] != o["eng"] or ops[i]["kind"] != "c" or o["kind"] != "c"
-                if r[0] in _P and other:
-                    deps[j][i] = True
-                elif r[0] in _P and o["eng"] == "p":
+                pe = o["eng"] == "p" and ops[i]["eng"] == "p"
+                if c0 < r[2] and r[1] < c1 and (wr or iw):
+                    deps[j][i] = deps[j].get(i, False) or not pe or (iw and not wr)
+                elif pe and o["tag"][:4] == ops[i]["tag"][:4] == "sums" and r[0] in _P:
                     deps[j].setdefault(i, False)
-                elif c0 < r[2] and r[1] < c1 and (wr or iw):
-                    deps[j][i] = deps[j].get(i, False) or other or (iw and not wr) or (SAMEQ and o["eng"] != "p")
         for r, wr in acc:
             seen.setdefault(r[0], []).append((j, r[1], r[2], wr))
-    for a, b in zip(range(NLOAD - 1), range(1, NLOAD)):
-        deps[b].setdefault(a, False)
-    eng = [o["eng"] for o in ops]
+    for a in range(n - 1):
+        if ops[a + 1]["tag"] == "load" and ops[a + 1]["eng"] == ops[a]["eng"]:
+            deps[a + 1].setdefault(a, False)
+    ei = ["vspgy".index(o["eng"]) for o in ops]
+    banks = [tuple(sorted(set(_P.index(r[0]) for r in o["rd"] + o["wr"] if r[0] in _P))) for o in ops]
     anc, near = [0] * n, []
     for j in range(n):
         far = 0
@@ -519,47 +525,74 @@ def schedule():
     sets = []
     for oo, lat in others:
         sets.append(([o["cost"] for o in oo], [o["lat"] for o in oo],
-                     [[(i, oo[i]["lat"] + lat if w else 0.0) for i, w in near[j].items()] for j in range(n)]))
-    cost, tail, pred = sets[0]
-    back = [[] for _ in range(n)]
-    for j in range(n):
-        for i, d in pred[j]:
-            back[i].append((j, d))
+                     [[(i, oo[i]["lat"] + lat if w else 0.0) for i, w in near[j].items()] for j in range(n)], lat))
+    backs = []
+    for s in sets:
+        backs.append([[] for _ in range(n)])
+        for j in range(n):
+            for i, d in s[2][j]:
+                backs[-1][i].append((j, d))
+    cost, tail, pred = sets[0][:3]
+    back = backs[0]
+    ends = [j for j in range(n) if not back[j]]
+    norm = [max(sum(c for c, e in zip(s[0], ei) if e == x) for x in range(5)) for s in sets]
 
-    def place(seq, pr, first):
-        busy = {e: [] for e in "vspgy"}
-        st = [0.0] * n
-        for j in seq:
-            t = first[j]
-            for i, d in pr[j]:
-                x = st[i] + cost[i] + d
-                if x > t:
-                    t = x
-            b, c = busy[eng[j]], cost[j]
-            k = len(b)
-            while k > 0 and b[k - 1][1] > t:
-                k -= 1
-            while k < len(b) and b[k][0] < t + c:
-                t = max(t, b[k][1])
-                k += 1
-            b.insert(k, (t, t + c))
-            st[j] = t
-        return st
-
-    def replay(seq):
-        tot = 0.0
-        for c, tl, pr in sets:
-            free = {e: 0.0 for e in "vspgy"}
-            en = [0.0] * n
-            for j in seq:
-                t = free[eng[j]]
+    def run(seq, k0, old):
+        lq, lb = [-1] * 5, [-1] * 8
+        for j in seq[:k0]:
+            lq[ei[j]] = j
+            for b in banks[j]:
+                lb[b] = j
+        out, tot, rest = [], 0.0, seq[k0:]
+        for (c, tl, pr, lat), (en0, why0), nm in zip(sets, old, norm):
+            en, why, q, bk = list(en0), list(why0), list(lq), list(lb)
+            for j in rest:
+                e = ei[j]
+                w = q[e]
+                t = en[w]
                 for i, d in pr[j]:
                     x = en[i] + d
                     if x > t:
-                        t = x
-                en[j] = free[eng[j]] = t + c[j]
-            tot += max(en[j] + tl[j] for j in range(n)) / sum(c)
-        return tot
+                        t, w = x, i
+                for b in banks[j]:
+                    i = bk[b]
+                    if ei[i] != e and en[i] + lat > t:
+                        t, w = en[i] + lat, i
+                    bk[b] = j
+                en[j], why[j], q[e] = t + c[j], w, j
+            tot += (max([en[j] + tl[j] for j in ends]) + SOON * sum(en) / n) / nm
+            out.append((en, why))
+        return tot, out
+
+    ei.append(-1)
+    blank = [([0.0] * (n + 1), [-1] * (n + 1))] * len(sets)
+
+    def place(seq, pr, first, c, lat):
+        busy, held, st = [[] for _ in range(5)], [[] for _ in range(8)], [0.0] * n
+        for j in seq:
+            t, e, cj = first[j], ei[j], c[j]
+            for i, d in pr[j]:
+                x = st[i] + c[i] + d
+                if x > t:
+                    t = x
+            b, again = busy[e], True
+            while again:
+                k, again = len(b), False
+                while k > 0 and b[k - 1][1] > t:
+                    k -= 1
+                while k < len(b) and b[k][0] < t + cj:
+                    if b[k][1] > t:
+                        t = b[k][1]
+                    k += 1
+                for q in banks[j]:
+                    for s0, e0, x in held[q][-12:]:
+                        if x != e and s0 < t + cj + lat and e0 + lat > t:
+                            t, again = e0 + lat, True
+            b.insert(k, (t, t + cj))
+            for q in banks[j]:
+                held[q].append((t, t + cj, e))
+            st[j] = t
+        return st
 
     def topo_by(key):
         k2 = list(key)
@@ -569,53 +602,31 @@ def schedule():
                     k2[j] = k2[i] + 1e-3
         return sorted(range(n), key=lambda j: k2[j])
 
-    zero = [0.0] * n
-
-    def eager(key, eps):
-        left = [len(p) for p in pred]
-        ready, st = [0.0] * n, [0.0] * n
-        free = {e: 0.0 for e in "vspgy"}
-        pool = {e: [] for e in "vspgy"}
-        nxt = {e: 1e18 for e in "vspgy"}
-        for j in range(n):
-            if not left[j]:
-                pool[eng[j]].append(j)
-                nxt[eng[j]] = 0.0
-        for _ in range(n):
-            e = min(nxt, key=nxt.get)
-            t0, p = nxt[e] + eps, pool[e]
-            j = min((j for j in p if ready[j] <= t0), key=lambda j: key[j])
-            p.remove(j)
-            st[j] = max(nxt[e], ready[j])
-            f = free[e] = st[j] + cost[j]
-            for k, d in back[j]:
-                if f + d > ready[k]:
-                    ready[k] = f + d
-                left[k] -= 1
-                if not left[k]:
-                    pool[eng[k]].append(k)
-                    nxt[eng[k]] = min(nxt[eng[k]], max(free[eng[k]], ready[k]))
-            nxt[e] = max(f, min(ready[k] for k in p)) if p else 1e18
-        return st
-
-    def improve(key, k=2):
-        st = place(topo_by(key), pred, zero)
+    def improve(key, k, s):
+        c, tl, pr, lat = sets[s]
+        st = place(topo_by(key), pr, [0.0] * n, c, lat)
         for _ in range(k):
-            fw = sorted(range(n), key=lambda j: (st[j] + cost[j], j), reverse=True)
-            bk = place(fw, back, tail)
-            st = place(topo_by([-(bk[j] + cost[j]) for j in range(n)]), pred, zero)
+            bk = place(sorted(range(n), key=lambda j: (st[j] + c[j], j), reverse=True), backs[s], tl, c, lat)
+            st = place(topo_by([-(bk[j] + c[j]) for j in range(n)]), pr, [0.0] * n, c, lat)
         seq = sorted(range(n), key=lambda j: (st[j], j))
-        res = (replay(seq), seq, st)
-        s2 = eager(st, EPS)
-        seq = sorted(range(n), key=lambda j: (s2[j], j))
-        return min(res, (replay(seq), seq, s2), key=lambda x: x[0])
+        v, s2 = run(seq, 0, blank)
+        return v, seq, [s2[0][0][j] - cost[j] for j in range(n)]
 
     prio = [0.0] * n
     for i in range(n - 1, -1, -1):
         prio[i] = cost[i] + max([prio[j] + d for j, d in back[i]] + [tail[i]])
-    whole = [o["tag"][:4] in ("mask", "list", "lowe", "name", "swit") for o in ops]
-    best = min((improve([-p - (b if w else 0.0) for p, w in zip(prio, whole)]) for b in (0.0, 5e3, 1e4, 2e4, 4e4)), key=lambda x: x[0])
+    whole = [o["tag"][:4] in ("fres", "list", "lowe", "name", "swit") for o in ops]
+
+    def ahead(b):
+        key = [-p - (b if w else 0.0) for p, w in zip(prio, whole)]
+        for i in range(n - 1, -1, -1):
+            key[i] = min([key[i]] + [key[j] - d - cost[i] for j, d in back[i]])
+        return key
+
+    best = min((improve(ahead(b), k, s) for b in (0.0, 5e3, 1e4, 2e4) for k in (0, 1, 3) for s in (0, 1)), key=lambda x: x[0])
     tags = sorted(set(o["tag"] for o in ops))
+    kind = ["".join(x for x in o["tag"] if not x.isdigit()) for o in ops]
+    kinds = sorted(set(kind))
     cur, rnd = best, [SEED]
 
     def draw():
@@ -623,65 +634,68 @@ def schedule():
         return rnd[0] / 2147483648.0
 
     for it in range(ROUNDS):
-        amp = (100.0, 400.0, 1500.0)[it % 3]
-        mv = {tags[int(draw() * len(tags))]: (draw() - 0.5) * 12000.0 for _ in range(1 + it % 4)}
-        new = improve([cur[2][j] + amp * draw() + mv.get(ops[j]["tag"], 0.0) for j in range(n)], it % 2)
-        if new[0] < cur[0] * 1.001:
+        amp = (30.0, 100.0, 400.0)[it % 3]
+        mv = {tags[int(draw() * len(tags))]: (draw() - 0.5) * 8000.0 for _ in range(int(draw() * 3))}
+        mk = {kinds[int(draw() * len(kinds))]: (draw() - 0.5) * 6000.0 for _ in range(int(draw() * 1.5))}
+        new = improve([cur[2][j] + amp * draw() + mv.get(ops[j]["tag"], 0.0) + mk.get(kind[j], 0.0) for j in range(n)],
+                      it % 2, int(draw() * len(sets)))
+        if new[0] < cur[0] + 0.004 * draw():
             cur = new
         if new[0] < best[0]:
             best = new
-    ei = ["vspgy".index(e) for e in eng]
-    norm = [sum(s[0]) for s in sets]
-    ends = [j for j in range(n) if not back[j]]
 
-    def run(seq, k0, old):
-        out, tot = [], 0.0
-        for (c, tl, pr), en0, nm in zip(sets, old, norm):
-            en, free, k = list(en0), [-1.0] * 5, k0 - 1
-            miss = 5
-            while k >= 0 and miss:
-                if free[ei[seq[k]]] < 0:
-                    free[ei[seq[k]]] = en[seq[k]]
-                    miss -= 1
-                k -= 1
-            for j in seq[k0:]:
-                e = ei[j]
-                t = free[e]
-                for i, d in pr[j]:
-                    x = en[i] + d
-                    if x > t:
-                        t = x
-                en[j] = free[e] = t + c[j]
-            tot += (max([en[j] + tl[j] for j in ends]) + 0.1 * sum(en) / n) / nm
-            out.append(en)
-        return tot, out
+    def shift(seq, a, b, up):
+        mid = seq[a:b + 1]
+        if up:
+            m = anc[seq[b]] | 1 << seq[b]
+            return seq[:a] + [x for x in mid if m >> x & 1] + [x for x in mid if not m >> x & 1] + seq[b + 1:]
+        i = seq[a]
+        go = [x == i or anc[x] >> i & 1 for x in mid]
+        return seq[:a] + [x for x, f in zip(mid, go) if not f] + [x for x, f in zip(mid, go) if f] + seq[b + 1:]
 
-    seq = list(best[1])
-    val, en = run(seq, 0, [zero] * len(sets))
-    top = (val, list(seq), en)
+    seq = best[1]
+    val, st = run(seq, 0, blank)
+    top = (val, seq, st)
+    arcs = None
     for it in range(MOVES):
-        a = int(draw() * n)
-        j, step, hops = seq[a], (1 if draw() < 0.5 else -1), 1 + int(draw() * draw() * 6)
-        b = a
-        while hops and 0 <= b + step < n:
-            i = seq[b + step]
-            if (anc[i] >> j & 1) if step > 0 else (anc[j] >> i & 1):
-                break
-            b += step
-            hops -= ei[i] == ei[j]
-        if hops:
+        if draw() < ONPATH:
+            if arcs is None:
+                arcs, pos = [], [0] * n
+                for k, j in enumerate(seq):
+                    pos[j] = k
+                for (en, why), s in zip(st, sets):
+                    j = max(ends, key=lambda j: en[j] + s[1][j])
+                    while why[j] >= 0:
+                        if not anc[j] >> why[j] & 1:
+                            arcs.append((why[j], j))
+                        j = why[j]
+            i, j = arcs[int(draw() * len(arcs))]
+            a, b, up = pos[i], pos[j], draw() < 0.5
+            far = int(draw() * draw() * 40)
+            if up:
+                a = max(0, a - far)
+            else:
+                b = min(n - 1, b + far)
+        else:
+            a = int(draw() * (n - 1))
+            b, up = min(n - 1, a + 1 + int(draw() * draw() * 40)), draw() < 0.5
+        new = shift(seq, a, b, up)
+        if new == seq:
             continue
-        new = list(seq)
-        new.insert(b, new.pop(a))
-        v2, en2 = run(new, min(a, b), en)
-        if v2 <= val + 0.0004 * (1.0 - it / MOVES) * draw():
-            seq, val, en = new, v2, en2
+        v2, s2 = run(new, a, st)
+        if v2 <= val + HEAT * (1.0 - it / MOVES) ** 2 * draw():
+            seq, val, st, arcs = new, v2, s2, None
             if val < top[0]:
-                top = (val, list(seq), en)
-    order = top[1]
-    start = [top[2][0][j] - cost[j] for j in range(n)]
-    best = (replay(order),)
-    done = [start[j] + cost[j] + tail[j] for j in range(n)]
+                top = (val, seq, st)
+    order, st = top[1], top[2]
+    start = [st[0][0][j] - cost[j] for j in range(n)]
+    done = [st[0][0][j] + tail[j] for j in range(n)]
+    last = [-1] * 8
+    for j in order:
+        for b in banks[j]:
+            if last[b] >= 0 and ei[last[b]] != ei[j]:
+                deps[j][last[b]] = True
+            last[b] = j
     token, count, nd = {}, {e: 0 for e in "vspg"}, 0
     known = {e: {} for e in "vspgy"}
     clock, waits = {}, {}
@@ -699,6 +713,8 @@ def schedule():
         if o["kind"] == "c":
             count[e] += 1
             token[j] = ("q" + e, count[e])
+        elif o["kind"] == "d" and o["name"]:
+            token[j] = (o["name"], 16 * sum(x["name"] == o["name"] for x in ops))
         elif o["kind"] == "d":
             token[j] = ("d%d" % nd, 16)
             nd += 1
@@ -708,7 +724,8 @@ def schedule():
             token[j] = (o["name"], 8)
         clock[j] = {} if o["kind"] == "r" else dict(known[e])
         clock[j][token[j][0]] = token[j][1]
-    return ops, {"score": best[0], "order": order, "waits": waits, "token": token, "count": count, "start": start, "done": done, "nd": nd}
+    spans = [max(en[j] + s[1][j] for j in ends) for (en, why), s in zip(st, sets)]
+    return ops, {"spans": spans, "order": order, "waits": waits, "token": token, "count": count, "start": start, "done": done}
 
 
 _PLAN = {}
@@ -727,7 +744,7 @@ def rank_program(g, core, T, topo):
         rid, pid, _ = topo.addr(d)
         eng = topo.engines(core, d)
         k = len(eng) // 2
-        to.append((rid, pid, sum(1 << e for e in eng[h * k:h * k + 4])))
+        to.append((rid, pid, sum(1 << e for e in eng[h * k:h * k + k])))
     X = {"to": to}
     q = {"v": g.vector, "s": g.scalar, "p": g.tensor, "g": g, "y": g.sync}
     outs = sends = 0

@@ -7,9 +7,20 @@ A, W0, B, STEPS = 1024, 1792, 256, 5
 OFF = 256
 CEN = 1280
 BIG = 4096.0
+ROUND = 1.5 * 2.0 ** 23
 NS, NV = 4, 4
 APART = 1
 ONV = 0
+CFG = {
+    "ysum": "DDDDB",
+    "clip": "VSSSS",
+    "spare": "11111",
+    "equal": "VVMMMM",
+    "scan": 96, "help": [[]] * 5 + [["PC", "PG", "PL", "PK"]],
+    "copy": [], "votes": [], "fresh": "PL", "zero": "D", "w": [[256, 0]] + [[256, 128, 0]] * 4,
+    "early": 32, "late": [256, 192, 128, 64, 0], "last": [256, 176, 96, 0],
+    "parts": [256, 128, 64, 0], "units": [256, 192, 128, 64, 0], "close": [256, 176, 96],
+}
 
 F32, BF, F16, U16, I32 = "float32", "bfloat16", "float16", "uint16", "int32"
 _S = {
@@ -18,46 +29,64 @@ _S = {
     "cmpi": (240, I32), "cmpb": (240, BF), "nxi": (128, I32), "nxh": (256, I32), "nxc": (256, BF),
     "NX": (2048, BF), "R1": (3840, BF), "RR": (2560, BF), "zsb": (256, BF), "tgb": (256, BF),
     "py": (3 * 4096, F32), "prod": (4096, F32),
-    "oh": (2560, BF), "oh0": (512, BF), "dd": (256, F32), "id16": (128, F32), "trb": (288, BF), "nw": (512, F32), "kj": (160, U16), "hl": (80, BF),
+    "oh": (2560, BF), "oh0": (512, BF), "id16": (128, F32), "nw": (512, F32), "kj": (160, U16), "hl": (80, BF),
     "nm": (6 * 512, F32), "n16": (6 * 512, U16), "M": (2 * 1024, F16),
     "XR": (6 * 512, BF), "xs": (5 * 256, BF), "au": (6 * 16, U16), "KL": (6 * 32, F16), "L16": (5 * 32, F16),
     "pj": (5 * 32, U16), "sg": (5 * 16, BF), "rs": (5 * 16, BF), "Gs": (5 * 16, BF),
     "tmn": (5 * 32, F32), "o12": (5 * 32, U16), "tmx": (6 * 32, F32), "o03": (6 * 32, U16),
-    "ab": (256, BF), "eq": (768, BF),
+    "ab": (512, BF), "eq": (512, BF), "dq": (2 * 256, F32), "bgt": (2 * 256, F32), "ntg": (256, F32), "sz": (2 * 256, F32),
+    "cm": (256, F32),
     "seg": (1024, BF), "bg": (3 * 256, F32), "yj": (2 * 256, F32), "cn": (5 * 256, F32), "more": (256, F32),
-    "w": (256, F32), "less": (256, F32), "y": (6 * 256, F32), "r1": (256, F32), "r2": (256, F32),
+    "w": (256, F32), "less": (256, F32), "y": (6 * 256, F32), "r1": (256, F32),
     "zo": (5 * 256, F32), "z": (6 * 256, F32), "fcl": (256, F32),
-    "pi": (8, I32), "pc": (8, F32), "pb": (8, BF), "one": (144, BF), "idf": (128, F32), "bot": (128, BF), "Zb": (128, BF),
+    "pi": (8, I32), "pc": (8, F32), "pb": (8, BF), "one": (144, BF), "idf": (128, F32), "bot": (128, BF), "Tb": (128, BF),
     "Ib": (128, BF), "nIb": (128, BF), "I5": (128, BF), "In": (384, BF), "BOb": (128, BF), "Fb": (144, BF), "nFb": (144, BF),
     "Sel": (144, BF), "irow": (256, BF), "cf": (16, F32), "csf": (144, F32), "cs": (144, F32), "seatb": (16, BF),
-    "s16f": (160, F32), "s16": (160, BF), "colb": (32, BF), "colf": (16, F32), "DL": (2048, BF), "TR": (2304, BF),
+    "s16f": (160, F32), "s16": (160, BF), "colb": (16, BF), "colf": (16, F32), "RT": (1024, BF), "LS": (1024, BF),
+    "R3": (256, BF), "Br": (512, BF),
 }
+_D3 = ("M", "R3")
 _S["cst"] = _S.pop("cs")
 _P = ["PA", "PB", "PC", "PG", "PH", "PL", "PK", "PE"]
-SCRATCH = {k: ("sbuf", [128, v[0]], v[1]) for k, v in _S.items()}
+SCRATCH = {k: ("sbuf", [128, v[0] // 32, 32] if k in _D3 else [128, v[0]], v[1]) for k, v in _S.items()}
 for _b in _P:
     SCRATCH[_b] = ("psum", [128, 512], F32)
 SCRATCH["RD"] = ("dram", [8, 2560], BF)
-NDMA = 24
+NDMA = 72
 SEMAPHORES = (["qv", "qs", "qp", "qg", "sent", "outs", "rd", "rr"] + ["d%d" % i for i in range(NDMA)]
               + ["a%s%d" % (k, t) for k in "xc" for t in range(STEPS)] + ["az%d%d" % (t, h) for t in range(STEPS) for h in range(2)])
 
-COSTS = [(0.85, 0.43, 1.56, 3.8, 3000.0, 150.0), (0.95, 0.48, 1.15, 2.2, 4000.0, 200.0), (1.15, 0.58, 1.9, 5.2, 3000.0, 120.0),
-         (1.1, 0.56, 1.5, 3.5, 5500.0, 250.0)]
-ROUNDS, MOVES, SEED, SOON, ONPATH, HEAT = 3000, 35000, 1, 0.1, 0.6, 0.001
-PARTS = [("PA", 0, 128, 256), ("PE", 0, 64, 128), ("PB", 0, 0, 64)]
+COSTS = [(0.85, 0.43, 1.56, 3.8, 3000.0, 700.0, 2000.0, 150.0), (0.95, 0.48, 1.15, 2.2, 4000.0, 1000.0, 2500.0, 200.0),
+         (1.15, 0.58, 1.9, 5.2, 3000.0, 700.0, 2000.0, 120.0), (1.1, 0.56, 1.5, 3.5, 5500.0, 1000.0, 2800.0, 250.0)]
+ROUNDS, SWEEPS, MOVES, SEED, SOON, EVEN, ONPATH, HEAT = 200, (20, 5, 3), 250, 1, 0.02, 0.3, 0.6, 0.004
+JOIN, SWAP, WEIGHTS = 60.0, 0.1, (1.0, 1.0, 1.0, 1.0)
+WINDOWS = (60, 100, 40, 140)
+FIRST, STEP = 5700.0, 12300.0
+PLAN = {"late": 0.0, "sums": 1400.0, "tail": 6000.0, "earl": -3000.0, "clip": 9000.0, "side": 3000.0, "help": 0.0, "scan": 5000.0,
+        "list": -6000.0, "name": -5000.0, "lowe": -4000.0, "fres": -3500.0, "swit": -2000.0}
+LEADS = []
+AHEAD = (5e3, 1e4)
+TRIES = []
+SUMS = ["PA", "PE", "PB"]
 CB = ("PL", 256, 512)
+BT0 = ("PH", 0)
+
+
+CUTS = {}
 
 
 def n0(t):
     return W0 + B * (t // 2)
 
 
-def build(CYC, PCY, GA, SC, RL):
+def build(CYC, PCY, GA, SC, RL, GD, DL):
     ops = []
     tag = ["0"]
 
     def ap(T, r):
+        if r[0] in _D3:
+            x = slice(r[4], r[4] + 16) if len(r) == 5 else slice(r[1] % 32, 32, r[3] if len(r) == 4 else 1)
+            return T[r[0]][:, r[1] // 32:r[2] // 32, x]
         if len(r) == 3:
             return T[r[0]][:, r[1]:r[2]]
         if len(r) == 4:
@@ -92,13 +121,10 @@ def build(CYC, PCY, GA, SC, RL):
         add("v", 50 + width(a) * SC * CYC,
             lambda g, T, X: g.vector.tensor_tensor(ap(T, win).indirect(ap(T, off)), ap(T, a), ap(T, b), op), [off, a, b], [win])
 
-    def scatter(eng, win, off, a):
-        if eng == "v":
-            add("v", 50 + width(a) * SC * CYC,
-                lambda g, T, X: g.vector.tensor_copy(ap(T, win).indirect(ap(T, off)), ap(T, a)), [off, a], [win])
-        else:
-            add("s", 65 + width(a) * SC * CYC,
-                lambda g, T, X: g.scalar.activation(ap(T, win).indirect(ap(T, off)), ap(T, a), AF.Silu), [off, a], [win])
+    def scatter(win, off, a):
+        add("s", 65 + width(a) * SC * CYC,
+            lambda g, T, X: g.scalar.activation(ap(T, win).indirect(ap(T, off)), ap(T, a), AF.Silu), [off, a], [win])
+        ops[-1]["alt"] = (50 + width(a) * SC * CYC, lambda g, T, X: g.vector.tensor_copy(ap(T, win).indirect(ap(T, off)), ap(T, a)))
 
     def ts(out, a, s1, op0, s2=None, op1=None, more=()):
         rd = [a] + [s for s in (s1, s2) if isinstance(s, tuple)]
@@ -121,7 +147,7 @@ def build(CYC, PCY, GA, SC, RL):
     def mset(out, v):
         add("v", vcost(width(out), short(out)), lambda g, T, X: g.vector.memset(ap(T, out), v), [], [out])
 
-    def act(out, a, f, bias=0.0, scale=1.0, off=None, more=(), extra=0.0):
+    def act(out, a, f, bias=0.0, scale=1.0, off=None, more=(), extra=0.0, same=None):
         rd = [a] + ([off] if off else []) + [x for x in (bias, scale) if isinstance(x, tuple)] + list(more)
 
         def fn(g, T, X):
@@ -130,9 +156,20 @@ def build(CYC, PCY, GA, SC, RL):
             ss = ap(T, scale) if isinstance(scale, tuple) else scale
             return g.scalar.activation(ap(T, out), x, f, bias=bb, scale=ss)
         add("s", extra + (65 + width(out) * GA * CYC if off else vcost(width(out))), fn, rd, [out])
+        if f in (AF.Copy, AF.Identity):
+            same = (scale, AL.mult, bias, AL.add)
+        elif f == AF.Relu and scale == 1.0:
+            same = (bias, AL.add, 0.0, AL.max)
+        if same:
+
+            def other(g, T, X):
+                x = ap(T, a).indirect(ap(T, off)) if off else ap(T, a)
+                s1, s2 = [ap(T, s) if isinstance(s, tuple) else s for s in same[::2]]
+                return g.vector.tensor_scalar(ap(T, out), x, s1, s2, same[1], same[3])
+            ops[-1]["alt"] = (50 + width(out) * GA * CYC if off else vcost(width(out), short(out, *rd)), other)
 
     def mm(lst, f32=False, first=True, last=True, solo=False):
-        cost = sum(max(64, width(m[2])) for m in lst) * (4 if f32 else 1) * PCY + (40 if last else 0)
+        cost = sum(max(64, width(m[2])) * (4 if _S[m[2][0]][1] == F32 else 1) for m in lst) * PCY + (40 if last else 0)
 
         def fn(g, T, X):
             ins = None
@@ -145,7 +182,14 @@ def build(CYC, PCY, GA, SC, RL):
     def dma(q, fo, fi, rd, wr, nbytes, kind="d", name=""):
         def fn(g, T, X):
             return {"g": g, "y": g.sync, "s": g.scalar}[q].dma_start(fo(T), fi(T))
-        add(q, 700.0 if q == "g" else 100.0, fn, rd, wr, kind, 2000.0 + nbytes / 600.0, name)
+        add(q, GD if q == "g" else 100.0, fn, rd, wr, kind, DL + nbytes / 600.0, name)
+
+    def dcopy(out, a):
+        dma("y", lambda T: ap(T, out), lambda T: ap(T, a), [a], [out], 512 * width(out))
+
+    def dadd(out, a):
+        add("g", GD, lambda g, T, X: g.dma_start(ap(T, out), ap(T, a), accum_op=AL.add), [a, out], [out], "d",
+            DL + 300.0 + 2 * 512 * width(out) / 600.0)
 
     def iota(out, pat, base, cm):
         fl = _S[out[0]][1] != I32
@@ -160,22 +204,18 @@ def build(CYC, PCY, GA, SC, RL):
         add("g", 170 + 2 * width(out) * CYC,
             lambda g, T, X: g.affine_select(ap(T, out), ap(T, a), pat, op, fill, base, cm), [a], [out])
 
-    def send(sem, src, dst, nbytes, halves=(0, 1)):
-        if len(halves) == 1:
-            h = halves[0]
-            add("g", 300.0, lambda g, T, X: g.remote_dma(ap(T, dst), ap(T, src), T.sem[sem], T.sem["sent"], X["to"][h][1], X["to"][h][0],
-                                                         X["to"][0][2] | X["to"][1][2]), [src], [dst], "r", RL + nbytes / 100.0, sem)
-            return
-
+    def send(sem, srcs, dst, nbytes, halves=(0, 1), alu=0):
         def fn(g, T, X):
             tr = []
-            for h in range(2):
+            for i, h in enumerate(halves):
                 rid, pid, m = X["to"][h]
+                if len(halves) == 1:
+                    m = X["to"][0][2] | X["to"][1][2]
+                part = [ap(T, (r[0], r[1] + 128 * i, r[1] + 128 * i + 128)) for r in srcs + [dst]]
                 tr.append(RemoteDMATransfer(dst_ids=[DstId(rid=rid, pnc=pid)], dma_engine_mask=m, remote_sem=T.sem[sem],
-                                            src=T[src[0]][:, src[1] + 128 * h:src[1] + 128 * h + 128],
-                                            dst=T[dst[0]][:, dst[1] + 128 * h:dst[1] + 128 * h + 128]))
+                                            srcs=part[:-1], dsts=part[-1:], alu_op=alu))
             return g.remote_dma_fused(tr, local_sem=T.sem["sent"])
-        add("g", 300.0, fn, [src], [dst], "r", RL + nbytes / 100.0, sem)
+        add("g", 300.0, fn, srcs, [dst], "r", RL + len(srcs) * nbytes / 100.0, sem)
 
     def sel(buf, r, k=128):
         return (buf, 15 - r, 143 - r, 1, 0, k)
@@ -183,8 +223,8 @@ def build(CYC, PCY, GA, SC, RL):
     def blk(buf, t, n):
         return (buf, t * n, (t + 1) * n)
 
-    def tri(r):
-        return ("TR", 143 * r, 143 * r + 128)
+    def rot(d):
+        return ("R3", 0, 256, 2, d)
 
     tag[0] = "load"
     dma("y", lambda T: T.adi[:], lambda T: T.ad[:], [], [("adi", 0, 16)], 8192)
@@ -206,18 +246,23 @@ def build(CYC, PCY, GA, SC, RL):
     P0, PB0 = ("pc", 0, 1), ("pb", 0, 1)
     ID, NID, ONE = ("Ib", 0, 128), ("nIb", 0, 128), ("one", 0, 128)
     mset(("one", 0, 144), 1.0)
-    mset(("NX", 0, 2048), 0.0)
+    if CFG["zero"] == "V":
+        mset(("NX", 0, 2048), 0.0)
+    else:
+        mset(("NX", 0, 512), 0.0)
+        for m in range(1, 4):
+            dcopy(blk("NX", m, 512), ("NX", 0, 512))
     mset(("Fb", 0, 144), 0.0)
     iota(("pi", 0, 1), [[0, 1]], 0, 1)
     iota(("cf", 0, 16), [[1, 16]], 0, 0)
     asel(("idf", 0, 128), ONE, [[-1, 128]], AL.is_equal, 0, 1)
     asel(("bot", 0, 128), ONE, [[-16, 8], [0, 16]], AL.is_ge, 0, 1)
     asel(("BOb", 0, 128), ("bot", 0, 128), [[16, 8], [0, 16]], AL.is_ge, 15, -1)
-    asel(("Zb", 0, 128), ("BOb", 0, 128), [[-1, 128]], AL.not_equal, 0, 1, -1.0)
+    iota(("Tb", 0, 128), [[1, 128]], 0, -1)
     asel(("Sel", 0, 144, 1, 0, 8), ("one", 0, 144, 1, 0, 8), [[1, 144]], AL.is_equal, -15, -16)
     iota(("irow", 0, 256, 1, 0, 1), [[1, 256]], 0, 0)
     iota(("s16f", 0, 160), [[0, 10], [16, 16]], 0, 0)
-    iota(("csf", 0, 96), [[256, 3], [W0 - A, 2], [16, 16]], A - CEN, 0)
+    iota(("csf", 0, 96), [[256, 3], [A - W0, 2], [16, 16]], W0 - CEN, 0)
     iota(("csf", 96, 128), [[0, 2], [16, 16]], -CEN - 256, 0)
     iota(("csf", 128, 144), [[16, 16]], 0, 0)
     for m in range(8):
@@ -227,24 +272,30 @@ def build(CYC, PCY, GA, SC, RL):
     cp(PB0, ("pi", 4, 5))
     ts(("cst", 0, 144), ("csf", 0, 144), P0, AL.add)
     ts(("s16", 0, 160), ("s16f", 0, 160), P0, AL.add, 16.0, AL.mult)
-    ts(("colb", 0, 16), ("cf", 0, 16), P0, AL.is_equal)
-    ts(("colb", 16, 32), ("cf", 0, 16), P0, AL.is_equal, -1.0, AL.add)
-    ts(("colf", 0, 16), ("cf", 0, 16), P0, AL.is_lt, -BIG, AL.mult)
+    ts(("colf", 0, 16), ("cf", 0, 16), P0, AL.is_equal)
+    ts(("r1", 0, 16), ("cf", 0, 16), P0, AL.add, 16.0, AL.is_lt)
+    tt(("colb", 0, 16), ("r1", 0, 16), ("cf", 0, 16), AL.mult)
+    mset(("cm", 0, 128), -0.0625)
+    if "V" in CFG["clip"]:
+        mset(("cm", 128, 256), 0.0625)
     act(ID, ("idf", 0, 128), AF.Copy)
     act(NID, ("idf", 0, 128), AF.Copy, scale=-1.0)
     act(("I5", 0, 128), ("idf", 0, 128), AF.Copy, scale=512.0)
     for m in range(3):
-        act(blk("In", m, 128), ("idf", 0, 128), AF.Silu, scale=float(n0(2 * m) + OFF), extra=0.0 if m else 1300.0)
+        act(blk("In", m, 128), ("idf", 0, 128), AF.Copy if m else AF.Silu, scale=float(n0(2 * m) + OFF), extra=0.0 if m else 1300.0)
     act(("Fb", 15, 143, 16), ("BOb", 0, 128, 16), AF.Copy)
-    act(("nFb", 0, 144), ("Fb", 0, 144), AF.Copy, scale=-1.0)
+    act(("nFb", 0, 144), ("Fb", 0, 144), AF.Copy, scale=-4 * BIG)
     act(("seatb", 0, 16), ("cst", 128, 144), AF.Copy)
-    for r in range(16):
-        ts(blk("DL", r, 128), ("Zb", 0, 128), ("colb", 16 + r, 17 + r), AL.max, ("colb", r, r + 1), AL.min)
-        act(tri(r), ("idf", 0, 128), AF.Copy, scale=("colf", r, r + 1))
-    iota(("trb", 0, 144), [[0, 144]], -int(BIG), 0)
-    asel(("trb", 144, 288), ("trb", 0, 144), [[0, 16], [-16, 9]], AL.is_ge, 0, 1)
-    asel(("TR", 0, 2304, 16), ("trb", 144, 288), [[1, 16], [16, 9]], AL.is_ge, -1, -1)
-    act(("id16", 0, 128), ("idf", 0, 128), AF.Copy, scale=16.0)
+    for c in (0, 16):
+        act(rot(c), ("idf", 0, 128), AF.Copy)
+    for b, bank in enumerate(SUMS[:2]):
+        mm([((bank, 128 * d, 128 * d + 128), m, x) for d in range(4) for m, x in ((ID, ID), (NID, rot(4 * b + d + 1)))])
+        act(blk("RT", b, 512), (bank, 0, 512), AF.Copy)
+    for d in range(1, 9):
+        ts(blk("LS", d - 1, 128), ("Tb", 0, 128), ("colb", d, d + 1), AL.is_equal, -4 * BIG, AL.mult)
+    for r in range(4):
+        act(blk("Br", r, 128), ("BOb", 0, 128), AF.Copy, scale=("colf", r, r + 1))
+    act(("id16", 0, 128), ("idf", 0, 128), AF.Copy, scale=-16.0)
 
     cp(("au", 0, 16), ("adi", 0, 16))
     cpg(("n16", 256, 512), ("voi", 0, 1024), ("au", 0, 16))
@@ -252,14 +303,16 @@ def build(CYC, PCY, GA, SC, RL):
     ts(("OT", 256, 1280), ("voi", 0, 1024), float(OFF), AL.add)
     ts(("IT", 256, 1280), ("uii", 0, 1024), float(OFF), AL.add)
     ts(("KL", 0, 16), ("adi", 0, 16), -float(CEN), AL.add)
-    act(("z", 0, 256), ("zsb", 0, 256), AF.Copy, scale=0.0625)
-    for bank, col, lo, hi in PARTS:
-        act((bank, 256 + col, 256 + col + hi - lo), ("tgb", lo, hi), AF.Copy)
+    ts(("less", 0, 16), ("adi", 0, 16), -float(CEN), AL.add)
+    act(("w", 0, 128), ("BOb", 0, 128), AF.Copy)
+    act(("z", 0, 256), ("zsb", 0, 256), AF.Copy, scale=-0.0625)
+    if "D" in CFG["ysum"]:
+        act(("ntg", 0, 256), ("tgb", 0, 256), AF.Copy, scale=-1.0)
 
     cp(("cmpb", 160, 240), ("cmpi", 160, 240))
     cp(("cmpb", 0, 160), ("cmpi", 0, 160))
-    mm([(("PG", 256 * k + 80 * r, 256 * k + min(256, 80 * r + 80)), m, ("cmpb", 80 * k, 80 * k + min(80, 256 - 80 * r)))
-        for k in range(2) for r in range(4) for m in (blk("DL", r, 128), ID)])
+    mm([(("PG", 256 * k + 80 * r, 256 * k + min(256, 80 * r + 80)), blk("Br", r, 128), ("cmpb", 80 * k, 80 * k + min(80, 256 - 80 * r)))
+        for k in range(2) for r in range(4)])
     ts(("oh0", 0, 512), ("PG", 0, 512), P0, AL.is_equal)
     for k in range(2):
         dma("y", lambda T, k=k: T.RD[:, 1280 * k:1280 * k + 1280], lambda T, k=k: T.cmpb[:, 80 * k:80 * k + 80],
@@ -286,50 +339,57 @@ def build(CYC, PCY, GA, SC, RL):
     def lists_in(t, parts=(0, 1)):
         s = t - 1
         tag[0] = "list%d" % t
-        p0, p1 = parts[0], parts[-1] + 1
-        mm([(("PK", 16 * p0, 16 * p1), sel("Fb", r), ("XR", 512 * t + 256 * p0 + r, 512 * t + 256 * p1, 16)) for r in range(16)]
-           + [(("PK", 16, 32), NID, ("seatb", 0, 16))] * (p1 - 1))
-        if p0 == 0:
-            ts(blk("au", t, 16), ("PK", 0, 16), float(CEN), AL.add)
-            if t < STEPS:
-                cp(("KL", 32 * t, 32 * t + 16), ("PK", 0, 16))
-        if p1 == 1:
+        c0, c1 = 1 - parts[-1], 2 - parts[0]
+        mm([(("PK", 16 * c0, 16 * c1), sel("Fb", r), ("XR", 512 * t + 256 * c0 + r, 512 * t + 256 * c1, 16)) for r in range(16)]
+           + [(("PK", 0, 16), NID, ("seatb", 0, 16))] * (1 - c0))
+        if c1 == 2:
+            ts(blk("au", t, 16), ("PK", 16, 32), float(CEN), AL.add)
+        if c0 == 1:
+            cp(("KL", 32 * t, 32 * t + 16), ("PK", 16, 32))
             return
         G = blk("Gs", s, 16)
-        act(G, ("PK", 16, 32), AF.Relu, bias=BIG, scale=-4 * BIG)
-        mm([(("PK", 64, 80), ID, ("KL", 32 * s, 32 * s + 16)), (("PK", 64, 80), ID, G)])
-        lst = [(("PK", 80, 112), ID, blk("L16", s, 32)), (("PK", 80, 96), ID, G), (("PK", 96, 112), NID, G)]
+        act(G, ("PK", 0, 16), AF.Relu, bias=BIG, scale=-4 * BIG, same=(0.25, AL.is_lt, 2 * BIG, AL.mult))
+        lst = [(("PK", 32, 64), ID, blk("L16", s, 32)), (("PK", 32, 48), NID, G), (("PK", 48, 64), ID, G),
+               (("PK", 64, 80), ID, ("KL", 32 * s, 32 * s + 16)), (("PK", 64, 80), ID, G)]
         if s >= 2:
-            lst.append((("PK", 96, 112), NID, blk("rs", s, 16)))
+            lst.append((("PK", 32, 48), NID, blk("rs", s, 16)))
         mm(lst)
-        ts(("KL", 32 * t + 16, 32 * t + 32), ("PK", 96, 112), -BIG, AL.max)
-        tt(blk("tmn", s, 32), ("PK", 64, 96), blk("cst", s // 2, 32), AL.min)
+        k = 16 if c1 == 2 and t < STEPS else 32
+        ts(("KL", 32 * t + k - 16, 32 * t + 32), ("PK", k, 48), -BIG, AL.max)
+        tt(blk("tmn", s, 32), ("PK", 48, 80), blk("cst", s // 2, 32), AL.min)
         ts(blk("o12", s, 32), blk("tmn", s, 32), CEN + 0.25, AL.add)
 
     def lowest(t, parts=(0, 1)):
         parts = [h for h in parts if (t < STEPS if h == 0 else t > 0)]
         p0, p1 = parts[0], parts[-1] + 1
         tag[0] = "lowe%d" % t
-        rows = {0: ("XR", 512 * t), 1: ("M", 1024 * ((t - 1) % 2) + 256)}
         k0, k1 = 32 * t + 16 * p0, 32 * t + 16 * p1
-        mm([(("PG", 256 * p0 + r, 256 * p1, 16), blk("DL", r, 128), ("KL", k0, k1)) for r in range(16)], solo=True)
-        act(("eq", 256 * p0, 256 * p1), ("PG", 256 * p0, 256 * p1), AF.Sign, bias=0.5)
-        lst = []
+        wd = k1 - k0
+        x, n = 8 * wd, 16 * wd
+        lst = [(("PG", wd * d, wd * d + wd), blk("RT", d, 128), ("KL", k0, k1)) for d in range(8)]
         if t == 0:
-            lst += [(("PH", r, 128, 16), m, ("KL", 1, 16, 2)) for r in range(16) for m in (blk("DL", r, 128), ID)]
+            for m in range(8):
+                act(blk("more", m, 16), ("colf", 0, 16), AF.Copy, scale=("less", 2 * m + 1, 2 * m + 2))
+            lst += [(("PG", x, n), ("w", 0, 128), ("more", 0, 128))]
         else:
-            for h in parts:
-                for m in range(8):
-                    c = rows[h][1] + 32 * m + 16
-                    lst.append((("PH", 128 * h + 16 * m, 128 * h + 16 * m + 16), ("BOb", 0, 128), (rows[h][0], c, c + 16)))
-        lst += [(("PH", 128 * p0 + r, 128 * p1, 16), NID, ("KL", k0, k1, 2)) for r in range(16)]
+            if p0 == 0:
+                c = 512 * t + 256 + 16
+                lst += [(("PG", x + 16 * m, x + 16 * m + 16), ("BOb", 0, 128), ("XR", c + 32 * m, c + 32 * m + 16)) for m in range(8)]
+            if p1 == 2:
+                c = 1024 * ((t - 1) % 2)
+                lst += [(("PG", n - 128, n), ("BOb", 0, 128), ("M", c, c + 256, 2, 16))]
+        lst += [(("PG", x + r, n, 16), NID, ("KL", k0, k1, 2)) for r in range(16)]
         mm(lst)
-        act(("ab", 128 * p0, 128 * p1), ("PH", 128 * p0, 128 * p1), AF.Abs)
-        act(("eq", 512 + 128 * p0, 512 + 128 * p1), ("ab", 128 * p0, 128 * p1), AF.Relu, bias=4 * BIG, scale=-8 * BIG)
+        v = {"S": n, "M": x, "V": 0}[CFG["equal"][t]]
+        if v:
+            act(("ab", 0, v), ("PG", 0, v), AF.Abs)
+            act(("eq", 0, v), ("ab", 0, v), AF.Relu, bias=4 * BIG, scale=-8 * BIG)
+        if v < n:
+            ts(("eq", v, n), ("PG", v, n), ROUND, AL.add, ROUND, AL.is_equal)
         c0, c1 = 128 + 16 * p0, 128 + 16 * p1
         mm([(("PK", c0, c1), ID, ("KL", k0, k1))]
-           + [(("PK", c0, c1), tri(r), ("eq", 256 * p0 + r, 256 * p1, 16)) for r in range(16)]
-           + [(("PK", c0 + 1, c1, 2), sel("nFb", r), ("eq", 512 + 128 * p0 + r, 512 + 128 * p1, 16)) for r in range(16)])
+           + [(("PK", c0, c1), blk("LS", d, 128), ("eq", wd * d, wd * d + wd)) for d in range(8)]
+           + [(("PK", c0 + 1, c1, 2), sel("nFb", r), ("eq", x + r, n, 16)) for r in range(16)])
         tt(("tmx", k0, k1), ("PK", c0, c1), ("cst", 96 + 16 * p0, 96 + 16 * p1), AL.max)
         ts(("o03", k0, k1), ("tmx", k0, k1), CEN + 256 + (0.1 if t % 2 else 0.35), AL.add)
 
@@ -356,21 +416,31 @@ def build(CYC, PCY, GA, SC, RL):
         mm([(OJ, ID, ohj)])
         act(PC, P, AF.Identity, bias=-float(OFF + CEN))
         tt(("M", m + 512, m + 768), PC, Q, AL.is_lt if t % 2 else AL.is_gt)
-        tt(("M", m, m + 256), PC, ohk, AL.mult)
-        tt(("M", m + 256, m + 512), OJ, Q, AL.mult)
+        tt(("M", m + 256, m + 512), PC, ohk, AL.mult)
+        tt(("M", m, m + 256), OJ, Q, AL.mult)
         tt(("M", m + 768, m + 1024), PC, ohj, AL.mult)
-        mm([(("PL", 0, 64), sel("Fb", r), ("M", m + r, m + 1024, 16)) for r in range(16)] + [(("PL", 32, 48), NID, blk("hl", t, 16))])
+        if t in CFG["votes"]:
+            mm([(("PL", 32, 48), sel("Fb", r), ("M", m + 512 + r, m + 768, 16)) for r in range(16)] + [(("PL", 32, 48), NID, blk("hl", t, 16))])
+            mm([(("PL", 48, 64), sel("Fb", r), ("M", m + 768 + r, m + 1024, 16)) for r in range(16)])
+            mm([(("PL", 0, 32), sel("Fb", r), ("M", m + r, m + 512, 16)) for r in range(16)])
+        else:
+            mm([(("PL", 0, 64), sel("Fb", r), ("M", m + r, m + 1024, 16)) for r in range(16)] + [(("PL", 32, 48), NID, blk("hl", t, 16))])
         act(blk("sg", t, 16), ("PL", 32, 48), AF.Sign, bias=0.5)
         if t >= 2:
-            act(blk("rs", t, 16), ("PL", 48, 64), AF.Relu, bias=-4 * BIG * (n0(t - 2) - CEN - 0.5), scale=4 * BIG)
+            act(blk("rs", t, 16), ("PL", 48, 64), AF.Relu, bias=-4 * BIG * (n0(t - 2) - CEN - 0.5), scale=4 * BIG,
+                same=(n0(t - 2) - CEN - 0.5, AL.is_gt, 2 * BIG, AL.mult))
         cp(blk("L16", t, 32), ("PL", 0, 32))
         mm([(("PL", 64, 80), ("I5", 0, 128), blk("sg", t, 16)), (("PL", 64, 80), ("I5", 0, 128), ("one", 0, 16)),
             (("PL", 64, 80), ID, ("KL", 32 * t, 32 * t + 16))])
-        ts(blk("pj", t, 32), ("PL", 48, 80), CEN + 0.25, AL.add)
+        if t in CFG["votes"]:
+            ts(("pj", 32 * t + 16, 32 * t + 32), ("PL", 64, 80), CEN + 0.25, AL.add)
+            ts(("pj", 32 * t, 32 * t + 16), ("PL", 48, 64), CEN + 0.25, AL.add)
+        else:
+            ts(blk("pj", t, 32), ("PL", 48, 80), CEN + 0.25, AL.add)
         act(blk("xs", t, 256), ("NX", 0, 2048), AF.Copy, off=("pj", 32 * t + 16, 32 * t + 32), more=[("NXp", 0, 2)])
-        send("ax%d" % t, blk("xs", t, 256), ("XR", 512 * (t + 1), 512 * (t + 1) + 256), 65536)
+        send("ax%d" % t, [blk("xs", t, 256)], ("XR", 512 * (t + 1) + 256, 512 * (t + 1) + 512), 65536)
         tag[0] = "fres%d" % t
-        E = ("PH", 256, 512)
+        E = (CFG["fresh"], 256, 512)
         mm([(E, blk("In", t // 2, 128), ohk), (E, ("one", 0, 128, 1, 0, 1), ("irow", 0, 256, 1, 0, 1))])
         tt(blk("nw", t % 2, 256), E, P, AL.max)
 
@@ -379,8 +449,8 @@ def build(CYC, PCY, GA, SC, RL):
         tag[0] = "swit%d" % t
         for m in range(7, -1, -1):
             c = 256 * (t % 2) + 32 * m
-            scatter("v" if m < ONV else "s", (tab, 0, 1280), ("o03", 32 * t + 2 * m, 32 * t + 2 * m + 2), ("nw", c, c + 32))
-        act(("XR", 512 * (t + 1) + 256, 512 * (t + 1) + 512), (tab, 256, 1280), AF.Relu, bias=0.75 - n0(t) - OFF, off=blk("au", t, 16))
+            scatter((tab, 0, 1280), ("o03", 32 * t + 2 * m, 32 * t + 2 * m + 2), ("nw", c, c + 32))
+        act(("XR", 512 * (t + 1), 512 * (t + 1) + 256), (tab, 256, 1280), AF.Relu, bias=0.75 - n0(t) - OFF, off=blk("au", t, 16))
 
     def filled(tab, t):
         return 256 + W0 + B * ((t + 1) // 2 if tab == "U" else t // 2)
@@ -388,81 +458,138 @@ def build(CYC, PCY, GA, SC, RL):
     def early(t):
         tab = "V" if t % 2 == 0 else "U"
         q = 512 * t + 256 * (1 - t % 2)
-        n = 4096 // NS
+        o = 4096 * (t % 3)
         tag[0] = "early%d" % t
-        for c in range(NS - 1, -1, -1):
-            o = 4096 * (t % 3) + n * c
-            act(("py", o, o + n), (tab, 256, filled(tab, t)) if t else ("Vb", 0, W0), AF.Copy, scale=0.0625 if t < STEPS else 1.0,
-                off=("n16", q + c * n // 16, q + (c + 1) * n // 16))
+        for hi, lo in steps_of(CUTS["early", t]):
+            act(("py", o + 16 * lo, o + 16 * hi), (tab, 256, filled(tab, t)) if t else ("Vb", 0, W0), AF.Copy,
+                scale=0.0625 if t < STEPS else -1.0, off=("n16", q + lo, q + hi))
+            ops[-1]["piece"] = ("early", t, hi, lo)
+
+    def steps_of(x):
+        return list(zip(x[:-1], x[1:]))
 
     def late(t):
         tab = "U" if t % 2 == 0 else "V"
-        p = 512 * t + 256 * (t % 2)
-        n = 4096 // NV
-        o, oy = 0, 4096 * (t % 3)
-        todo = list(PARTS)
-        for c in range(NV - 1, -1, -1):
+        win = (tab, 256, filled(tab, t)) if t else ("Ub", 0, W0)
+        p, oy = 512 * t + 256 * (t % 2), 4096 * (t % 3)
+        end = t == STEPS
+        HELP = CFG["help"][t]
+        scan, aid = CFG["scan"] if end else 0, 32 * len(HELP)
+        units = steps_of(CFG["close"] if end else CFG["units"])
+        parts = [(SUMS[i % 3], hi, lo) for i, (hi, lo) in enumerate(units if end else steps_of(CFG["parts"]))]
+        cuts = [x for x in CUTS["late", t] if x > aid] + list(range(aid, -1, -32))
+        if t == 0:
+            win = ("Ub", 0, W0)
+        if aid:
+            tag[0] = "help%d" % t
+            for hi, lo in steps_of(cuts):
+                if hi <= aid:
+                    if lo // 32 in CFG["copy"]:
+                        act((HELP[lo // 32], 0, 512), ("py", oy + 16 * lo, oy + 16 * hi), AF.Copy)
+                    else:
+                        mm([((HELP[lo // 32], 0, 512), ("idf", 0, 128), ("py", oy + 16 * lo, oy + 16 * hi))], True)
+                    act(("prod", 16 * lo, 16 * hi), win, AF.Copy, off=("n16", p + lo, p + hi))
+        for hi, lo in steps_of(cuts):
             tag[0] = "late%d" % t
-            ttg(("prod", o + n * c, o + n * c + n), (tab, 256, filled(tab, t)) if t else ("Ub", 0, W0),
-                ("n16", p + c * n // 16, p + (c + 1) * n // 16), ("py", oy + n * c, oy + n * c + n), AL.mult)
-            if c * n % 1024 == 0:
-                h = c * n // 1024
-                if t == STEPS and h == 0:
-                    add("v", vcost(1024), lambda g, T, X: g.vector.tensor_tensor_scan(
-                        T.py[:, 0:1024], T.seg[:, 0:1024], T.prod[:, 0:1024], 0.0, AL.mult, AL.add),
-                        [("seg", 0, 1024), ("prod", 0, 1024)], [("py", 0, 1024)])
-                    continue
-                bank, col, lo = [x[:3] for x in PARTS if x[2] <= 64 * h < x[3]][0]
-                while todo[0][0] == bank and todo[0][2] > 64 * h:
-                    tail(t, *todo.pop(0))
-                col += 64 * h - lo
+            pr = ("prod", 16 * lo, 16 * hi)
+            if hi <= aid:
+                tt(pr, pr, (HELP[lo // 32], 0, 512), AL.mult)
+            else:
+                ttg(pr, win, ("n16", p + lo, p + hi), ("py", oy + 16 * lo, oy + 16 * hi), AL.mult)
+                ops[-1]["piece"] = ("late", t, hi, lo)
+            while units and units[0][1] >= lo:
+                u1, u0 = units.pop(0)
+                bank, top, base = parts[0]
                 tag[0] = "sums%d" % t
                 for k0 in range(0, 16, 4):
-                    mm([((bank, col, col + 64), ("id16" if t < STEPS else "idf", 0, 128), ("prod", o + 1024 * h + k, o + 1024 * h + 1024, 16))
+                    mm([((bank, u0 - base, u1 - base), ("idf" if end else "id16", 0, 128), ("prod", 16 * u0 + k, 16 * u1, 16))
                         for k in range(k0, k0 + 4)], True, k0 == 0, k0 == 12)
-        for x in todo:
-            tail(t, *x)
+                if u0 == base:
+                    tail(t, (bank, 0, top - base), base, top)
+                    parts.pop(0)
+        for lo in range((scan - 1) // 64 * 64 if scan else -1, -1, -64):
+            a, b = 16 * lo, 16 * min(scan, lo + 64)
+            tag[0] = "scan%d" % t
+            add("v", vcost(b - a), lambda g, T, X, a=a, b=b: g.vector.tensor_tensor_scan(
+                T.py[:, a:b], T.seg[:, 0:b - a], T.prod[:, a:b], 0.0, AL.mult, AL.add),
+                [("seg", 0, 1024), ("prod", a, b)], [("py", a, b)])
+        if scan:
+            tail(t, ("py", 15, 16 * scan, 16), 0, scan)
 
     def side(t):
         X, oy = ("U" if t % 2 == 0 else "V"), 4096 * (t % 3)
         f = filled(X, t)
         tag[0] = "side%d" % t
-        act(blk("cn", t, 256), (X, 256, f + 256), AF.Copy, off=("o12", 32 * t + 16, 32 * t + 32))
+        cn, dq = blk("cn", t, 256), blk("dq", t % 2, 256)
+        act(cn, (X, 256, f + 256), AF.Copy, off=("o12", 32 * t, 32 * t + 16))
         Y = "V" if t % 2 == 0 else "U"
-        send("ac%d" % t, blk("cn", t, 256), (Y, filled(Y, t), filled(Y, t) + 256) if t < STEPS - 1 else ("fcl", 0, 256), 131072)
+        send("ac%d" % t, [cn], (Y, filled(Y, t), filled(Y, t) + 256) if t < STEPS - 1 else ("fcl", 0, 256), 131072)
         act(blk("yj", t % 2, 256), ("py", oy, oy + 4096), AF.Copy, scale=16.0, off=blk("kj", 5 + t, 16))
-        act(CB, (X, f, f + 256), AF.Copy)
-        act(("dd", 0, 256), ("py", oy, oy + 4096), AF.Copy, off=blk("kj", t, 16))
-        tt(CB, blk("cn", t, 256), CB, AL.subtract)
-        tt(("more", 0, 256), CB, ("dd", 0, 256), AL.mult)
-        tts(("BT", 0, 1792), ("o12", 32 * t, 32 * t + 16), blk("bg", t % 3, 256), ("more", 0, 256), AL.add)
-        for h in (1, 0):
-            tag[0] = "w%d%d" % (t, h)
-            ttg(blk("w", h, 128), (X, 256, f), ("pj", 32 * t + 8 * h, 32 * t + 8 * h + 8), blk("z", 2 * t + h, 128), AL.mult)
+        if CFG["spare"][t] == "1":
+            act(dq, (X, f, f + 256), AF.Copy, scale=-1.0)
+            dadd(dq, cn)
+        else:
+            act(CB, (X, f, f + 256), AF.Copy)
+            tt(dq, cn, CB, AL.subtract)
+        ttg(("more", 0, 256), ("py", oy, oy + 4096), blk("kj", t, 16), dq, AL.mult)
+        tts(("BT", 0, 1792), ("o12", 32 * t + 16, 32 * t + 32), blk("bg", t % 3, 256), ("more", 0, 256), AL.add)
+        for hi, lo in steps_of(CFG["w"][t]):
+            tag[0] = "w%d%d" % (t, lo)
+            ttg(("w", lo, hi), (X, 256, f), ("pj", 32 * t + lo // 16, 32 * t + hi // 16), ("z", 256 * t + lo, 256 * t + hi), AL.mult)
 
-    def tail(t, bank, col, lo, hi):
+    def base(t):
+        tag[0] = "bg%d" % t
+        bg, to = blk("bg", t % 3, 256), (BT0[0], BT0[1], BT0[1] + 256)
+        act(bg, ("BT", 0, 1024), AF.Copy, off=blk("au", t, 16))
+        if t == STEPS:
+            return
+        if CFG["ysum"][t] == "D":
+            bt = blk("bgt", t % 2, 256)
+            dcopy(bt, ("ntg", 0, 256))
+            dadd(bt, bg)
+            dcopy(blk("y", t, 256), bg)
+            act(to, bt, AF.Copy)
+        elif CFG["ysum"][t] == "T":
+            mm([(to, ("idf", 0, 128), bg), (to, NID, ("tgb", 0, 256))])
+            dcopy(blk("y", t, 256), bg)
+        elif t == 0 or CFG["ysum"][t - 1] != "B":
+            act(to, ("tgb", 0, 256), AF.Copy)
+
+    def tail(t, S0, lo, hi):
         Y = "V" if t % 2 == 0 else "U"
         k, j, b, bb = 32 * (t + 1) + 16, 256 * (t % 2), 256 * t, 256 * (t % 3)
         tag[0] = "tail%d%d" % (t, lo)
-        S, y = (bank, col, col + hi - lo), ("y", b + lo, b + hi)
-        tt(S, ("py", 15, 1024, 16) if t == STEPS and lo == 0 else S, ("z", b + lo, b + hi), AL.mult)
-        tt(y, S, ("bg", bb + lo, bb + hi), AL.add)
-        if t == STEPS:
-            dma("y", lambda T: T.ys[:, y[1]:y[2]], lambda T: ap(T, y), [y], [], 32768, "o")
-            return
-        tt(S, y, (bank, 256 + col, 256 + col + hi - lo), AL.subtract)
+        S, y = S0 if psum(S0) else ("PG", 0, hi - lo), ("y", b + lo, b + hi)
+        z, to = ("z", b + lo, b + hi), (BT0[0], BT0[1] + lo, BT0[1] + hi)
+        if t < STEPS and CFG["ysum"][t] != "B":
+            sz = ("sz", j + lo, j + hi)
+            tt(sz, S, z, AL.mult)
+            tt(S, sz, to, AL.add)
+        else:
+            tt(S, S0, z, AL.mult)
+            tt(y, S, ("bg", bb + lo, bb + hi), AL.add)
+            if t == STEPS:
+                dma("y", lambda T: T.ys[:, y[1]:y[2]], lambda T: ap(T, y), [y], [], 32768, "o")
+                return
+            tt(S, y, to, AL.subtract)
         tt(("less", lo, hi), S, ("w", lo, hi), AL.mult)
         for m in range(hi // 32 - 1, lo // 32 - 1, -1):
             tts((Y, 0, filled(Y, t)), ("o03", k + 2 * m, k + 2 * m + 2), ("yj", j + 32 * m, j + 32 * m + 32),
-                ("less", 32 * m, 32 * m + 32), AL.subtract)
+                ("less", 32 * m, 32 * m + 32), AL.add)
         if lo % 128:
             return
         h = lo // 128
         tag[0] = "clip%d%d" % (t, h)
-        act(blk("r1", h, 128), blk("y", 2 * t + h, 128), AF.Relu, bias=1.0)
-        act(blk("r2", h, 128), blk("r1", h, 128), AF.Relu, bias=2.0, scale=-1.0)
-        act(blk("zo", 2 * t + h, 128), blk("r2", h, 128), AF.Identity, bias=0.0625, scale=-0.0625)
-        send("az%d%d" % (t, h), blk("zo", 2 * t + h, 128), blk("z", 2 * t + 2 + h, 128), 65536, (h,))
+        y, zo = blk("y", 2 * t + h, 128), blk("zo", 2 * t + h, 128)
+        if CFG["ysum"][t] != "B":
+            dadd(y, blk("sz", 2 * (t % 2) + h, 128))
+        if CFG["clip"][t] == "S":
+            act(blk("r1", h, 128), y, AF.Relu, bias=1.0)
+            act(zo, blk("r1", h, 128), AF.Relu, bias=0.125, scale=-0.0625)
+            send("az%d%d" % (t, h), [zo, ("cm", 0, 128)], blk("z", 2 * t + 2 + h, 128), 65536, (h,), 1)
+        else:
+            ts(zo, y, 1.0, AL.min, -0.0625, AL.mult)
+            send("az%d%d" % (t, h), [zo, ("cm", 128, 256)], blk("z", 2 * t + 2 + h, 128), 65536, (h,), 3)
         if h == 0:
             dma("y", lambda T: T.ys[:, b:b + 256], lambda T: T.y[:, b:b + 256], [blk("y", t, 256)], [], 131072, "o")
 
@@ -471,8 +598,7 @@ def build(CYC, PCY, GA, SC, RL):
     lowest(0)
     switch(0)
     for t in range(STEPS + 1):
-        tag[0] = "bg%d" % t
-        act(blk("bg", t % 3, 256), ("BT", 0, 1024), AF.Copy, off=blk("au", t, 16))
+        base(t)
         if t < STEPS:
             if t < APART:
                 lists_in(t + 1, (1,))
@@ -492,7 +618,25 @@ def build(CYC, PCY, GA, SC, RL):
 
 
 def schedule():
-    others = [(build(*c[:5]), c[5]) for c in COSTS]
+    for t in range(STEPS + 1):
+        CUTS["early", t] = list(range(256, -1, -CFG["early"]))
+        CUTS["late", t] = list(CFG["late" if t < STEPS else "last"])
+    places = None
+    for k, sweeps in enumerate(SWEEPS):
+        ops, s = arrange(places, sweeps, k)
+        if k + 1 < len(SWEEPS):
+            places = {mark(ops[j]): (float(x), "alt" in ops[j] and ops[j]["eng"] == "v") for x, j in enumerate(s["order"])}
+            for kind, t, x in s["join"]:
+                CUTS[kind, t].remove(x)
+    return ops, s
+
+
+def mark(o):
+    return ("piece",) + o["piece"][:2] + o["piece"][3:] if "piece" in o else (o["tag"], o["kind"], tuple(o["rd"]), tuple(o["wr"]))
+
+
+def arrange(places, sweeps, phase):
+    others = [(build(*c[:-1]), c[-1]) for c in COSTS]
     ops = others[0][0]
     n = len(ops)
     deps = [dict() for _ in range(n)]
@@ -535,7 +679,16 @@ def schedule():
     cost, tail, pred = sets[0][:3]
     back = backs[0]
     ends = [j for j in range(n) if not back[j]]
-    norm = [max(sum(c for c, e in zip(s[0], ei) if e == x) for x in range(5)) for s in sets]
+    link = [j - 1 if phase + 1 < len(SWEEPS) and o.get("piece", "a")[0] == "early" and o["piece"][2] < 256 else -2 for j, o in enumerate(ops)]
+    norm = [max(sum(c for c, e in zip(s[0], ei) if e == x) for x in range(5)) / w for s, w in zip(sets, WEIGHTS)]
+    onv, spare = set(), [[o["alt"][0] if "alt" in o else 0.0 for o in oo] for oo, lat in others]
+
+    def flip(js):
+        for j in js:
+            ei[j] = 1 - ei[j]
+            for s, x in zip(sets, spare):
+                s[0][j], x[j] = x[j], s[0][j]
+        onv.symmetric_difference_update(js)
 
     def run(seq, k0, old):
         lq, lb = [-1] * 5, [-1] * 8
@@ -549,7 +702,7 @@ def schedule():
             for j in rest:
                 e = ei[j]
                 w = q[e]
-                t = en[w]
+                t = en[w] - JOIN if w == link[j] else en[w]
                 for i, d in pr[j]:
                     x = en[i] + d
                     if x > t:
@@ -617,32 +770,45 @@ def schedule():
         prio[i] = cost[i] + max([prio[j] + d for j, d in back[i]] + [tail[i]])
     whole = [o["tag"][:4] in ("fres", "list", "lowe", "name", "swit") for o in ops]
 
+    def planned(lead):
+        key = [1e9] * n
+        for j, o in enumerate(ops):
+            k = o["tag"][:4]
+            if k in PLAN:
+                t = int([x for x in o["tag"] if x.isdigit()][0])
+                key[j] = FIRST + STEP * t + PLAN[k] + 1e-3 * j - (lead[t] if whole[j] else 0.0)
+        for i in range(n - 1, -1, -1):
+            key[i] = min([key[i]] + [key[j] - d - cost[i] for j, d in back[i]])
+        return key
+
     def ahead(b):
         key = [-p - (b if w else 0.0) for p, w in zip(prio, whole)]
         for i in range(n - 1, -1, -1):
             key[i] = min([key[i]] + [key[j] - d - cost[i] for j, d in back[i]])
         return key
 
-    best = min((improve(ahead(b), k, s) for b in (0.0, 5e3, 1e4, 2e4) for k in (0, 1, 3) for s in (0, 1)), key=lambda x: x[0])
     tags = sorted(set(o["tag"] for o in ops))
     kind = ["".join(x for x in o["tag"] if not x.isdigit()) for o in ops]
     kinds = sorted(set(kind))
-    cur, rnd = best, [SEED]
+    rnd = [SEED]
 
     def draw():
         rnd[0] = (rnd[0] * 1103515245 + 12345) % 2147483648
         return rnd[0] / 2147483648.0
 
-    for it in range(ROUNDS):
-        amp = (30.0, 100.0, 400.0)[it % 3]
-        mv = {tags[int(draw() * len(tags))]: (draw() - 0.5) * 8000.0 for _ in range(int(draw() * 3))}
-        mk = {kinds[int(draw() * len(kinds))]: (draw() - 0.5) * 6000.0 for _ in range(int(draw() * 1.5))}
-        new = improve([cur[2][j] + amp * draw() + mv.get(ops[j]["tag"], 0.0) + mk.get(kind[j], 0.0) for j in range(n)],
-                      it % 2, int(draw() * len(sets)))
-        if new[0] < cur[0] + 0.004 * draw():
-            cur = new
-        if new[0] < best[0]:
-            best = new
+    def rounds(key):
+        cur = best = min((improve(key, k, s) for k in (0, 1, 3) for s in range(len(sets))), key=lambda x: x[0])
+        for it in range(ROUNDS):
+            amp = (30.0, 100.0, 400.0)[it % 3]
+            mv = {tags[int(draw() * len(tags))]: (draw() - 0.5) * 8000.0 for _ in range(int(draw() * 3))}
+            mk = {kinds[int(draw() * len(kinds))]: (draw() - 0.5) * 6000.0 for _ in range(int(draw() * 1.5))}
+            new = improve([cur[2][j] + amp * draw() + mv.get(ops[j]["tag"], 0.0) + mk.get(kind[j], 0.0) for j in range(n)],
+                          it % 2, int(draw() * len(sets)))
+            if new[0] < cur[0] + 0.004 * draw():
+                cur = new
+            if new[0] < best[0]:
+                best = new
+        return best[1]
 
     def shift(seq, a, b, up):
         mid = seq[a:b + 1]
@@ -653,41 +819,159 @@ def schedule():
         go = [x == i or anc[x] >> i & 1 for x in mid]
         return seq[:a] + [x for x, f in zip(mid, go) if not f] + [x for x, f in zip(mid, go) if f] + seq[b + 1:]
 
-    seq = best[1]
-    val, st = run(seq, 0, blank)
-    top = (val, seq, st)
-    arcs = None
-    for it in range(MOVES):
-        if draw() < ONPATH:
-            if arcs is None:
-                arcs, pos = [], [0] * n
-                for k, j in enumerate(seq):
-                    pos[j] = k
-                for (en, why), s in zip(st, sets):
-                    j = max(ends, key=lambda j: en[j] + s[1][j])
-                    while why[j] >= 0:
+    def sweep(seq, W, moves, heat):
+        seq = list(seq)
+        starts = list(range(-int(draw() * W / 2), n - W // 2, W // 2))
+        stops = {min(n, a + W): None for a in starts}
+        qs = [[0.0] * (n + 1) for _ in sets]
+        nq, nb = [-1] * 5, [-1] * 8
+        for k in range(n, 0, -1):
+            if k in stops:
+                stops[k] = (list(nq), list(nb))
+            j = seq[k - 1]
+            e = ei[j]
+            for (c, tl, pr, lat), bk, q in zip(sets, backs, qs):
+                x = max(tl[j], q[nq[e]])
+                for i, d in bk[j]:
+                    if d + q[i] > x:
+                        x = d + q[i]
+                for b in banks[j]:
+                    if ei[nb[b]] != e and lat + q[nb[b]] > x:
+                        x = lat + q[nb[b]]
+                q[j] = x + c[j]
+            nq[e] = j
+            for b in banks[j]:
+                nb[b] = j
+        ens, whys = [[0.0] * (n + 1) for _ in sets], [[-1] * (n + 1) for _ in sets]
+        lq, lb = [-1] * 5, [-1] * 8
+        for a0 in starts:
+            a0, b0 = max(0, a0), min(n, a0 + W)
+            win = seq[a0:b0]
+            inside = set(win)
+            nq, nb = stops[b0]
+            outs = [{j: max([s[1][j]] + [d + q[i] for i, d in bk[j] if i not in inside]) for j in win} for s, bk, q in zip(sets, backs, qs)]
+
+            def value(win):
+                tot, tips = 0.0, []
+                for (c, tl, pr, lat), en, why, out, qq, nm in zip(sets, ens, whys, outs, qs, norm):
+                    q, bk, top, tip, sm = list(lq), list(lb), 0.0, -1, 0.0
+                    for j in win:
+                        e = ei[j]
+                        w = q[e]
+                        t = en[w] - JOIN if w == link[j] else en[w]
+                        for i, d in pr[j]:
+                            x = en[i] + d
+                            if x > t:
+                                t, w = x, i
+                        for b in banks[j]:
+                            i = bk[b]
+                            if ei[i] != e and en[i] + lat > t:
+                                t, w = en[i] + lat, i
+                            bk[b] = j
+                        t += c[j]
+                        en[j], why[j], q[e] = t, w, j
+                        sm += t
+                        t += out[j]
+                        if t > top:
+                            top, tip = t, j
+                    sq = 0.0
+                    for e in range(4):
+                        t = en[q[e]] + qq[nq[e]]
+                        sq += t
+                        if t > top:
+                            top, tip = t, q[e]
+                    for b in range(8):
+                        if ei[bk[b]] != ei[nb[b]] and en[bk[b]] + lat + qq[nb[b]] > top:
+                            top, tip = en[bk[b]] + lat + qq[nb[b]], bk[b]
+                    tot += (top + EVEN * sq / 4 + SOON * sm / len(win)) / nm
+                    tips.append(tip)
+                return tot, tips
+
+            def path(win, tips):
+                pos = {j: k for k, j in enumerate(win)}
+                arcs = []
+                for why, j in zip(whys, tips):
+                    while j in pos and why[j] in pos:
                         if not anc[j] >> why[j] & 1:
-                            arcs.append((why[j], j))
+                            arcs.append((pos[why[j]], pos[j]))
                         j = why[j]
-            i, j = arcs[int(draw() * len(arcs))]
-            a, b, up = pos[i], pos[j], draw() < 0.5
-            far = int(draw() * draw() * 40)
-            if up:
-                a = max(0, a - far)
-            else:
-                b = min(n - 1, b + far)
-        else:
-            a = int(draw() * (n - 1))
-            b, up = min(n - 1, a + 1 + int(draw() * draw() * 40)), draw() < 0.5
-        new = shift(seq, a, b, up)
-        if new == seq:
-            continue
-        v2, s2 = run(new, a, st)
-        if v2 <= val + HEAT * (1.0 - it / MOVES) ** 2 * draw():
-            seq, val, st, arcs = new, v2, s2, None
-            if val < top[0]:
-                top = (val, seq, st)
+                return arcs
+
+            val, tips = value(win)
+            arcs, keep, m = path(win, tips), (val, win, set(onv)), len(win)
+            free = [j for j in win if "alt" in ops[j]]
+            for it in range(moves):
+                up = draw() < 0.5
+                if free and draw() < SWAP:
+                    j = free[int(draw() * len(free))]
+                    flip({j})
+                    v2, tips = value(win)
+                    if v2 <= val + heat * (1.0 - it / moves) * draw():
+                        val, arcs = v2, path(win, tips)
+                        if val < keep[0]:
+                            keep = (val, win, set(onv))
+                    else:
+                        flip({j})
+                    continue
+                if arcs and draw() < ONPATH:
+                    a, b = arcs[int(draw() * len(arcs))]
+                    far = int(draw() * draw() * 30)
+                    a, b = (max(0, a - far), b) if up else (a, min(m - 1, b + far))
+                else:
+                    a = int(draw() * (m - 1))
+                    b = min(m - 1, a + 1 + int(draw() * draw() * 40))
+                new = shift(win, a, b, up)
+                if new == win:
+                    continue
+                v2, tips = value(new)
+                if v2 <= val + heat * (1.0 - it / moves) * draw():
+                    win, val, arcs = new, v2, path(new, tips)
+                    if val < keep[0]:
+                        keep = (val, win, set(onv))
+            win = keep[1]
+            flip(onv ^ keep[2])
+            value(win)
+            seq[a0:b0] = win
+            for j in seq[a0:max(0, a0 + (b0 - a0 if b0 == n else W // 2 - (W - (b0 - a0))))]:
+                lq[ei[j]] = j
+                for b in banks[j]:
+                    lb[b] = j
+        return seq
+
+    if places:
+        flip({j for j, o in enumerate(ops) if places[mark(o)][1]})
+        seq = topo_by([places[mark(o)][0] for o in ops])
+    else:
+        tries = []
+        for key in [ahead(b) for b in AHEAD] + [planned(x) for x in LEADS]:
+            flip(set(onv))
+            seq = rounds(key)
+            for W in WINDOWS[:3]:
+                seq = sweep(seq, W, MOVES // 2, HEAT)
+            tries.append((run(seq, 0, blank)[0], seq, set(onv)))
+        seq, x = min(tries)[1:]
+        flip(onv ^ x)
+        TRIES.append(sorted(x[0] for x in tries))
+    val, st = run(seq, 0, blank)
+    top = (val, seq, st, set(onv))
+    for it in range(sweeps):
+        seq = sweep(seq, WINDOWS[it % len(WINDOWS)], MOVES, HEAT * (1.0 - it / sweeps) / (1 + phase))
+        val, st = run(seq, 0, blank)
+        if val < top[0]:
+            top = (val, seq, st, set(onv))
     order, st = top[1], top[2]
+    flip(onv ^ top[3])
+    for j in onv:
+        ops[j]["eng"], ops[j]["cost"], ops[j]["fn"] = "v", ops[j]["alt"][0], ops[j]["alt"][1]
+    join, prev = [], [-1] * 5
+    for j in order:
+        i = prev[ei[j]]
+        a, b = ops[i].get("piece", "a"), ops[j].get("piece", "b")
+        if a[:2] == b[:2] and a[3] == b[2]:
+            if all(en[k] - s[0][k] - d >= en[j] - JOIN for (en, why), s, bk in zip(st, sets, backs) for k, d in bk[i]):
+                join.append(a[:2] + a[3:])
+                j = -1 if phase % 2 else j
+        prev[ei[j if j >= 0 else i]] = j
     start = [st[0][0][j] - cost[j] for j in range(n)]
     done = [st[0][0][j] + tail[j] for j in range(n)]
     last = [-1] * 8
@@ -725,7 +1009,8 @@ def schedule():
         clock[j] = {} if o["kind"] == "r" else dict(known[e])
         clock[j][token[j][0]] = token[j][1]
     spans = [max(en[j] + s[1][j] for j in ends) for (en, why), s in zip(st, sets)]
-    return ops, {"spans": spans, "order": order, "waits": waits, "token": token, "count": count, "start": start, "done": done}
+    return ops, {"spans": spans, "order": order, "waits": waits, "token": token, "count": count, "start": start, "done": done,
+                 "join": join, "st": st}
 
 
 _PLAN = {}

from concourse.bass import DstId, RemoteDMATransfer
from concourse.mybir import AluOpType, ActivationFunctionType

AL = AluOpType
AF = ActivationFunctionType
A, W0, B, STEPS = 1024, 1792, 256, 5
OFF = 256
CEN = 1280
BIG = 4096.0
ROUND = 1.5 * 2.0 ** 23
NS, NV = 4, 4
APART = 1
ONV = 0
CFG = {
    "ysum": "DDDDB",
    "clip": "VSSSS",
    "spare": "11111",
    "equal": "VVMMMM",
    "scan": 96, "help": [[]] * 5 + [["PC", "PG", "PL", "PK"]],
    "copy": [], "votes": [], "fresh": "PL", "zero": "D", "w": [[256, 0]] + [[256, 128, 0]] * 4,
    "early": 32, "late": [256, 192, 128, 64, 0], "last": [256, 176, 96, 0],
    "parts": [256, 128, 64, 0], "units": [256, 192, 128, 64, 0], "close": [256, 176, 96],
}

F32, BF, F16, U16, I32 = "float32", "bfloat16", "float16", "uint16", "int32"
_S = {
    "U": (2816, F32), "V": (2816, F32), "IT": (1280, F32), "OT": (1280, F32), "BT": (1792, F32),
    "Ub": (W0, BF), "Vb": (W0, BF), "uii": (1024, I32), "voi": (1024, I32), "adi": (16, I32),
    "cmpi": (240, I32), "cmpb": (240, BF), "nxi": (128, I32), "nxh": (256, I32), "nxc": (256, BF),
    "NX": (2048, BF), "R1": (3840, BF), "RR": (2560, BF), "zsb": (256, BF), "tgb": (256, BF),
    "py": (3 * 4096, F32), "prod": (4096, F32),
    "oh": (2560, BF), "oh0": (512, BF), "id16": (128, F32), "nw": (512, F32), "kj": (160, U16), "hl": (80, BF),
    "nm": (6 * 512, F32), "n16": (6 * 512, U16), "M": (2 * 1024, F16),
    "XR": (6 * 512, BF), "xs": (5 * 256, BF), "au": (6 * 16, U16), "KL": (6 * 32, F16), "L16": (5 * 32, F16),
    "pj": (5 * 32, U16), "sg": (5 * 16, BF), "rs": (5 * 16, BF), "Gs": (5 * 16, BF),
    "tmn": (5 * 32, F32), "o12": (5 * 32, U16), "tmx": (6 * 32, F32), "o03": (6 * 32, U16),
    "ab": (512, BF), "eq": (512, BF), "dq": (2 * 256, F32), "bgt": (2 * 256, F32), "ntg": (256, F32), "sz": (2 * 256, F32),
    "cm": (256, F32),
    "seg": (1024, BF), "bg": (3 * 256, F32), "yj": (2 * 256, F32), "cn": (5 * 256, F32), "more": (256, F32),
    "w": (256, F32), "less": (256, F32), "y": (6 * 256, F32), "r1": (256, F32),
    "zo": (5 * 256, F32), "z": (6 * 256, F32), "fcl": (256, F32),
    "pi": (8, I32), "pc": (8, F32), "pb": (8, BF), "one": (144, BF), "idf": (128, F32), "bot": (128, BF), "Tb": (128, BF),
    "Ib": (128, BF), "nIb": (128, BF), "I5": (128, BF), "In": (384, BF), "BOb": (128, BF), "Fb": (144, BF), "nFb": (144, BF),
    "Sel": (144, BF), "irow": (256, BF), "cf": (16, F32), "csf": (144, F32), "cs": (144, F32), "seatb": (16, BF),
    "s16f": (160, F32), "s16": (160, BF), "colb": (16, BF), "colf": (16, F32), "RT": (1024, BF), "LS": (1024, BF),
    "R3": (256, BF), "Br": (512, BF),
}
_D3 = ("M", "R3")
_S["cst"] = _S.pop("cs")
_P = ["PA", "PB", "PC", "PG", "PH", "PL", "PK", "PE"]
SCRATCH = {k: ("sbuf", [128, v[0] // 32, 32] if k in _D3 else [128, v[0]], v[1]) for k, v in _S.items()}
for _b in _P:
    SCRATCH[_b] = ("psum", [128, 512], F32)
SCRATCH["RD"] = ("dram", [8, 2560], BF)
NDMA = 72
SEMAPHORES = (["qv", "qs", "qp", "qg", "sent", "outs", "rd", "rr"] + ["d%d" % i for i in range(NDMA)]
              + ["a%s%d" % (k, t) for k in "xc" for t in range(STEPS)] + ["az%d%d" % (t, h) for t in range(STEPS) for h in range(2)])

COSTS = [(0.85, 0.43, 1.56, 3.8, 3000.0, 700.0, 2000.0, 150.0), (0.95, 0.48, 1.15, 2.2, 4000.0, 1000.0, 2500.0, 200.0),
         (1.15, 0.58, 1.9, 5.2, 3000.0, 700.0, 2000.0, 120.0), (1.1, 0.56, 1.5, 3.5, 5500.0, 1000.0, 2800.0, 250.0)]
ROUNDS, SWEEPS, MOVES, SEED, SOON, EVEN, ONPATH, HEAT = 200, (20, 5, 3), 250, 1, 0.02, 0.3, 0.6, 0.004
JOIN, SWAP, WEIGHTS = 60.0, 0.1, (1.0, 1.0, 1.0, 1.0)
WINDOWS = (60, 100, 40, 140)
FIRST, STEP = 5700.0, 12300.0
PLAN = {"late": 0.0, "sums": 1400.0, "tail": 6000.0, "earl": -3000.0, "clip": 9000.0, "side": 3000.0, "help": 0.0, "scan": 5000.0,
        "list": -6000.0, "name": -5000.0, "lowe": -4000.0, "fres": -3500.0, "swit": -2000.0}
LEADS = []
AHEAD = (5e3, 1e4)
TRIES = []
SUMS = ["PA", "PE", "PB"]
CB = ("PL", 256, 512)
BT0 = ("PH", 0)


CUTS = {}


def n0(t):
    return W0 + B * (t // 2)


def build(CYC, PCY, GA, SC, RL, GD, DL):
    ops = []
    tag = ["0"]

    def ap(T, r):
        if r[0] in _D3:
            x = slice(r[4], r[4] + 16) if len(r) == 5 else slice(r[1] % 32, 32, r[3] if len(r) == 4 else 1)
            return T[r[0]][:, r[1] // 32:r[2] // 32, x]
        if len(r) == 3:
            return T[r[0]][:, r[1]:r[2]]
        if len(r) == 4:
            return T[r[0]][:, r[1]:r[2]:r[3]]
        return T[r[0]][r[4]:r[5], r[1]:r[2]:r[3]]

    def add(eng, cost, fn, rd, wr, kind="c", lat=0.0, name=""):
        ops.append({"eng": eng, "cost": cost, "fn": fn, "rd": [r[:3] for r in rd], "wr": [r[:3] for r in wr], "kind": kind,
                    "lat": lat, "name": name, "tag": tag[0]})

    def width(r):
        return (r[2] - r[1] + (r[3] if len(r) > 3 else 1) - 1) // (r[3] if len(r) > 3 else 1)

    def vcost(n, k=1.0):
        return 30.0 + max(64.0, n * k) * CYC

    def psum(r):
        return r[0] in _P

    def short(*rs):
        return 0.5 if all(r[0] in _S and _S[r[0]][1] in (BF, F16, U16) for r in rs) else 1.0

    def tt(out, a, b, op):
        k = 1.0 if psum(a) or psum(b) else 2.0
        add("v", vcost(width(out), k), lambda g, T, X: g.vector.tensor_tensor(ap(T, out), ap(T, a), ap(T, b), op), [a, b], [out])

    def ttg(out, win, off, b, op):
        add("v", 50 + width(out) * GA * CYC,
            lambda g, T, X: g.vector.tensor_tensor(ap(T, out), ap(T, win).indirect(ap(T, off)), ap(T, b), op), [win, off, b], [out])

    def tts(win, off, a, b, op):
        add("v", 50 + width(a) * SC * CYC,
            lambda g, T, X: g.vector.tensor_tensor(ap(T, win).indirect(ap(T, off)), ap(T, a), ap(T, b), op), [off, a, b], [win])

    def scatter(win, off, a):
        add("s", 65 + width(a) * SC * CYC,
            lambda g, T, X: g.scalar.activation(ap(T, win).indirect(ap(T, off)), ap(T, a), AF.Silu), [off, a], [win])
        ops[-1]["alt"] = (50 + width(a) * SC * CYC, lambda g, T, X: g.vector.tensor_copy(ap(T, win).indirect(ap(T, off)), ap(T, a)))

    def ts(out, a, s1, op0, s2=None, op1=None, more=()):
        rd = [a] + [s for s in (s1, s2) if isinstance(s, tuple)]

        def fn(g, T, X):
            x1 = ap(T, s1) if isinstance(s1, tuple) else s1
            x2 = ap(T, s2) if isinstance(s2, tuple) else s2
            if op1 is None:
                return g.vector.tensor_scalar(ap(T, out), ap(T, a), x1, None, op0)
            return g.vector.tensor_scalar(ap(T, out), ap(T, a), x1, x2, op0, op1)
        add("v", vcost(width(out), short(out, *rd)), fn, rd + list(more), [out])

    def cp(out, a):
        add("v", vcost(width(out), short(out, a)), lambda g, T, X: g.vector.tensor_copy(ap(T, out), ap(T, a)), [a], [out])

    def cpg(out, win, off):
        add("v", 50 + width(out) * GA * CYC,
            lambda g, T, X: g.vector.tensor_copy(ap(T, out), ap(T, win).indirect(ap(T, off))), [win, off], [out])

    def mset(out, v):
        add("v", vcost(width(out), short(out)), lambda g, T, X: g.vector.memset(ap(T, out), v), [], [out])

    def act(out, a, f, bias=0.0, scale=1.0, off=None, more=(), extra=0.0, same=None):
        rd = [a] + ([off] if off else []) + [x for x in (bias, scale) if isinstance(x, tuple)] + list(more)

        def fn(g, T, X):
            x = ap(T, a).indirect(ap(T, off)) if off else ap(T, a)
            bb = ap(T, bias) if isinstance(bias, tuple) else bias
            ss = ap(T, scale) if isinstance(scale, tuple) else scale
            return g.scalar.activation(ap(T, out), x, f, bias=bb, scale=ss)
        add("s", extra + (65 + width(out) * GA * CYC if off else vcost(width(out))), fn, rd, [out])
        if f in (AF.Copy, AF.Identity):
            same = (scale, AL.mult, bias, AL.add)
        elif f == AF.Relu and scale == 1.0:
            same = (bias, AL.add, 0.0, AL.max)
        if same:

            def other(g, T, X):
                x = ap(T, a).indirect(ap(T, off)) if off else ap(T, a)
                s1, s2 = [ap(T, s) if isinstance(s, tuple) else s for s in same[::2]]
                return g.vector.tensor_scalar(ap(T, out), x, s1, s2, same[1], same[3])
            ops[-1]["alt"] = (50 + width(out) * GA * CYC if off else vcost(width(out), short(out, *rd)), other)

    def mm(lst, f32=False, first=True, last=True, solo=False):
        cost = sum(max(64, width(m[2])) * (4 if _S[m[2][0]][1] == F32 else 1) for m in lst) * PCY + (40 if last else 0)

        def fn(g, T, X):
            ins = None
            for i, m in enumerate(lst):
                ins = g.tensor.matmul(ap(T, m[0]), ap(T, m[1]), ap(T, m[2]), solo or (first and i == 0),
                                      solo or (last and i == len(lst) - 1))
            return ins
        add("p", cost, fn, [m[1] for m in lst] + [m[2] for m in lst], [m[0] for m in lst])

    def dma(q, fo, fi, rd, wr, nbytes, kind="d", name=""):
        def fn(g, T, X):
            return {"g": g, "y": g.sync, "s": g.scalar}[q].dma_start(fo(T), fi(T))
        add(q, GD if q == "g" else 100.0, fn, rd, wr, kind, DL + nbytes / 600.0, name)

    def dcopy(out, a):
        dma("y", lambda T: ap(T, out), lambda T: ap(T, a), [a], [out], 512 * width(out))

    def dadd(out, a):
        add("g", GD, lambda g, T, X: g.dma_start(ap(T, out), ap(T, a), accum_op=AL.add), [a, out], [out], "d",
            DL + 300.0 + 2 * 512 * width(out) / 600.0)

    def iota(out, pat, base, cm):
        fl = _S[out[0]][1] != I32

        def fn(g, T, X):
            if fl:
                return g.iota(ap(T, out), pat, base, cm, allow_small_or_imprecise_dtypes=True)
            return g.iota(ap(T, out), pat, base, cm)
        add("g", 130 + 2 * width(out) * CYC, fn, [], [out])

    def asel(out, a, pat, op, base, cm, fill=0.0):
        add("g", 170 + 2 * width(out) * CYC,
            lambda g, T, X: g.affine_select(ap(T, out), ap(T, a), pat, op, fill, base, cm), [a], [out])

    def send(sem, srcs, dst, nbytes, halves=(0, 1), alu=0):
        def fn(g, T, X):
            tr = []
            for i, h in enumerate(halves):
                rid, pid, m = X["to"][h]
                if len(halves) == 1:
                    m = X["to"][0][2] | X["to"][1][2]
                part = [ap(T, (r[0], r[1] + 128 * i, r[1] + 128 * i + 128)) for r in srcs + [dst]]
                tr.append(RemoteDMATransfer(dst_ids=[DstId(rid=rid, pnc=pid)], dma_engine_mask=m, remote_sem=T.sem[sem],
                                            srcs=part[:-1], dsts=part[-1:], alu_op=alu))
            return g.remote_dma_fused(tr, local_sem=T.sem["sent"])
        add("g", 300.0, fn, srcs, [dst], "r", RL + len(srcs) * nbytes / 100.0, sem)

    def sel(buf, r, k=128):
        return (buf, 15 - r, 143 - r, 1, 0, k)

    def blk(buf, t, n):
        return (buf, t * n, (t + 1) * n)

    def rot(d):
        return ("R3", 0, 256, 2, d)

    tag[0] = "load"
    dma("y", lambda T: T.adi[:], lambda T: T.ad[:], [], [("adi", 0, 16)], 8192)
    dma("y", lambda T: T.voi[:], lambda T: T.vo[:], [], [("voi", 0, 1024)], 600000)
    dma("y", lambda T: T.uii[:], lambda T: T.ui[:], [], [("uii", 0, 1024)], 1100000)
    dma("y", lambda T: T.Vb[:], lambda T: T.vt[:], [], [("Vb", 0, W0)], 1550000)
    dma("y", lambda T: T.Ub[:], lambda T: T.ut[:], [], [("Ub", 0, W0)], 2000000)
    dma("y", lambda T: T.zsb[:], lambda T: T.zs[:], [], [("zsb", 0, 256)], 2000000)
    dma("y", lambda T: T.tgb[:], lambda T: T.tg[:], [], [("tgb", 0, 256)], 2000000)
    for k, nme in ((2, "hv"), (0, "sl"), (1, "tr")):
        dma("s", lambda T, k=k: T.cmpi[:, 80 * k:80 * k + 80], lambda T, nme=nme: T[nme][:], [], [("cmpi", 80 * k, 80 * k + 80)], 100000)
    dma("s", lambda T: T.nxi[:], lambda T: T.nx[:], [], [("nxi", 0, 128)], 200000)
    tag[0] = "0"
    dma("g", lambda T: T.BT[:, 0:1024], lambda T: T.bs[:], [("uii", 0, 1)], [("BT", 0, 1024)], 1500000)
    dma("g", lambda T: T.U[:, 256:2048], lambda T: T.ut[:], [("uii", 0, 1)], [("U", 256, 2048)], 2000000)
    dma("g", lambda T: T.U[:, 2048:2304], lambda T: T.cs[:], [("uii", 0, 1)], [("U", 2048, 2304)], 2000000)
    dma("g", lambda T: T.V[:, 256:2048], lambda T: T.vt[:], [("uii", 0, 1)], [("V", 256, 2048)], 2000000)

    P0, PB0 = ("pc", 0, 1), ("pb", 0, 1)
    ID, NID, ONE = ("Ib", 0, 128), ("nIb", 0, 128), ("one", 0, 128)
    mset(("one", 0, 144), 1.0)
    if CFG["zero"] == "V":
        mset(("NX", 0, 2048), 0.0)
    else:
        mset(("NX", 0, 512), 0.0)
        for m in range(1, 4):
            dcopy(blk("NX", m, 512), ("NX", 0, 512))
    mset(("Fb", 0, 144), 0.0)
    iota(("pi", 0, 1), [[0, 1]], 0, 1)
    iota(("cf", 0, 16), [[1, 16]], 0, 0)
    asel(("idf", 0, 128), ONE, [[-1, 128]], AL.is_equal, 0, 1)
    asel(("bot", 0, 128), ONE, [[-16, 8], [0, 16]], AL.is_ge, 0, 1)
    asel(("BOb", 0, 128), ("bot", 0, 128), [[16, 8], [0, 16]], AL.is_ge, 15, -1)
    iota(("Tb", 0, 128), [[1, 128]], 0, -1)
    asel(("Sel", 0, 144, 1, 0, 8), ("one", 0, 144, 1, 0, 8), [[1, 144]], AL.is_equal, -15, -16)
    iota(("irow", 0, 256, 1, 0, 1), [[1, 256]], 0, 0)
    iota(("s16f", 0, 160), [[0, 10], [16, 16]], 0, 0)
    iota(("csf", 0, 96), [[256, 3], [A - W0, 2], [16, 16]], W0 - CEN, 0)
    iota(("csf", 96, 128), [[0, 2], [16, 16]], -CEN - 256, 0)
    iota(("csf", 128, 144), [[16, 16]], 0, 0)
    for m in range(8):
        asel(blk("seg", m, 128), ONE, [[0, 8], [1, 16]], AL.is_gt, 0, 0)
    ts(("pi", 4, 5), ("pi", 0, 1), 15, AL.bitwise_and)
    cp(P0, ("pi", 4, 5))
    cp(PB0, ("pi", 4, 5))
    ts(("cst", 0, 144), ("csf", 0, 144), P0, AL.add)
    ts(("s16", 0, 160), ("s16f", 0, 160), P0, AL.add, 16.0, AL.mult)
    ts(("colf", 0, 16), ("cf", 0, 16), P0, AL.is_equal)
    ts(("r1", 0, 16), ("cf", 0, 16), P0, AL.add, 16.0, AL.is_lt)
    tt(("colb", 0, 16), ("r1", 0, 16), ("cf", 0, 16), AL.mult)
    mset(("cm", 0, 128), -0.0625)
    if "V" in CFG["clip"]:
        mset(("cm", 128, 256), 0.0625)
    act(ID, ("idf", 0, 128), AF.Copy)
    act(NID, ("idf", 0, 128), AF.Copy, scale=-1.0)
    act(("I5", 0, 128), ("idf", 0, 128), AF.Copy, scale=512.0)
    for m in range(3):
        act(blk("In", m, 128), ("idf", 0, 128), AF.Copy if m else AF.Silu, scale=float(n0(2 * m) + OFF), extra=0.0 if m else 1300.0)
    act(("Fb", 15, 143, 16), ("BOb", 0, 128, 16), AF.Copy)
    act(("nFb", 0, 144), ("Fb", 0, 144), AF.Copy, scale=-4 * BIG)
    act(("seatb", 0, 16), ("cst", 128, 144), AF.Copy)
    for c in (0, 16):
        act(rot(c), ("idf", 0, 128), AF.Copy)
    for b, bank in enumerate(SUMS[:2]):
        mm([((bank, 128 * d, 128 * d + 128), m, x) for d in range(4) for m, x in ((ID, ID), (NID, rot(4 * b + d + 1)))])
        act(blk("RT", b, 512), (bank, 0, 512), AF.Copy)
    for d in range(1, 9):
        ts(blk("LS", d - 1, 128), ("Tb", 0, 128), ("colb", d, d + 1), AL.is_equal, -4 * BIG, AL.mult)
    for r in range(4):
        act(blk("Br", r, 128), ("BOb", 0, 128), AF.Copy, scale=("colf", r, r + 1))
    act(("id16", 0, 128), ("idf", 0, 128), AF.Copy, scale=-16.0)

    cp(("au", 0, 16), ("adi", 0, 16))
    cpg(("n16", 256, 512), ("voi", 0, 1024), ("au", 0, 16))
    cpg(("n16", 0, 256), ("uii", 0, 1024), ("au", 0, 16))
    ts(("OT", 256, 1280), ("voi", 0, 1024), float(OFF), AL.add)
    ts(("IT", 256, 1280), ("uii", 0, 1024), float(OFF), AL.add)
    ts(("KL", 0, 16), ("adi", 0, 16), -float(CEN), AL.add)
    ts(("less", 0, 16), ("adi", 0, 16), -float(CEN), AL.add)
    act(("w", 0, 128), ("BOb", 0, 128), AF.Copy)
    act(("z", 0, 256), ("zsb", 0, 256), AF.Copy, scale=-0.0625)
    if "D" in CFG["ysum"]:
        act(("ntg", 0, 256), ("tgb", 0, 256), AF.Copy, scale=-1.0)

    cp(("cmpb", 160, 240), ("cmpi", 160, 240))
    cp(("cmpb", 0, 160), ("cmpi", 0, 160))
    mm([(("PG", 256 * k + 80 * r, 256 * k + min(256, 80 * r + 80)), blk("Br", r, 128), ("cmpb", 80 * k, 80 * k + min(80, 256 - 80 * r)))
        for k in range(2) for r in range(4)])
    ts(("oh0", 0, 512), ("PG", 0, 512), P0, AL.is_equal)
    for k in range(2):
        dma("y", lambda T, k=k: T.RD[:, 1280 * k:1280 * k + 1280], lambda T, k=k: T.cmpb[:, 80 * k:80 * k + 80],
            [("cmpb", 80 * k, 80 * k + 80)], [("RD", 1280 * k, 1280 * k + 1280)], 50000, "d", "rd")
    for k in (2, 0, 1):
        dma("y", lambda T, k=k: T.R1[0:8, 1280 * k:1280 * k + 1280], lambda T, k=k: T.cmpb[:, 80 * k:80 * k + 80],
            [("cmpb", 80 * k, 80 * k + 80)], [("R1", 1280 * k, 1280 * k + 1280)], 200000)
    for r in range(16):
        dma("y", lambda T, r=r: T.RR[r:128:16, :], lambda T: T.RD[:, :], [("RD", 0, 2560)], [("RRp", r, r + 1)], 400000, "d", "rr")
    for k in range(2):
        ts(("oh", 1280 * k + 256, 1280 * k + 1280), ("RR", 1280 * k + 256, 1280 * k + 1280), PB0, AL.is_equal, more=[("RRp", 0, 16)])
    ts(("nxh", 0, 128), ("nxi", 0, 128), 992, AL.bitwise_and)
    ts(("nxh", 128, 256), ("nxi", 0, 128), 31, AL.bitwise_and)
    ts(("nxc", 0, 128), ("nxh", 0, 128), -float(CEN), AL.add)
    cp(("nxc", 128, 256), ("nxh", 128, 256))
    for k in range(2):
        dma("y", lambda T, k=k: T.NX[k:128:16, :], lambda T, k=k: T.nxc[:, 128 * k:128 * k + 128],
            [blk("nxc", k, 128), ("NX", 0, 2048)], [("NXp", k, k + 1)], 200000)
    mm([(("PK", 0, 80), sel("Sel", r, 8), ("R1", 2560 + r, 3840, 16, 0, 8)) for r in range(16)])
    act(("hl", 0, 80), ("PK", 0, 80), AF.Copy)
    mm([(("PB", 0, 160), sel("Sel", r, 8), ("R1", r, 2560, 16, 0, 8)) for r in range(16)] + [(("PB", 0, 160), ID, ("s16", 0, 160))])
    cp(("kj", 0, 160), ("PB", 0, 160))

    def lists_in(t, parts=(0, 1)):
        s = t - 1
        tag[0] = "list%d" % t
        c0, c1 = 1 - parts[-1], 2 - parts[0]
        mm([(("PK", 16 * c0, 16 * c1), sel("Fb", r), ("XR", 512 * t + 256 * c0 + r, 512 * t + 256 * c1, 16)) for r in range(16)]
           + [(("PK", 0, 16), NID, ("seatb", 0, 16))] * (1 - c0))
        if c1 == 2:
            ts(blk("au", t, 16), ("PK", 16, 32), float(CEN), AL.add)
        if c0 == 1:
            cp(("KL", 32 * t, 32 * t + 16), ("PK", 16, 32))
            return
        G = blk("Gs", s, 16)
        act(G, ("PK", 0, 16), AF.Relu, bias=BIG, scale=-4 * BIG, same=(0.25, AL.is_lt, 2 * BIG, AL.mult))
        lst = [(("PK", 32, 64), ID, blk("L16", s, 32)), (("PK", 32, 48), NID, G), (("PK", 48, 64), ID, G),
               (("PK", 64, 80), ID, ("KL", 32 * s, 32 * s + 16)), (("PK", 64, 80), ID, G)]
        if s >= 2:
            lst.append((("PK", 32, 48), NID, blk("rs", s, 16)))
        mm(lst)
        k = 16 if c1 == 2 and t < STEPS else 32
        ts(("KL", 32 * t + k - 16, 32 * t + 32), ("PK", k, 48), -BIG, AL.max)
        tt(blk("tmn", s, 32), ("PK", 48, 80), blk("cst", s // 2, 32), AL.min)
        ts(blk("o12", s, 32), blk("tmn", s, 32), CEN + 0.25, AL.add)

    def lowest(t, parts=(0, 1)):
        parts = [h for h in parts if (t < STEPS if h == 0 else t > 0)]
        p0, p1 = parts[0], parts[-1] + 1
        tag[0] = "lowe%d" % t
        k0, k1 = 32 * t + 16 * p0, 32 * t + 16 * p1
        wd = k1 - k0
        x, n = 8 * wd, 16 * wd
        lst = [(("PG", wd * d, wd * d + wd), blk("RT", d, 128), ("KL", k0, k1)) for d in range(8)]
        if t == 0:
            for m in range(8):
                act(blk("more", m, 16), ("colf", 0, 16), AF.Copy, scale=("less", 2 * m + 1, 2 * m + 2))
            lst += [(("PG", x, n), ("w", 0, 128), ("more", 0, 128))]
        else:
            if p0 == 0:
                c = 512 * t + 256 + 16
                lst += [(("PG", x + 16 * m, x + 16 * m + 16), ("BOb", 0, 128), ("XR", c + 32 * m, c + 32 * m + 16)) for m in range(8)]
            if p1 == 2:
                c = 1024 * ((t - 1) % 2)
                lst += [(("PG", n - 128, n), ("BOb", 0, 128), ("M", c, c + 256, 2, 16))]
        lst += [(("PG", x + r, n, 16), NID, ("KL", k0, k1, 2)) for r in range(16)]
        mm(lst)
        v = {"S": n, "M": x, "V": 0}[CFG["equal"][t]]
        if v:
            act(("ab", 0, v), ("PG", 0, v), AF.Abs)
            act(("eq", 0, v), ("ab", 0, v), AF.Relu, bias=4 * BIG, scale=-8 * BIG)
        if v < n:
            ts(("eq", v, n), ("PG", v, n), ROUND, AL.add, ROUND, AL.is_equal)
        c0, c1 = 128 + 16 * p0, 128 + 16 * p1
        mm([(("PK", c0, c1), ID, ("KL", k0, k1))]
           + [(("PK", c0, c1), blk("LS", d, 128), ("eq", wd * d, wd * d + wd)) for d in range(8)]
           + [(("PK", c0 + 1, c1, 2), sel("nFb", r), ("eq", x + r, n, 16)) for r in range(16)])
        tt(("tmx", k0, k1), ("PK", c0, c1), ("cst", 96 + 16 * p0, 96 + 16 * p1), AL.max)
        ts(("o03", k0, k1), ("tmx", k0, k1), CEN + 256 + (0.1 if t % 2 else 0.35), AL.add)

    def names(t):
        b = 512 * t
        tag[0] = "name%d" % t
        au = blk("au", t, 16)
        p, q = b + 256 * (t % 2), b + 256 * (1 - t % 2)
        P, Q = ("nm", p, p + 256), ("nm", q, q + 256)
        lean = -0.2 if t % 2 else 0.2
        if t == 0:
            ts(Q, ("n16", q, q + 256), lean - CEN, AL.add)
            ts(P, ("n16", p, p + 256), float(OFF), AL.add)
        else:
            act(Q, ("IT" if t % 2 else "OT", 256, 1280), AF.Identity, bias=lean - OFF - CEN, off=au)
            act(P, ("OT" if t % 2 else "IT", 256, 1280), AF.Copy, off=au)
            ts(("n16", q, q + 256), Q, CEN - lean + 0.25, AL.add)
            ts(("n16", p, p + 256), P, 0.25 - OFF, AL.add)
        if t == STEPS:
            return
        m = 1024 * (t % 2)
        ohk, ohj = (blk("oh", t, 256), blk("oh", 5 + t, 256)) if t else (blk("oh0", 0, 256), blk("oh0", 1, 256))
        PC, OJ = ("PC", 0, 256), ("PC", 256, 512)
        mm([(OJ, ID, ohj)])
        act(PC, P, AF.Identity, bias=-float(OFF + CEN))
        tt(("M", m + 512, m + 768), PC, Q, AL.is_lt if t % 2 else AL.is_gt)
        tt(("M", m + 256, m + 512), PC, ohk, AL.mult)
        tt(("M", m, m + 256), OJ, Q, AL.mult)
        tt(("M", m + 768, m + 1024), PC, ohj, AL.mult)
        if t in CFG["votes"]:
            mm([(("PL", 32, 48), sel("Fb", r), ("M", m + 512 + r, m + 768, 16)) for r in range(16)] + [(("PL", 32, 48), NID, blk("hl", t, 16))])
            mm([(("PL", 48, 64), sel("Fb", r), ("M", m + 768 + r, m + 1024, 16)) for r in range(16)])
            mm([(("PL", 0, 32), sel("Fb", r), ("M", m + r, m + 512, 16)) for r in range(16)])
        else:
            mm([(("PL", 0, 64), sel("Fb", r), ("M", m + r, m + 1024, 16)) for r in range(16)] + [(("PL", 32, 48), NID, blk("hl", t, 16))])
        act(blk("sg", t, 16), ("PL", 32, 48), AF.Sign, bias=0.5)
        if t >= 2:
            act(blk("rs", t, 16), ("PL", 48, 64), AF.Relu, bias=-4 * BIG * (n0(t - 2) - CEN - 0.5), scale=4 * BIG,
                same=(n0(t - 2) - CEN - 0.5, AL.is_gt, 2 * BIG, AL.mult))
        cp(blk("L16", t, 32), ("PL", 0, 32))
        mm([(("PL", 64, 80), ("I5", 0, 128), blk("sg", t, 16)), (("PL", 64, 80), ("I5", 0, 128), ("one", 0, 16)),
            (("PL", 64, 80), ID, ("KL", 32 * t, 32 * t + 16))])
        if t in CFG["votes"]:
            ts(("pj", 32 * t + 16, 32 * t + 32), ("PL", 64, 80), CEN + 0.25, AL.add)
            ts(("pj", 32 * t, 32 * t + 16), ("PL", 48, 64), CEN + 0.25, AL.add)
        else:
            ts(blk("pj", t, 32), ("PL", 48, 80), CEN + 0.25, AL.add)
        act(blk("xs", t, 256), ("NX", 0, 2048), AF.Copy, off=("pj", 32 * t + 16, 32 * t + 32), more=[("NXp", 0, 2)])
        send("ax%d" % t, [blk("xs", t, 256)], ("XR", 512 * (t + 1) + 256, 512 * (t + 1) + 512), 65536)
        tag[0] = "fres%d" % t
        E = (CFG["fresh"], 256, 512)
        mm([(E, blk("In", t // 2, 128), ohk), (E, ("one", 0, 128, 1, 0, 1), ("irow", 0, 256, 1, 0, 1))])
        tt(blk("nw", t % 2, 256), E, P, AL.max)

    def switch(t):
        tab = "IT" if t % 2 == 0 else "OT"
        tag[0] = "swit%d" % t
        for m in range(7, -1, -1):
            c = 256 * (t % 2) + 32 * m
            scatter((tab, 0, 1280), ("o03", 32 * t + 2 * m, 32 * t + 2 * m + 2), ("nw", c, c + 32))
        act(("XR", 512 * (t + 1), 512 * (t + 1) + 256), (tab, 256, 1280), AF.Relu, bias=0.75 - n0(t) - OFF, off=blk("au", t, 16))

    def filled(tab, t):
        return 256 + W0 + B * ((t + 1) // 2 if tab == "U" else t // 2)

    def early(t):
        tab = "V" if t % 2 == 0 else "U"
        q = 512 * t + 256 * (1 - t % 2)
        o = 4096 * (t % 3)
        tag[0] = "early%d" % t
        for hi, lo in steps_of(CUTS["early", t]):
            act(("py", o + 16 * lo, o + 16 * hi), (tab, 256, filled(tab, t)) if t else ("Vb", 0, W0), AF.Copy,
                scale=0.0625 if t < STEPS else -1.0, off=("n16", q + lo, q + hi))
            ops[-1]["piece"] = ("early", t, hi, lo)

    def steps_of(x):
        return list(zip(x[:-1], x[1:]))

    def late(t):
        tab = "U" if t % 2 == 0 else "V"
        win = (tab, 256, filled(tab, t)) if t else ("Ub", 0, W0)
        p, oy = 512 * t + 256 * (t % 2), 4096 * (t % 3)
        end = t == STEPS
        HELP = CFG["help"][t]
        scan, aid = CFG["scan"] if end else 0, 32 * len(HELP)
        units = steps_of(CFG["close"] if end else CFG["units"])
        parts = [(SUMS[i % 3], hi, lo) for i, (hi, lo) in enumerate(units if end else steps_of(CFG["parts"]))]
        cuts = [x for x in CUTS["late", t] if x > aid] + list(range(aid, -1, -32))
        if t == 0:
            win = ("Ub", 0, W0)
        if aid:
            tag[0] = "help%d" % t
            for hi, lo in steps_of(cuts):
                if hi <= aid:
                    if lo // 32 in CFG["copy"]:
                        act((HELP[lo // 32], 0, 512), ("py", oy + 16 * lo, oy + 16 * hi), AF.Copy)
                    else:
                        mm([((HELP[lo // 32], 0, 512), ("idf", 0, 128), ("py", oy + 16 * lo, oy + 16 * hi))], True)
                    act(("prod", 16 * lo, 16 * hi), win, AF.Copy, off=("n16", p + lo, p + hi))
        for hi, lo in steps_of(cuts):
            tag[0] = "late%d" % t
            pr = ("prod", 16 * lo, 16 * hi)
            if hi <= aid:
                tt(pr, pr, (HELP[lo // 32], 0, 512), AL.mult)
            else:
                ttg(pr, win, ("n16", p + lo, p + hi), ("py", oy + 16 * lo, oy + 16 * hi), AL.mult)
                ops[-1]["piece"] = ("late", t, hi, lo)
            while units and units[0][1] >= lo:
                u1, u0 = units.pop(0)
                bank, top, base = parts[0]
                tag[0] = "sums%d" % t
                for k0 in range(0, 16, 4):
                    mm([((bank, u0 - base, u1 - base), ("idf" if end else "id16", 0, 128), ("prod", 16 * u0 + k, 16 * u1, 16))
                        for k in range(k0, k0 + 4)], True, k0 == 0, k0 == 12)
                if u0 == base:
                    tail(t, (bank, 0, top - base), base, top)
                    parts.pop(0)
        for lo in range((scan - 1) // 64 * 64 if scan else -1, -1, -64):
            a, b = 16 * lo, 16 * min(scan, lo + 64)
            tag[0] = "scan%d" % t
            add("v", vcost(b - a), lambda g, T, X, a=a, b=b: g.vector.tensor_tensor_scan(
                T.py[:, a:b], T.seg[:, 0:b - a], T.prod[:, a:b], 0.0, AL.mult, AL.add),
                [("seg", 0, 1024), ("prod", a, b)], [("py", a, b)])
        if scan:
            tail(t, ("py", 15, 16 * scan, 16), 0, scan)

    def side(t):
        X, oy = ("U" if t % 2 == 0 else "V"), 4096 * (t % 3)
        f = filled(X, t)
        tag[0] = "side%d" % t
        cn, dq = blk("cn", t, 256), blk("dq", t % 2, 256)
        act(cn, (X, 256, f + 256), AF.Copy, off=("o12", 32 * t, 32 * t + 16))
        Y = "V" if t % 2 == 0 else "U"
        send("ac%d" % t, [cn], (Y, filled(Y, t), filled(Y, t) + 256) if t < STEPS - 1 else ("fcl", 0, 256), 131072)
        act(blk("yj", t % 2, 256), ("py", oy, oy + 4096), AF.Copy, scale=16.0, off=blk("kj", 5 + t, 16))
        if CFG["spare"][t] == "1":
            act(dq, (X, f, f + 256), AF.Copy, scale=-1.0)
            dadd(dq, cn)
        else:
            act(CB, (X, f, f + 256), AF.Copy)
            tt(dq, cn, CB, AL.subtract)
        ttg(("more", 0, 256), ("py", oy, oy + 4096), blk("kj", t, 16), dq, AL.mult)
        tts(("BT", 0, 1792), ("o12", 32 * t + 16, 32 * t + 32), blk("bg", t % 3, 256), ("more", 0, 256), AL.add)
        for hi, lo in steps_of(CFG["w"][t]):
            tag[0] = "w%d%d" % (t, lo)
            ttg(("w", lo, hi), (X, 256, f), ("pj", 32 * t + lo // 16, 32 * t + hi // 16), ("z", 256 * t + lo, 256 * t + hi), AL.mult)

    def base(t):
        tag[0] = "bg%d" % t
        bg, to = blk("bg", t % 3, 256), (BT0[0], BT0[1], BT0[1] + 256)
        act(bg, ("BT", 0, 1024), AF.Copy, off=blk("au", t, 16))
        if t == STEPS:
            return
        if CFG["ysum"][t] == "D":
            bt = blk("bgt", t % 2, 256)
            dcopy(bt, ("ntg", 0, 256))
            dadd(bt, bg)
            dcopy(blk("y", t, 256), bg)
            act(to, bt, AF.Copy)
        elif CFG["ysum"][t] == "T":
            mm([(to, ("idf", 0, 128), bg), (to, NID, ("tgb", 0, 256))])
            dcopy(blk("y", t, 256), bg)
        elif t == 0 or CFG["ysum"][t - 1] != "B":
            act(to, ("tgb", 0, 256), AF.Copy)

    def tail(t, S0, lo, hi):
        Y = "V" if t % 2 == 0 else "U"
        k, j, b, bb = 32 * (t + 1) + 16, 256 * (t % 2), 256 * t, 256 * (t % 3)
        tag[0] = "tail%d%d" % (t, lo)
        S, y = S0 if psum(S0) else ("PG", 0, hi - lo), ("y", b + lo, b + hi)
        z, to = ("z", b + lo, b + hi), (BT0[0], BT0[1] + lo, BT0[1] + hi)
        if t < STEPS and CFG["ysum"][t] != "B":
            sz = ("sz", j + lo, j + hi)
            tt(sz, S, z, AL.mult)
            tt(S, sz, to, AL.add)
        else:
            tt(S, S0, z, AL.mult)
            tt(y, S, ("bg", bb + lo, bb + hi), AL.add)
            if t == STEPS:
                dma("y", lambda T: T.ys[:, y[1]:y[2]], lambda T: ap(T, y), [y], [], 32768, "o")
                return
            tt(S, y, to, AL.subtract)
        tt(("less", lo, hi), S, ("w", lo, hi), AL.mult)
        for m in range(hi // 32 - 1, lo // 32 - 1, -1):
            tts((Y, 0, filled(Y, t)), ("o03", k + 2 * m, k + 2 * m + 2), ("yj", j + 32 * m, j + 32 * m + 32),
                ("less", 32 * m, 32 * m + 32), AL.add)
        if lo % 128:
            return
        h = lo // 128
        tag[0] = "clip%d%d" % (t, h)
        y, zo = blk("y", 2 * t + h, 128), blk("zo", 2 * t + h, 128)
        if CFG["ysum"][t] != "B":
            dadd(y, blk("sz", 2 * (t % 2) + h, 128))
        if CFG["clip"][t] == "S":
            act(blk("r1", h, 128), y, AF.Relu, bias=1.0)
            act(zo, blk("r1", h, 128), AF.Relu, bias=0.125, scale=-0.0625)
            send("az%d%d" % (t, h), [zo, ("cm", 0, 128)], blk("z", 2 * t + 2 + h, 128), 65536, (h,), 1)
        else:
            ts(zo, y, 1.0, AL.min, -0.0625, AL.mult)
            send("az%d%d" % (t, h), [zo, ("cm", 128, 256)], blk("z", 2 * t + 2 + h, 128), 65536, (h,), 3)
        if h == 0:
            dma("y", lambda T: T.ys[:, b:b + 256], lambda T: T.y[:, b:b + 256], [blk("y", t, 256)], [], 131072, "o")

    early(0)
    names(0)
    lowest(0)
    switch(0)
    for t in range(STEPS + 1):
        base(t)
        if t < STEPS:
            if t < APART:
                lists_in(t + 1, (1,))
                lowest(t + 1, (1,))
            lists_in(t + 1, (0,) if t < APART else (0, 1))
            names(t + 1)
            lowest(t + 1, (0,) if t < APART else (0, 1))
            if t + 1 < STEPS:
                switch(t + 1)
            early(t + 1)
            side(t)
        late(t)
        if t == STEPS - 1:
            dma("y", lambda T: T.fb[:], lambda T: T.BT[:, 0:1024], [("BT", 0, 1024)], [], 524288, "o")
            dma("y", lambda T: T.fc[:], lambda T: T.fcl[:], [("fcl", 0, 256)], [], 131072, "o")
    return ops


def schedule():
    for t in range(STEPS + 1):
        CUTS["early", t] = list(range(256, -1, -CFG["early"]))
        CUTS["late", t] = list(CFG["late" if t < STEPS else "last"])
    places = None
    for k, sweeps in enumerate(SWEEPS):
        ops, s = arrange(places, sweeps, k)
        if k + 1 < len(SWEEPS):
            places = {mark(ops[j]): (float(x), "alt" in ops[j] and ops[j]["eng"] == "v") for x, j in enumerate(s["order"])}
            for kind, t, x in s["join"]:
                CUTS[kind, t].remove(x)
    return ops, s


def mark(o):
    return ("piece",) + o["piece"][:2] + o["piece"][3:] if "piece" in o else (o["tag"], o["kind"], tuple(o["rd"]), tuple(o["wr"]))


def arrange(places, sweeps, phase):
    others = [(build(*c[:-1]), c[-1]) for c in COSTS]
    ops = others[0][0]
    n = len(ops)
    deps = [dict() for _ in range(n)]
    seen = {}
    for j, o in enumerate(ops):
        acc = [(r, False) for r in o["rd"]] + [(r, True) for r in o["wr"]]
        for r, wr in acc:
            for (i, c0, c1, iw) in seen.get(r[0], ()):
                pe = o["eng"] == "p" and ops[i]["eng"] == "p"
                if c0 < r[2] and r[1] < c1 and (wr or iw):
                    deps[j][i] = deps[j].get(i, False) or not pe or (iw and not wr)
                elif pe and o["tag"][:4] == ops[i]["tag"][:4] == "sums" and r[0] in _P:
                    deps[j].setdefault(i, False)
        for r, wr in acc:
            seen.setdefault(r[0], []).append((j, r[1], r[2], wr))
    for a in range(n - 1):
        if ops[a + 1]["tag"] == "load" and ops[a + 1]["eng"] == ops[a]["eng"]:
            deps[a + 1].setdefault(a, False)
    ei = ["vspgy".index(o["eng"]) for o in ops]
    banks = [tuple(sorted(set(_P.index(r[0]) for r in o["rd"] + o["wr"] if r[0] in _P))) for o in ops]
    anc, near = [0] * n, []
    for j in range(n):
        far = 0
        for i in deps[j]:
            far |= anc[i]
        near.append({i: w for i, w in deps[j].items() if not far >> i & 1 or ops[i]["lat"]})
        for i in deps[j]:
            far |= 1 << i
        anc[j] = far
    sets = []
    for oo, lat in others:
        sets.append(([o["cost"] for o in oo], [o["lat"] for o in oo],
                     [[(i, oo[i]["lat"] + lat if w else 0.0) for i, w in near[j].items()] for j in range(n)], lat))
    backs = []
    for s in sets:
        backs.append([[] for _ in range(n)])
        for j in range(n):
            for i, d in s[2][j]:
                backs[-1][i].append((j, d))
    cost, tail, pred = sets[0][:3]
    back = backs[0]
    ends = [j for j in range(n) if not back[j]]
    link = [j - 1 if phase + 1 < len(SWEEPS) and o.get("piece", "a")[0] == "early" and o["piece"][2] < 256 else -2 for j, o in enumerate(ops)]
    norm = [max(sum(c for c, e in zip(s[0], ei) if e == x) for x in range(5)) / w for s, w in zip(sets, WEIGHTS)]
    onv, spare = set(), [[o["alt"][0] if "alt" in o else 0.0 for o in oo] for oo, lat in others]

    def flip(js):
        for j in js:
            ei[j] = 1 - ei[j]
            for s, x in zip(sets, spare):
                s[0][j], x[j] = x[j], s[0][j]
        onv.symmetric_difference_update(js)

    def run(seq, k0, old):
        lq, lb = [-1] * 5, [-1] * 8
        for j in seq[:k0]:
            lq[ei[j]] = j
            for b in banks[j]:
                lb[b] = j
        out, tot, rest = [], 0.0, seq[k0:]
        for (c, tl, pr, lat), (en0, why0), nm in zip(sets, old, norm):
            en, why, q, bk = list(en0), list(why0), list(lq), list(lb)
            for j in rest:
                e = ei[j]
                w = q[e]
                t = en[w] - JOIN if w == link[j] else en[w]
                for i, d in pr[j]:
                    x = en[i] + d
                    if x > t:
                        t, w = x, i
                for b in banks[j]:
                    i = bk[b]
                    if ei[i] != e and en[i] + lat > t:
                        t, w = en[i] + lat, i
                    bk[b] = j
                en[j], why[j], q[e] = t + c[j], w, j
            tot += (max([en[j] + tl[j] for j in ends]) + SOON * sum(en) / n) / nm
            out.append((en, why))
        return tot, out

    ei.append(-1)
    blank = [([0.0] * (n + 1), [-1] * (n + 1))] * len(sets)

    def place(seq, pr, first, c, lat):
        busy, held, st = [[] for _ in range(5)], [[] for _ in range(8)], [0.0] * n
        for j in seq:
            t, e, cj = first[j], ei[j], c[j]
            for i, d in pr[j]:
                x = st[i] + c[i] + d
                if x > t:
                    t = x
            b, again = busy[e], True
            while again:
                k, again = len(b), False
                while k > 0 and b[k - 1][1] > t:
                    k -= 1
                while k < len(b) and b[k][0] < t + cj:
                    if b[k][1] > t:
                        t = b[k][1]
                    k += 1
                for q in banks[j]:
                    for s0, e0, x in held[q][-12:]:
                        if x != e and s0 < t + cj + lat and e0 + lat > t:
                            t, again = e0 + lat, True
            b.insert(k, (t, t + cj))
            for q in banks[j]:
                held[q].append((t, t + cj, e))
            st[j] = t
        return st

    def topo_by(key):
        k2 = list(key)
        for j in range(n):
            for i, d in pred[j]:
                if k2[j] <= k2[i]:
                    k2[j] = k2[i] + 1e-3
        return sorted(range(n), key=lambda j: k2[j])

    def improve(key, k, s):
        c, tl, pr, lat = sets[s]
        st = place(topo_by(key), pr, [0.0] * n, c, lat)
        for _ in range(k):
            bk = place(sorted(range(n), key=lambda j: (st[j] + c[j], j), reverse=True), backs[s], tl, c, lat)
            st = place(topo_by([-(bk[j] + c[j]) for j in range(n)]), pr, [0.0] * n, c, lat)
        seq = sorted(range(n), key=lambda j: (st[j], j))
        v, s2 = run(seq, 0, blank)
        return v, seq, [s2[0][0][j] - cost[j] for j in range(n)]

    prio = [0.0] * n
    for i in range(n - 1, -1, -1):
        prio[i] = cost[i] + max([prio[j] + d for j, d in back[i]] + [tail[i]])
    whole = [o["tag"][:4] in ("fres", "list", "lowe", "name", "swit") for o in ops]

    def planned(lead):
        key = [1e9] * n
        for j, o in enumerate(ops):
            k = o["tag"][:4]
            if k in PLAN:
                t = int([x for x in o["tag"] if x.isdigit()][0])
                key[j] = FIRST + STEP * t + PLAN[k] + 1e-3 * j - (lead[t] if whole[j] else 0.0)
        for i in range(n - 1, -1, -1):
            key[i] = min([key[i]] + [key[j] - d - cost[i] for j, d in back[i]])
        return key

    def ahead(b):
        key = [-p - (b if w else 0.0) for p, w in zip(prio, whole)]
        for i in range(n - 1, -1, -1):
            key[i] = min([key[i]] + [key[j] - d - cost[i] for j, d in back[i]])
        return key

    tags = sorted(set(o["tag"] for o in ops))
    kind = ["".join(x for x in o["tag"] if not x.isdigit()) for o in ops]
    kinds = sorted(set(kind))
    rnd = [SEED]

    def draw():
        rnd[0] = (rnd[0] * 1103515245 + 12345) % 2147483648
        return rnd[0] / 2147483648.0

    def rounds(key):
        cur = best = min((improve(key, k, s) for k in (0, 1, 3) for s in range(len(sets))), key=lambda x: x[0])
        for it in range(ROUNDS):
            amp = (30.0, 100.0, 400.0)[it % 3]
            mv = {tags[int(draw() * len(tags))]: (draw() - 0.5) * 8000.0 for _ in range(int(draw() * 3))}
            mk = {kinds[int(draw() * len(kinds))]: (draw() - 0.5) * 6000.0 for _ in range(int(draw() * 1.5))}
            new = improve([cur[2][j] + amp * draw() + mv.get(ops[j]["tag"], 0.0) + mk.get(kind[j], 0.0) for j in range(n)],
                          it % 2, int(draw() * len(sets)))
            if new[0] < cur[0] + 0.004 * draw():
                cur = new
            if new[0] < best[0]:
                best = new
        return best[1]

    def shift(seq, a, b, up):
        mid = seq[a:b + 1]
        if up:
            m = anc[seq[b]] | 1 << seq[b]
            return seq[:a] + [x for x in mid if m >> x & 1] + [x for x in mid if not m >> x & 1] + seq[b + 1:]
        i = seq[a]
        go = [x == i or anc[x] >> i & 1 for x in mid]
        return seq[:a] + [x for x, f in zip(mid, go) if not f] + [x for x, f in zip(mid, go) if f] + seq[b + 1:]

    def sweep(seq, W, moves, heat):
        seq = list(seq)
        starts = list(range(-int(draw() * W / 2), n - W // 2, W // 2))
        stops = {min(n, a + W): None for a in starts}
        qs = [[0.0] * (n + 1) for _ in sets]
        nq, nb = [-1] * 5, [-1] * 8
        for k in range(n, 0, -1):
            if k in stops:
                stops[k] = (list(nq), list(nb))
            j = seq[k - 1]
            e = ei[j]
            for (c, tl, pr, lat), bk, q in zip(sets, backs, qs):
                x = max(tl[j], q[nq[e]])
                for i, d in bk[j]:
                    if d + q[i] > x:
                        x = d + q[i]
                for b in banks[j]:
                    if ei[nb[b]] != e and lat + q[nb[b]] > x:
                        x = lat + q[nb[b]]
                q[j] = x + c[j]
            nq[e] = j
            for b in banks[j]:
                nb[b] = j
        ens, whys = [[0.0] * (n + 1) for _ in sets], [[-1] * (n + 1) for _ in sets]
        lq, lb = [-1] * 5, [-1] * 8
        for a0 in starts:
            a0, b0 = max(0, a0), min(n, a0 + W)
            win = seq[a0:b0]
            inside = set(win)
            nq, nb = stops[b0]
            outs = [{j: max([s[1][j]] + [d + q[i] for i, d in bk[j] if i not in inside]) for j in win} for s, bk, q in zip(sets, backs, qs)]

            def value(win):
                tot, tips = 0.0, []
                for (c, tl, pr, lat), en, why, out, qq, nm in zip(sets, ens, whys, outs, qs, norm):
                    q, bk, top, tip, sm = list(lq), list(lb), 0.0, -1, 0.0
                    for j in win:
                        e = ei[j]
                        w = q[e]
                        t = en[w] - JOIN if w == link[j] else en[w]
                        for i, d in pr[j]:
                            x = en[i] + d
                            if x > t:
                                t, w = x, i
                        for b in banks[j]:
                            i = bk[b]
                            if ei[i] != e and en[i] + lat > t:
                                t, w = en[i] + lat, i
                            bk[b] = j
                        t += c[j]
                        en[j], why[j], q[e] = t, w, j
                        sm += t
                        t += out[j]
                        if t > top:
                            top, tip = t, j
                    sq = 0.0
                    for e in range(4):
                        t = en[q[e]] + qq[nq[e]]
                        sq += t
                        if t > top:
                            top, tip = t, q[e]
                    for b in range(8):
                        if ei[bk[b]] != ei[nb[b]] and en[bk[b]] + lat + qq[nb[b]] > top:
                            top, tip = en[bk[b]] + lat + qq[nb[b]], bk[b]
                    tot += (top + EVEN * sq / 4 + SOON * sm / len(win)) / nm
                    tips.append(tip)
                return tot, tips

            def path(win, tips):
                pos = {j: k for k, j in enumerate(win)}
                arcs = []
                for why, j in zip(whys, tips):
                    while j in pos and why[j] in pos:
                        if not anc[j] >> why[j] & 1:
                            arcs.append((pos[why[j]], pos[j]))
                        j = why[j]
                return arcs

            val, tips = value(win)
            arcs, keep, m = path(win, tips), (val, win, set(onv)), len(win)
            free = [j for j in win if "alt" in ops[j]]
            for it in range(moves):
                up = draw() < 0.5
                if free and draw() < SWAP:
                    j = free[int(draw() * len(free))]
                    flip({j})
                    v2, tips = value(win)
                    if v2 <= val + heat * (1.0 - it / moves) * draw():
                        val, arcs = v2, path(win, tips)
                        if val < keep[0]:
                            keep = (val, win, set(onv))
                    else:
                        flip({j})
                    continue
                if arcs and draw() < ONPATH:
                    a, b = arcs[int(draw() * len(arcs))]
                    far = int(draw() * draw() * 30)
                    a, b = (max(0, a - far), b) if up else (a, min(m - 1, b + far))
                else:
                    a = int(draw() * (m - 1))
                    b = min(m - 1, a + 1 + int(draw() * draw() * 40))
                new = shift(win, a, b, up)
                if new == win:
                    continue
                v2, tips = value(new)
                if v2 <= val + heat * (1.0 - it / moves) * draw():
                    win, val, arcs = new, v2, path(new, tips)
                    if val < keep[0]:
                        keep = (val, win, set(onv))
            win = keep[1]
            flip(onv ^ keep[2])
            value(win)
            seq[a0:b0] = win
            for j in seq[a0:max(0, a0 + (b0 - a0 if b0 == n else W // 2 - (W - (b0 - a0))))]:
                lq[ei[j]] = j
                for b in banks[j]:
                    lb[b] = j
        return seq

    if places:
        flip({j for j, o in enumerate(ops) if places[mark(o)][1]})
        seq = topo_by([places[mark(o)][0] for o in ops])
    else:
        tries = []
        for key in [ahead(b) for b in AHEAD] + [planned(x) for x in LEADS]:
            flip(set(onv))
            seq = rounds(key)
            for W in WINDOWS[:3]:
                seq = sweep(seq, W, MOVES // 2, HEAT)
            tries.append((run(seq, 0, blank)[0], seq, set(onv)))
        seq, x = min(tries)[1:]
        flip(onv ^ x)
        TRIES.append(sorted(x[0] for x in tries))
    val, st = run(seq, 0, blank)
    top = (val, seq, st, set(onv))
    for it in range(sweeps):
        seq = sweep(seq, WINDOWS[it % len(WINDOWS)], MOVES, HEAT * (1.0 - it / sweeps) / (1 + phase))
        val, st = run(seq, 0, blank)
        if val < top[0]:
            top = (val, seq, st, set(onv))
    order, st = top[1], top[2]
    flip(onv ^ top[3])
    for j in onv:
        ops[j]["eng"], ops[j]["cost"], ops[j]["fn"] = "v", ops[j]["alt"][0], ops[j]["alt"][1]
    join, prev = [], [-1] * 5
    for j in order:
        i = prev[ei[j]]
        a, b = ops[i].get("piece", "a"), ops[j].get("piece", "b")
        if a[:2] == b[:2] and a[3] == b[2]:
            if all(en[k] - s[0][k] - d >= en[j] - JOIN for (en, why), s, bk in zip(st, sets, backs) for k, d in bk[i]):
                join.append(a[:2] + a[3:])
                j = -1 if phase % 2 else j
        prev[ei[j if j >= 0 else i]] = j
    start = [st[0][0][j] - cost[j] for j in range(n)]
    done = [st[0][0][j] + tail[j] for j in range(n)]
    last = [-1] * 8
    for j in order:
        for b in banks[j]:
            if last[b] >= 0 and ei[last[b]] != ei[j]:
                deps[j][last[b]] = True
            last[b] = j
    token, count, nd = {}, {e: 0 for e in "vspg"}, 0
    known = {e: {} for e in "vspgy"}
    clock, waits = {}, {}
    for j in order:
        o, e = ops[j], ops[j]["eng"]
        w = {}
        for i in sorted((i for i in deps[j] if deps[j][i]), key=lambda i: -done[i]):
            s, v = token[i]
            if known[e].get(s, 0) >= v:
                continue
            w[s] = max(w.get(s, 0), v)
            for s2, v2 in clock[i].items():
                known[e][s2] = max(known[e].get(s2, 0), v2)
        waits[j] = w
        if o["kind"] == "c":
            count[e] += 1
            token[j] = ("q" + e, count[e])
        elif o["kind"] == "d" and o["name"]:
            token[j] = (o["name"], 16 * sum(x["name"] == o["name"] for x in ops))
        elif o["kind"] == "d":
            token[j] = ("d%d" % nd, 16)
            nd += 1
        elif o["kind"] == "o":
            token[j] = ("outs", 0)
        else:
            token[j] = (o["name"], 8)
        clock[j] = {} if o["kind"] == "r" else dict(known[e])
        clock[j][token[j][0]] = token[j][1]
    spans = [max(en[j] + s[1][j] for j in ends) for (en, why), s in zip(st, sets)]
    return ops, {"spans": spans, "order": order, "waits": waits, "token": token, "count": count, "start": start, "done": done,
                 "join": join, "st": st}


_PLAN = {}


def rank_program(g, core, T, topo):
    rank = T.rank_of(core)
    if rank is None:
        return
    if not _PLAN:
        _PLAN["ops"], _PLAN["s"] = schedule()
    ops, s = _PLAN["ops"], _PLAN["s"]
    n = len(T.cores)
    to = []
    for h, d in enumerate((T.cores[(rank + 1) % n], T.cores[(rank - 1) % n])):
        rid, pid, _ = topo.addr(d)
        eng = topo.engines(core, d)
        k = len(eng) // 2
        to.append((rid, pid, sum(1 << e for e in eng[h * k:h * k + k])))
    X = {"to": to}
    q = {"v": g.vector, "s": g.scalar, "p": g.tensor, "g": g, "y": g.sync}
    outs = sends = 0
    for j in s["order"]:
        o = ops[j]
        for sem, v in s["waits"][j].items():
            q[o["eng"]].wait_ge(T.sem[sem], v)
        ins = o["fn"](g, T, X)
        if o["kind"] == "c":
            ins.then_inc(T.sem[s["token"][j][0]], 1)
        elif o["kind"] == "r":
            sends += 1
        else:
            ins.then_inc(T.sem[s["token"][j][0]], 16)
            outs += o["kind"] == "o"
    for e, v in s["count"].items():
        g.wait_ge(T.sem["q" + e], v)
    g.wait_ge(T.sem["sent"], 8 * sends)
    g.sync.wait_ge(T.sem["outs"], 16 * outs)
